import numpy as np, ml_dtypes
CORES = [2,7,18,23,34]
N = 5
BF = ml_dtypes.bfloat16
W, H, P, RO, ST, TH = 3072, 1024, 512, 3, 2, 40
def place(o, i):
    return o[np.arange(8)[None, :, None, None], i]
def ground(rng):
    o = np.argsort(rng.random((8, W)), axis=-1); x = np.zeros((N, 8, 16, W), np.int64); top = np.zeros(8, np.int64)
    for g in range(8):
        m = int(rng.choice(np.array([3, 5, 8]))); c = rng.integers(0, 16, (m, 16)); s = np.linspace(0, m, W, endpoint=False)
        i = np.minimum(s.astype(np.int64), m - 1); f = (s - i)[:, None]
        b = np.rint(c[i] * (1 - f) + c[(i + 1) % m] * f).astype(np.int64).T
        y = b[None] + rng.integers(-1, 2, (N, 16, W))
        y = np.where(rng.random((N, 1, W)) < 0.03, rng.integers(0, 16, (N, 16, W)), y)
        x[:, g] = np.clip(y, 0, 15)[:, :, np.argsort(o[g])]; top[g] = W * 28 // (85 * m)
    return o, top, x
def knot(rng, r, share):
    k = (N, 8, 1, r.shape[3]); p = rng.integers(0, 15, k); q = np.minimum(p + rng.integers(1, 5, k), 15)
    hit = (rng.random(k) < share) & (np.arange(16)[None, None, :, None] == q)
    return np.where(hit, np.take_along_axis(r, p, 2), r)
def walk(rng, o, top, n):
    st = np.floor((rng.random((N, 8, 15, n)) * 1.2 - 0.2) * top[None, :, None, None]).astype(np.int64)
    st = st + np.where(rng.random(st.shape) < 0.01, rng.integers(0, W, st.shape), 0)
    a = rng.integers(0, W, (N, 8, 1, n))
    return knot(rng, place(o, np.concatenate([a, a + np.add.accumulate(st, axis=2)], axis=2) % W), 0.4)
def ladder(rng, lev):
    pm = np.argsort(rng.random((8, 16)), axis=-1)
    return np.clip(lev[:, :, None, :] - 15 * pm[None, :, :, None], 0, 15)
def pack(x, c, r):
    return {"x": np.ascontiguousarray(x.reshape(N, 128, W)).astype(np.float32).astype(BF), "c0": np.ascontiguousarray(c.reshape(N, 128, H)).astype(np.int32),
            "r0": np.ascontiguousarray(r.reshape(N, 128, P)).astype(np.int32)}
def setup_inputs(rng):
    o, top, x = ground(rng)
    return pack(x, walk(rng, o, top, H), walk(rng, o, top, P))
def setup_inputs_ties(rng):
    o = np.argsort(rng.random((8, W)), axis=-1); cls = np.argsort(o, axis=-1) % 7
    cr = np.where(rng.random((N, 8, W)) < 0.04, rng.integers(0, 7, (N, 8, W)), cls[None])
    lev = np.array([0, 1, TH, TH + 1, 2 * TH, 2 * TH + 1, 3 * TH + 2])[cr]
    def some(n):
        i = rng.integers(0, 6, (N, 8, n)); rows = [i]
        for p in range(15):
            jump = rng.random((N, 8, n)) < 0.04
            d = np.where(jump, rng.choice(np.array([-3, 3]), (N, 8, n)), rng.choice(np.array([-2, -2, -1, 0, 1, 2, 2]), (N, 8, n)))
            i = np.clip(i + d, 0, 5 + jump.astype(np.int64)); rows.append(i)
        i = np.stack(rows, axis=2)
        return place(o, i + 7 * rng.integers(0, W // 7, i.shape))
    return pack(ladder(rng, lev), some(H), some(P))
def setup_inputs_clash(rng):
    hi = np.arange(W - 64, W); last6 = (hi[:, None] * hi[None, :]) % 64 == 63; over = last6 & (hi[:, None] * (hi[None, :] + 64) > 2 ** 24)
    hu, hv = np.nonzero(over if np.any(over) else last6)
    nm = rng.random((8, W)) < 0.5; a = rng.integers(1, H - 1, 8); row = np.arange(16)[None, :, None]
    r = np.zeros((N, 8, 16, P), np.int64); c = np.zeros((N, 8, 16, H), np.int64); lev = np.zeros((N, 8, W), np.int64)
    for g in range(8):
        sp = np.array([0, H - 1, int(a[g]), int(a[g]) + H]); nm[g, sp] = True
        apart = rng.permutation(H)[:P] + H * rng.integers(0, 2, P)
        if g == 4: nm[g, apart] = True
        if g == 5: nm[g, W - 64:] = True
        ne, fa = np.flatnonzero(nm[g]), np.flatnonzero(~nm[g])
        if g < 2: u, v = sp[2:], np.array([0, 0])
        elif g < 4: u, v = sp[:2], np.array([int(rng.choice(ne)), 0])
        elif g == 4: u, v = apart, np.zeros(P, np.int64)
        elif g == 5: u, v = hi[hu], hi[hv]
        else: u, v = rng.choice(ne, 8), rng.choice(ne, 8)
        i = rng.integers(0, len(u), (N, P)); k = rng.integers(0, 16, (N, P))
        if g == 4: i = np.argsort(rng.random((N, P)), axis=-1)
        if g == 1 or g == 4: k = rng.integers(0, 14, (N, P))
        if g == 0: k[0, :3] = 15; k[0, 3] = 5; k[1] = 15; k[1, P - 1] = 3
        k[2] = np.minimum(k[2], 14)
        at = np.where(k < 15, k, rng.integers(0, 15, (N, P)))
        y = np.where(row > k[:, None], rng.choice(fa, (N, 16, P)), rng.choice(ne, (N, 16, P)))
        y = np.where(row == at[:, None], u[i][:, None], y)
        y[:, 15] = np.where(k == 14, y[:, 15], v[i]); r[:, g] = y
        flip = rng.random((N, W)) < 0.02; flip[:, sp] = False; flip[:3] = False
        lev[:, g] = np.where(nm[g][None] ^ flip, 0, 150) + rng.integers(0, 6, (N, W))
        c[:, g] = np.where(rng.random((N, 1, H)) < 0.5, rng.choice(ne, (N, 16, H)), rng.integers(0, W, (N, 16, H)))
    return pack(ladder(rng, lev), c, r)
def setup_inputs_loops(rng):
    o, top, x = ground(rng); x[:, ::2] = rng.integers(0, 3, (N, 4, 16, W))
    e = np.argsort(o, axis=-1); b = 1 + 2 * int(rng.integers(0, 4)); z = int(rng.integers(0, N))
    x[:, b] = np.where(e[b] % 3 == 0, rng.integers(0, 3, (N, 16, W)), x[:, b])
    def tie(r):
        kd = rng.integers(0, 8, (N, 8, r.shape[3]))
        for p in range(1, 16):
            r[:, :, p] = np.where(kd == 1, r[:, :, 0], r[:, :, p])
            if p > 1: r[:, :, p] = np.where(kd == 7, r[:, :, p % 2], r[:, :, p])
        for m, dst, src in ((2, 15, 0), (3, 15, 14), (4, 5, 0), (4, 9, 0), (5, 4, 1), (5, 6, 2), (6, 12, 3), (6, 8, 5)):
            r[:, :, dst] = np.where(kd == m, r[:, :, src], r[:, :, dst])
        return r
    w = walk(rng, o, top, P); w[z, b] = o[b][e[b][w[z, b]] // 3 * 3]
    return pack(x, tie(walk(rng, o, top, H)), tie(w))
def setup_inputs_calm(rng):
    o, top, x = ground(rng); q = rng.permutation(N)
    x[q[0]] = rng.integers(0, 3, (8, 16, W)); x[q[1]] = 15 * rng.integers(0, 2, (8, 16, W))
    x[:, int(rng.integers(0, 8))] = rng.integers(0, 3, (N, 16, W))
    e = np.argsort(o, axis=-1); home = e[None] % N == np.arange(N)[:, None, None]
    x = np.where(home[:, :, None], rng.integers(0, 3, x.shape), x)
    i = place(e, walk(rng, o, top, P)) // N * N + np.arange(N)[:, None, None, None]
    return pack(x, walk(rng, o, top, H), place(o, np.where(i < W, i, i - N)))
def setup_inputs_spread(rng):
    o = np.argsort(rng.random((8, W)), axis=-1); e = np.argsort(o, axis=-1) % 5
    x = np.floor(rng.random((N, 8, 16, W)) * np.exp2(4.0 - e)[None, :, None, :]).astype(np.int64)
    def some(n):
        k = rng.integers(0, 4, (N, 8, 1, n)); u = rng.random((N, 8, 16, n)); b = 5 * np.floor(u * (W // 5)).astype(np.int64)
        i = np.where(k == 0, np.floor(W * u).astype(np.int64), np.floor(W * u ** 4).astype(np.int64))
        i = np.where(k == 2, b + rng.integers(3, 5, u.shape), np.where(k == 3, b + rng.integers(2, 5, u.shape), i))
        return place(o, np.minimum(i, W - 1))
    return pack(x, some(H), some(P))
def check_inputs(d):
    bad = []; a = np.asarray(d["x"]).astype(np.float32)
    if not np.all((a >= 0) & (a <= 15) & (a == np.floor(a))): bad.append("whole numbers of x")
    for k in ("c0", "r0"):
        if np.min(d[k]) < 0 or np.max(d[k]) > W - 1: bad.append("range of " + k)
    return bad
def look(xs, R):
    return np.take_along_axis(xs, R.reshape(N, 8, 1, 16 * P), axis=3).reshape(N, 8, 16, 16, P)
def far(v, d):
    return np.add.reduce(np.abs(v[:, :, :, :16 - d] - v[:, :, :, d:]), axis=2)
def first(bad):
    return np.where(np.any(bad, axis=2), np.argmax(bad, axis=2), 15)[:, :, None, :]
def reference(x, c0, r0):
    xs = x.astype(np.float32).astype(np.int32).reshape(N, 8, 16, W); C = c0.astype(np.int64).reshape(N, 8, 16, H).copy()
    R = r0.astype(np.int64).reshape(N, 8, 16, P)
    kap = np.zeros(N, np.int64); row = np.arange(16)[None, None, :, None]
    for rnd in range(RO):
        if rnd > 0: R = np.roll(R, ST, axis=0)
        bad = far(look(xs, R), 1) > TH; fail = np.any(bad, axis=2); k = first(bad)
        rk = np.take_along_axis(R, k, 2)[:, :, 0]
        h = (((rk * R[:, :, 15]) >> 6) + rk + kap[:, None, None]) & (H - 1)
        R = np.where((row > k) & (row < 15), np.take_along_axis(C, h[:, :, None, :], 3), R)
        same = R[:, :, :, None] == R[:, :, None]
        q = 15 - np.argmax(same[:, :, :, ::-1], axis=3)
        p = first((q > row)[:, :, :15])
        R = np.where((row >= p) & (row <= np.take_along_axis(q, p, 2)), np.take_along_axis(R, p, 2), R)
        v = look(xs, R); k2 = first(far(v, 1) > TH)
        S = np.where((row > k2) & (row < 15), np.take_along_axis(R, k2, 2), R)
        for j in range(P - 1, -1, -1):
            a, g = np.nonzero(fail[:, :, j])
            C[a, g, :, h[a, g, j]] = S[:, :, :, j][a, g]
        near = far(v, 2) <= TH; R = R.copy()
        R[:, :, 1:14:2] = np.where(near[:, :, 0:13:2], R[:, :, 0:13:2], R[:, :, 1:14:2])
        kap = np.add.reduce(fail.astype(np.int64), axis=(1, 2))
    return {"yc": C.reshape(N, 128, H).astype(np.float32), "yr": R.reshape(N, 128, P).astype(np.float32)}

@@ -1,0 +1,670 @@
+from concourse.mybir import AluOpType as A, ActivationFunctionType as F
+
+W, H, P, RO, ST = 3072, 1024, 512, 3, 2
+SH = 1536
+CH = 256
+NC = P // CH
+NL = CH // 16
+KG = 32
+NAD = 4
+W0 = 128
+RT = 1024 // W0
+KW = CH + 16
+
+SCRATCH = {}
+
+
+def bufs(dtype, **sizes):
+    for k in sizes:
+        SCRATCH[k] = ("sbuf", [128, sizes[k]], dtype)
+
+
+bufs("bfloat16", xs=W, va=16 * P, vd=16 * P, eqw=32 * P, eqp=2048 * NC, sb=P, ind=P, sf=P, ee=P, sm=P, sb2=P, ind2=P, sn=P, lose=P,
+     ka=NC * KW, kb=NC * KW, smask=CH)
+bufs("int32", r0i=P, c0i=H, pri=32, fi=32, si=32, hm=32, ki=8, kp=8, kd=8, ks=8, kw=8)
+bufs("float32", cache=H + P, t1=P, t2=P, t3=P, t4=P, st=P, t5=P, yrs=P, r15=32, rkk=32, djn=32, hf=32, lt=32, lo=32, kacc=8, kcol=8,
+     onesf=128, vt=16, ve=16, rio=16, kf=8, mb=8, dj=32)
+bufs("float16", rf0=P, rf1=P, rf2=P, rn0=P, rn1=P, r2=P, rp=P, indr=P, fr=P, indr2=P, hh=32, hrep=P)
+bufs("uint16", ru=P, rpu=P, hu=32, wu=32)
+bufs("bfloat16", ones=2048, c1536=CH, zero=8, bo=128, bo1=128, ey=128, ney=128, ux=128, u15=128, u15s=128, u15n=128, tl=128, tl2=128,
+     au=128, au16=128, boq=128, boqm=128, boqp=128, hey=128, b8a=8, b8=8, b15=8, mst=144, mstn=144, mst15=144, mst8=144, mqa=128, mq=128,
+     hq=2048, pa=1024, pb=1024, vm=240, qm=128, qp=128)
+for _i in range(NAD):
+    SCRATCH["ad%d" % _i] = ("sbuf", [128, 1024], "bfloat16")
+for _i in range(2):
+    SCRATCH["d%d" % _i] = ("psum", [128, 1024], "float32")
+for _i in range(4):
+    SCRATCH["p%d" % _i] = ("psum", [128, 512], "float32")
+SEMAPHORES = (["qV", "qS", "qT", "qG", "lr", "lx", "lc", "oc"] + ["oy%d" % c for c in range(NC)]
+              + ["ar%d_%d" % (t, c) for t in range(1, RO) for c in range(NC)]
+              + ["ls%d_%d" % (t, c) for t in range(1, RO) for c in range(NC)])
+
+CYC, TCYC, LAT = 0.00083, 0.00042, 0.12
+GF, SCF = 1.56, 3.8
+POOLS = {"AD": ["ad%d" % i for i in range(NAD)], "D": ["d0", "d1"], "B": ["p0", "p1", "p2", "p3"]}
+BIAS = {'B00': 19.2, 'P00': 65.9, 'D00': 1.6, 'N00': 36.2, 'E00': 19.2, 'S00': 31.8, 'A00': 3.7, 'H00': 18.5, 'B01': -42.6, 'P01': 11.0,
+        'D01': 18.9, 'N01': 11.2, 'E01': 2.5, 'S01': -15.0, 'A01': -5.5, 'H01': -15.8, 'W00': -20.7, 'B10': 19.0, 'P10': 37.7, 'D10': 8.5,
+        'N10': 13.8, 'E10': -1.6, 'S10': 40.8, 'A10': 0.6, 'H10': 30.5, 'B11': -19.2, 'P11': 26.7, 'D11': 7.0, 'N11': 24.6, 'E11': 6.7,
+        'S11': 56.7, 'A11': 8.6, 'H11': -69.5, 'W10': -0.9, 'B20': -14.7, 'P20': 43.9, 'D20': 2.5, 'N20': 13.2, 'E20': 29.0, 'S20': 5.9,
+        'A20': 1.3, 'H20': 5.4, 'B21': -0.6, 'P21': 1.2, 'D21': 0.6, 'N21': -12.4, 'E21': -14.3, 'S21': -8.9, 'A21': -47.2, 'H21': -0.4,
+        'W20': -2.2, 'C': 2.7}
+QG = {'A01': 'V', 'D11': 'V'}
+
+
+def build_ops():
+    ops, tiles, cls = [], [], ["C"]
+
+    def tile(pool, chain):
+        tiles.append({"pool": pool, "chain": chain, "users": 0, "buf": None})
+        return ("tile", len(tiles) - 1)
+
+    def op(qs, fn, reads, writes, dur, name="", sem=None):
+        ops.append({"qs": qs, "fn": fn, "r": reads, "w": writes, "dur": dur, "name": name, "sem": sem, "id": len(ops), "cls": cls[0]})
+
+    def R(buf, lo=0, hi=None):
+        if isinstance(buf, tuple):
+            return (buf, 0, 512)
+        return (buf, lo, SCRATCH[buf][1][1] if hi is None else hi)
+
+    def v(fn, reads, writes, cyc, name=""):
+        op("V", fn, reads, writes, 0.055 + CYC * cyc, name)
+
+    def s(fn, reads, writes, cyc, name=""):
+        op("S", fn, reads, writes, 0.065 + CYC * cyc, name)
+
+    def gp(fn, reads, writes, n, name=""):
+        op("G", fn, reads, writes, 0.17 + 2 * CYC * n, name)
+
+    def mm(cols, fn, reads, writes, name=""):
+        op("T", fn, reads, writes, cols * TCYC + 0.03, name)
+
+    def ts(dst, src, s1, o1, s2=None, o2=None, lo=0, hi=1, cyc=64, slo=None, name="ts", extra=()):
+        a, b = (lo, hi) if slo is None else (slo, slo + hi - lo)
+        val = lambda B, x: B(x[0])[:, x[1]:x[1] + 1] if isinstance(x, tuple) else x
+
+        def fn(e, B, inc):
+            if o2 is None:
+                inc(e.tensor_scalar(out=B(dst)[:, lo:hi], in0=B(src)[:, a:b], scalar1=val(B, s1), scalar2=None, op0=o1))
+            else:
+                inc(e.tensor_scalar(out=B(dst)[:, lo:hi], in0=B(src)[:, a:b], scalar1=val(B, s1), scalar2=val(B, s2), op0=o1, op1=o2))
+        cols = [R(x[0], x[1], x[1] + 1) for x in (s1, s2) if isinstance(x, tuple)]
+        v(fn, [R(src, a, b)] + cols, [R(dst, lo, hi)], cyc, name)
+
+    def tt(dst, in0, in1, o, lo, hi, cyc=None, slo=None, name="tt"):
+        a, b = (lo, hi) if slo is None else (slo, slo + hi - lo)
+        v(lambda e, B, inc: inc(e.tensor_tensor(out=B(dst)[:, lo:hi], in0=B(in0)[:, a:b], in1=B(in1)[:, lo:hi], op=o)),
+          [R(in0, a, b), R(in1, lo, hi)], [R(dst, lo, hi)], (hi - lo) if cyc is None else cyc, name)
+
+    def cp(dst, src, lo, hi, cyc, slo=None, name="cp"):
+        a, b = (lo, hi) if slo is None else (slo, slo + hi - lo)
+        v(lambda e, B, inc: inc(e.tensor_copy(out=B(dst)[:, lo:hi], in_=B(src)[:, a:b])), [R(src, a, b)], [R(dst, lo, hi)], cyc, name)
+
+    op("A", lambda e, B, inc: inc(e.dma_start(B("r0i")[:, :], B("IN")["r0"][:, :])), [], [R("r0i")], 2.5, "load r0", sem="lr")
+    op("Y", lambda e, B, inc: inc(e.dma_start(B("xs")[:, :], B("IN")["x"][:, :])), [], [R("xs")], 5.0, "load x", sem="lx")
+    op("Y", lambda e, B, inc: inc(e.dma_start(B("c0i")[:, :], B("IN")["c0"][:, :])), [], [R("c0i")], 4.0, "load c0", sem="lc")
+
+    def fill(buf, val, n, lo=0):
+        v(lambda e, B, inc: inc(e.memset(B(buf)[:, lo:lo + n], val)), [], [R(buf, lo, lo + n)], n / 2)
+
+    def gsel(dst, src, pat, cmp, fillv, base, cm, n, view=None):
+        w = slice(0, n) if view is None else view
+        gp(lambda e, B, inc: inc(e.affine_select(out=B(dst)[:, w], in_=B(src)[:, w], pattern=pat, compare_op=cmp, fill=fillv, base=base, channel_multiplier=cm)),
+           [R(src)], [R(dst)], n, "sel " + dst)
+
+    def scale(dst, src, k):
+        n = SCRATCH[src][1][1]
+        ts(dst, src, float(k), A.mult, hi=n, cyc=n / 2)
+
+    fill("ones", 1.0, 2048)
+    gsel("ey", "ones", [[-1, 128]], A.is_equal, 0.0, 0, 1, 128)
+    gsel("b8a", "ones", [[-16, 8]], A.is_ge, 0.0, 0, 1, 8)
+    gsel("b8", "b8a", [[16, 8]], A.is_ge, 0.0, 15, -1, 8)
+    gsel("b15", "ones", [[-16, 8]], A.is_equal, 0.0, -15, 1, 8)
+    scale("ney", "ey", -1)
+    fill("mst", 0.0, 144)
+    fill("mst15", 0.0, 144)
+    for d_, s_ in (("mst", "b8"), ("mst15", "b15")):
+        v(lambda e, B, inc, d_=d_, s_=s_: inc(e.tensor_copy(out=B(d_)[:, 15:143:16], in_=B(s_)[:, 0:8])), [R(s_)], [R(d_)], 64)
+    scale("mstn", "mst", -1)
+    gsel("bo1", "ones", [[-16, 8], [0, 16]], A.is_ge, 0.0, 0, 1, 128)
+    gsel("bo", "bo1", [[16, 8], [0, 16]], A.is_ge, 0.0, 15, -1, 128)
+    gsel("ux", "bo", [[1, 128]], A.is_gt, 0.0, 0, -1, 128)
+    fill("smask", 1.0, CH)
+    v(lambda e, B, inc: inc(e.memset(B("smask")[:, 15:CH:16], 0.0)), [], [R("smask")], 64)
+    for c in range(NC):
+        fill("ka", 0.0, 16, c * KW)
+        fill("kb", 0.0, 16, c * KW)
+    gsel("u15", "ux", [[0, 8], [-1, 16]], A.is_gt, 0.0, 15, 0, 128)
+    scale("u15s", "u15", -SH)
+    scale("u15n", "u15", -1)
+    gp(lambda e, B, inc: inc(e.iota(B("ki")[:, 0:1], [[0, 1]], 0, 1)), [], [R("ki")], 8)
+    gp(lambda e, B, inc: inc(e.iota(B("rio")[:, 0:16], [[1, 16]], 0, 0, allow_small_or_imprecise_dtypes=True)), [], [R("rio")], 16)
+    gp(lambda e, B, inc: inc(e.iota(B("dj")[:, 0:32], [[16, 32]], H, 0, allow_small_or_imprecise_dtypes=True)), [], [R("dj")], 32)
+    ts("kp", "ki", 15, A.bitwise_and)
+    ts("mb", "kp", 16.0, A.mult, -17.0, A.add)
+    ts("kd", "ki", 4, A.arith_shift_right)
+    tt("ks", "kp", "kd", A.add, 0, 1, 64)
+    ts("kw", "ks", 1.0, A.add)
+    v(lambda e, B, inc: inc(e.tensor_scalar(out=B("ks")[:, 2:3], in0=B("kw")[:, 0:1], scalar1=15, scalar2=None, op0=A.bitwise_and)), [R("kw")], [R("ks")], 64)
+    v(lambda e, B, inc: inc(e.tensor_tensor(out=B("kf")[:, 0:1], in0=B("kp")[:, 0:1], in1=B("ks")[:, 2:3], op=A.min)), [R("kp"), R("ks")], [R("kf", 0, 1)], 64)
+    cp("kf", "kp", 1, 2, 64, slo=0)
+    ts("dj", "dj", ("kf", 1), A.add, hi=32)
+    fill("vm", 0.0, 240)
+    ts("vt", "rio", ("kf", 0), A.is_gt, -100.0, A.mult, hi=16)
+    ts("ve", "rio", ("kf", 0), A.is_equal, hi=16)
+    v(lambda e, B, inc: inc(e.tensor_tensor(out=B("vm")[:, 112:128], in0=B("vt")[:, 0:16], in1=B("ve")[:, 0:16], op=A.add)), [R("vt"), R("ve")], [R("vm")], 64)
+    fill("pa", 0.0, 1024)
+    gsel("pb", "pa", [[-16, 8], [0, 8], [-1, 16]], A.not_equal, 1.0, 0, 1, 1024)
+    gsel("pa", "pb", [[-16, 8], [-1, 8], [-1, 16]], A.not_equal, -1.0, -1, 1, 1024)
+    gsel("pb", "pa", [[-16, 8], [-1, 8], [-1, 16]], A.not_equal, -1.0, 15, 1, 1024)
+    gsel("pa", "pb", [[-16, 8], [0, 128]], A.is_ge, 0.0, 0, 1, 1024)
+    gsel("pb", "pa", [[16, 8], [0, 128]], A.is_ge, 0.0, 15, -1, 1024)
+    scale("boq", "bo", 0.25)
+    scale("hey", "ey", 0.5)
+    tt("boqp", "boq", "hey", A.add, 0, 128, 256)
+    tt("boqm", "boq", "hey", A.subtract, 0, 128, 256)
+    gsel("tl", "bo", [[-1, 128]], A.is_ge, 0.0, 0, 1, 128)
+    scale("tl2", "tl", 2)
+    gsel("au", "bo", [[1, 128]], A.is_ge, 0.0, 0, -1, 128)
+    scale("au16", "au", 16)
+    gsel("hq", "ones", [[-1, 16], [-16, 8], [0, 16]], A.is_equal, 0.0, 0, 1, 2048)
+    gsel("mqa", "ones", [[0, 16], [-16, 8]], A.is_ge, 0.0, 0, 1, 128)
+    gsel("mq", "mqa", [[1, 16], [16, 8]], A.is_ge, 0.0, -1, -1, 128)
+    gsel("mst8", "ones", [[-1, 144]], A.is_equal, 0.0, 15, 16, 144)
+    fill("qm", 0.0, 128)
+    gsel("qm", "qm", [[-2, 64]], A.not_equal, 0.5, 0, 1, 64, slice(1, 128, 2))
+    gsel("qm", "qm", [[-2, 64]], A.not_equal, -0.5, -1, 1, 64, slice(1, 128, 2))
+    v(lambda e, B, inc: inc(e.memset(B("qm")[:, 15:128:16], 0.0)), [], [R("qm")], 64)
+    tt("qp", "qm", "ey", A.add, 0, 128, 256)
+    fill("c1536", float(SH), CH)
+    fill("onesf", 1.0, 128)
+    fill("zero", 0.0, 8)
+    fill("cache", 0.0, P, H)
+    cp("cache", "c0i", 0, H, H)
+    for i, val in ((2, -40.5), (3, 40.5), (4, -0.5)):
+        v(lambda e, B, inc, i=i, val=val: inc(e.memset(B("kf")[:, i:i + 1], val)), [], [R("kf", i, i + 1)], 64)
+
+    def E(B, q, m="mst"):
+        return B(m)[:, 15 - q:143 - q]
+
+    def dist(vb, c, pairs, chain, flip):
+        ds = tile("B", chain)
+        for x in range(CH // W0):
+            for i0 in range(0, len(pairs), RT):
+                part = pairs[i0:i0 + RT]
+                lo, hi = 16 * (c * CH + x * W0), 16 * (c * CH + (x + 1) * W0)
+                d = tile("D", chain + "d")
+                ad = tile("AD", chain + "a")
+
+                def diff(e, B, inc, part=part, d=d, lo=lo, hi=hi):
+                    for i, (p, p2, row) in enumerate(part):
+                        o = B(d)[:, i * W0:(i + 1) * W0]
+                        inc(e.matmul(o, B("ey")[:, :], B(vb)[:, lo + p:hi:16], True, False))
+                        inc(e.matmul(o, B("ney")[:, :], B(vb)[:, lo + p2:hi:16], False, True))
+                mm(2 * W0 * len(part), diff, [R(vb, lo, hi), R("ey"), R("ney")], [R(d)], "diff")
+                w = W0 * len(part)
+                s(lambda e, B, inc, d=d, ad=ad, w=w: inc(e.activation(B(ad)[:, 0:w], B(d)[:, 0:w], F.Abs)), [R(d)], [R(ad)], w, "abs")
+
+                def summ(e, B, inc, part=part, ad=ad, i0=i0, x=x):
+                    for i, (p, p2, row) in enumerate(part):
+                        inc(e.matmul(B(ds)[:, x * W0:(x + 1) * W0], E(B, row), B(ad)[:, i * W0:(i + 1) * W0], i0 + i == 0, i0 + i == len(pairs) - 1))
+
+                def sumf(e, B, inc, part=part, ad=ad, x=x):
+                    b0 = x * W0
+                    for i, (p, p2, row) in enumerate(part):
+                        inc(e.matmul(B(ds)[:, b0 + row:b0 + 128:16], B(ad)[:, i * W0:i * W0 + 128], B("b8")[:, 0:8], True, True))
+                    if part[-1] == pairs[-1]:
+                        inc(e.matmul(B(ds)[:, b0 + 15:b0 + 128:16], B(ad)[:, 0:128], B("zero")[:, 0:8], True, True))
+                if flip:
+                    mm(W0 // 2 * len(part), sumf, [R(ad), R("b8"), R("zero")], [R(ds)], "sum")
+                else:
+                    mm(W0 * len(part), summ, [R(ad), R("mst")], [R(ds)], "sum")
+        return ds
+
+    def gather(vb, off, c):
+        for j in range(c * CH, (c + 1) * CH, KG):
+            def fn(e, B, inc, j=j):
+                o, w = B(vb)[:, 16 * j:16 * (j + KG)], B("xs")[:, 0:W].indirect(B(off)[:, j:j + KG])
+                if B("Q") == "V":
+                    inc(e.tensor_copy(out=o, in_=w))
+                else:
+                    inc(e.activation(o, w, F.Copy))
+            op(QG.get(cls[0], "VS"), fn, [R("xs"), R(off, j, j + KG)], [R(vb, 16 * j, 16 * (j + KG))], 0.06 + GF * CYC * 16 * KG, "gather")
+
+    def first_fail(ds, c, sbuf, kbuf, ibuf, chain, kacc=None):
+        j0, j1, i0 = c * CH, (c + 1) * CH, 16 + c * KW
+        s(lambda e, B, inc: inc(e.activation(B(sbuf)[:, j0:j1], B(ds)[:, 0:CH], F.Sign, bias=B("kf")[:, 2:3])), [R(ds), R("kf")], [R(sbuf, j0, j1)], CH, "bad")
+        v(lambda e, B, inc: inc(e.tensor_tensor_scan(B(kbuf)[:, i0:i0 + CH], B("smask")[:, 0:CH], B(sbuf)[:, j0:j1], 0.0, A.mult, A.max)),
+          [R("smask"), R(sbuf, j0, j1)], [R(kbuf, i0, i0 + CH)], CH / 2, "scan")
+        qt = tile("B", chain)
+
+        def fq(e, B, inc):
+            for x in range(0, CH, 128):
+                inc(e.matmul(B(qt)[:, x:x + 128], B(kbuf)[:, i0 + x:i0 + x + 128], B("ey")[:, :], True, False))
+                inc(e.matmul(B(qt)[:, x:x + 128], B(kbuf)[:, i0 + x - 1:i0 + x + 127], B("ney")[:, :], False, True))
+        mm(2 * CH, fq, [R("ey"), R("ney"), R(kbuf, i0 - 1, i0 + CH)], [R(qt)], "q")
+        if kacc is None:
+            def fn(e, B, inc):
+                if B("Q") == "S":
+                    inc(e.activation(B(ibuf)[:, j0:j1], B(qt)[:, 0:CH], F.Relu))
+                else:
+                    inc(e.tensor_scalar(out=B(ibuf)[:, j0:j1], in0=B(qt)[:, 0:CH], scalar1=0.0, scalar2=None, op0=A.max))
+            op("SV", fn, [R(qt)], [R(ibuf, j0, j1)], 0.06 + CYC * CH, "ind")
+        else:
+            op("S", lambda e, B, inc: inc(e.activation(B(ibuf)[:, j0:j1], B(qt)[:, 0:CH], F.Relu, accum_out=B("kacc")[:, kacc:kacc + 1])),
+               [R(qt)], [R(ibuf, j0, j1), R("kacc", kacc, kacc + 1)], 0.2 + CYC * CH, "ind")
+
+    def phase_a(t, c):
+        j0, j1, rf, ch = c * CH, (c + 1) * CH, "rf%d" % t, "A%d_%d" % (t, c)
+        if t == 0:
+            cp("ru", "r0i", j0, j1, CH)
+            ts(rf, "r0i", float(-SH), A.add, lo=j0, hi=j1, cyc=CH)
+        else:
+            ts("ru", rf, float(SH), A.add, lo=j0, hi=j1, cyc=CH / 2)
+        gather("va", "ru", c)
+        l15 = tile("B", ch + "r")
+
+        def f15(e, B, inc):
+            for q in range(16):
+                inc(e.matmul(B(l15)[:, 0:NL], E(B, q, "mst15"), B(rf)[:, j0 + q:j1:16], q == 0, q == 15))
+        mm(16 * 64, f15, [R("mst15"), R(rf, j0, j1)], [R(l15)], "r15")
+        ts("r15", l15, float(SH), A.add, lo=c * NL, hi=(c + 1) * NL, slo=0, name="r15")
+        ds = dist("va", c, [(p, p + 1, p) for p in range(15)], ch, True)
+        first_fail(ds, c, "sb", "ka", "ind", ch, t * NC + c if t < RO - 1 else None)
+
+    def phase_b(t, c):
+        j0, j1, k0, k1 = c * CH, (c + 1) * CH, c * NL, (c + 1) * NL
+        rf, ch = "rf%d" % t, "B%d_%d" % (t, c)
+        wm = tile("B", ch)
+
+        def fwm(e, B, inc):
+            inc(e.matmul(B(wm)[:, 0:CH], B("ey")[:, :], B(rf)[:, j0:j1], True, False))
+            inc(e.matmul(B(wm)[:, 0:CH], B("u15s")[:, :], B("ind")[:, j0:j1], False, True))
+            inc(e.matmul(B(wm)[:, CH:2 * CH], B("u15")[:, :], B("ind")[:, j0:j1], True, True))
+        mm(3 * CH, fwm, [R("ey"), R("u15"), R("u15s"), R(rf, j0, j1), R("ind", j0, j1)]
+           + ([R("kcol", t, t + 1)] if t else []) + ([R("cache")] if t and c else []), [R(wm)], "wm")
+        tt("indr", wm, "ind", A.mult, j0, j1, slo=0, name="indr")
+        ll = tile("B", ch)
+
+        def ffl(e, B, inc):
+            for q in range(16):
+                inc(e.matmul(B(ll)[:, NL:2 * NL], E(B, q, "mstn"), B("ind")[:, j0 + q:j1:16], q == 0, False))
+            inc(e.matmul(B(ll)[:, NL:2 * NL], B("ey")[:, :], B("ones")[:, 0:NL], False, True))
+        mm(17 * 64, ffl, [R("mstn"), R("ey"), R("ones"), R("ind", j0, j1)], [R(ll)], "fail list")
+
+        def frk(e, B, inc):
+            for q in range(16):
+                inc(e.matmul(B(ll)[:, 0:NL], E(B, q), B("indr")[:, j0 + q:j1:16], q == 0, False))
+            inc(e.matmul(B(ll)[:, 0:NL], B("ey")[:, :], B("c1536")[:, 0:NL], False, True))
+        mm(17 * 64, frk, [R("mst"), R("ey"), R("c1536"), R("indr", j0, j1)], [R(ll)], "rk list")
+        tt("pri", ll, "r15", A.mult, k0, k1, 64, slo=0, name="l")
+        if t:
+            ts("rkk", ll, ("kcol", t), A.add, lo=k0, hi=k1, slo=0, name="l")
+        tt("djn", ll, "dj", A.mult, k0, k1, 64, slo=NL, name="l")
+        ts("fi", "pri", 6, A.arith_shift_right, lo=k0, hi=k1, name="l")
+        if t:
+            tt("si", "rkk", "fi", A.add, k0, k1, 64, name="l")
+        else:
+            tt("si", ll, "fi", A.add, k0, k1, 64, slo=0, name="l")
+        ts("hm", "si", H - 1, A.bitwise_and, lo=k0, hi=k1, name="l")
+        tt("hf", "hm", "djn", A.max, k0, k1, 64, name="l")
+        cp("hu", "hf", k0, k1, 64, name="hu")
+        cls[0] = "P%d%d" % (t, c)
+        v(lambda e, B, inc: inc(e.tensor_tensor(out=B("t1")[:, j0:j1], in0=B("cache")[:, 0:H + P].indirect(B("hu")[:, k0:k1]), in1=B(rf)[:, j0:j1], op=A.subtract)),
+          [R("cache"), R("hu", k0, k1), R(rf, j0, j1)], [R("t1", j0, j1)], GF * CH, "cache gather")
+        tt("t2", wm, "t1", A.mult, j0, j1, slo=CH, name="t2")
+        tt("r2", wm, "t2", A.add, j0, j1, slo=0, name="r2")
+        gpt, b0 = 1024 // CH, c * 2048
+        for g0 in range(0, 8, gpt):
+            d = tile("D", ch + "p")
+
+            def fpr(e, B, inc, d=d, g0=g0):
+                for i in range(gpt):
+                    inc(e.matmul(B(d)[:, i * CH:(i + 1) * CH], B("pb")[:, 128 * (g0 + i):128 * (g0 + i + 1)], B("r2")[:, j0:j1], True, True))
+            mm(gpt * CH, fpr, [R("pb"), R("r2", j0, j1)], [R(d)], "pairs")
+            ts("eqp", d, 0.0, A.is_equal, lo=b0 + g0 * CH, hi=b0 + (g0 + gpt) * CH, cyc=gpt * CH, slo=0, name="eq")
+        vt = tile("B", ch)
+
+        def fv(e, B, inc):
+            for g in range(8):
+                inc(e.matmul(B(vt)[:, 0:CH], B("vm")[:, 112 - 16 * g:240 - 16 * g], B("eqp")[:, b0 + g * CH:b0 + (g + 1) * CH], g == 0, g == 7))
+        mm(8 * CH, fv, [R("vm"), R("eqp", b0, b0 + 8 * CH)], [R(vt)], "V")
+        s(lambda e, B, inc: inc(e.activation(B("sf")[:, j0:j1], B(vt)[:, 0:CH], F.Sign, bias=B("kf")[:, 4:5])), [R(vt), R("kf")], [R("sf", j0, j1)], CH, "f")
+        rc = tile("B", ch)
+        mm(CH, lambda e, B, inc: inc(e.matmul(B(rc)[:, 0:CH], B("ey")[:, :], B("r2")[:, j0:j1], True, True)), [R("ey"), R("r2", j0, j1)], [R(rc)], "copy r2")
+        tt("fr", rc, "sf", A.mult, j0, j1, slo=0, name="fr")
+        xm = tile("B", ch)
+
+        def fxm(e, B, inc):
+            inc(e.matmul(B(xm)[:, 0:CH], B("boqm")[:, :], B("r2")[:, j0:j1], True, False))
+            inc(e.matmul(B(xm)[:, 0:CH], B("boq")[:, :], B("fr")[:, j0:j1], False, True))
+        mm(2 * CH, fxm, [R("boqm"), R("boq"), R("r2", j0, j1), R("fr", j0, j1)], [R(xm)], "xm")
+        ts("ee", xm, 0.0, A.is_equal, lo=j0, hi=j1, cyc=CH, slo=0, name="E")
+        v2 = tile("B", ch)
+
+        def fv2(e, B, inc):
+            inc(e.matmul(B(v2)[:, 0:CH], B("au16")[:, :], B("sf")[:, j0:j1], True, False))
+            inc(e.matmul(B(v2)[:, 0:CH], B("tl2")[:, :], B("ee")[:, j0:j1], False, True))
+        mm(2 * CH, fv2, [R("au16"), R("tl2"), R("sf", j0, j1), R("ee", j0, j1)], [R(v2)], "v2")
+        s(lambda e, B, inc: inc(e.activation(B("sm")[:, j0:j1], B(v2)[:, 0:CH], F.Sign, bias=B("mb")[:, 0:1])), [R(v2), R("mb")], [R("sm", j0, j1)], CH, "M")
+        tt("t3", xm, "sm", A.mult, j0, j1, slo=0, name="t3")
+        xp = tile("B", ch)
+
+        def fxp(e, B, inc):
+            inc(e.matmul(B(xp)[:, 0:CH], B("boqp")[:, :], B("r2")[:, j0:j1], True, False))
+            inc(e.matmul(B(xp)[:, 0:CH], B("boq")[:, :], B("fr")[:, j0:j1], False, True))
+        mm(2 * CH, fxp, [R("boqp"), R("boq"), R("r2", j0, j1), R("fr", j0, j1), R("sm", j0, j1)], [R(xp)], "xp")
+        tt("rp", xp, "t3", A.add, j0, j1, slo=0, name="rp")
+        ts("rpu", "rp", float(SH), A.add, lo=j0, hi=j1, cyc=CH / 2, name="rpu")
+
+    def hrep(t, c):
+        j0, j1, k0, k1 = c * CH, (c + 1) * CH, c * NL, (c + 1) * NL
+        cp("hh", "hf", k0, k1, 64, name="hh")
+        hr = tile("B", "H%d_%d" % (t, c))
+
+        def fh(e, B, inc):
+            for q in range(16):
+                inc(e.matmul(B(hr)[:, q:CH:16], B("hq")[:, 128 * q:128 * (q + 1)], B("hh")[:, k0:k1], True, True))
+        mm(16 * 64, fh, [R("hq"), R("hh", k0, k1)], [R(hr)], "hrep")
+        cp("hrep", hr, j0, j1, CH, slo=0, name="hrep")
+
+    def winners(t):
+        if t < RO - 1:
+            kt = tile("B", "K%d" % t)
+
+            def fk(e, B, inc):
+                for c in range(NC):
+                    inc(e.matmul(B(kt)[:, 0:1], B("onesf")[:, :], B("kacc")[:, t * NC + c:t * NC + c + 1], c == 0, c == NC - 1))
+            mm(256 * NC, fk, [R("onesf"), R("kacc", t * NC, t * NC + NC)], [R(kt)], "K")
+            cp("kcol", kt, t + 1, t + 2, 64, slo=0, name="K")
+        for k in range(32):
+            n = P - 16 * k
+            v(lambda e, B, inc, k=k, n=n: inc(e.tensor_scalar(out=B("eqw")[:, P * k:P * k + n], in0=B("hrep")[:, 16 * k:P], scalar1=B("hf")[:, k:k + 1], scalar2=None, op0=A.is_equal)),
+              [R("hrep", 16 * k, P), R("hf", k, k + 1)], [R("eqw", P * k, P * k + n)], n / 2, "win")
+        z = tile("B", "W%d" % t)
+        for k0 in range(0, 32, 4):
+            def fz(e, B, inc, k0=k0):
+                if k0 == 0:
+                    inc(e.matmul(B(z)[0:8, 0:P], B("zero")[:, 0:8], B("eqw")[:, 0:P], True, False))
+                for k in range(k0, min(k0 + 4, 31)):
+                    inc(e.matmul(B(z)[0:8, 16 * (k + 1):P], B("b8")[:, 0:8], B("eqw")[:, P * k + 16:P * k + P - 16 * k], False, False))
+            mm(4 * (P - 16 * k0), fz, [R("zero"), R("b8"), R("eqw", P * k0, P * (k0 + 3) + P - 16 * (k0 + 3))], [R(z)], "Z")
+
+        def fzd(e, B, inc):
+            for q in range(16):
+                inc(e.matmul(B(z)[0:8, q:P:16], B("mq")[:, 8 * q:8 * q + 8], B("eqw")[:, q:32 * P:P], False, q == 15))
+        mm(16 * 32, fzd, [R("mq"), R("eqw")], [R(z)], "Zd")
+        s(lambda e, B, inc: inc(e.activation(B("lose")[0:8, 0:P], B(z)[0:8, 0:P], F.Sign)), [R(z)], [R("lose")], P, "lose")
+        wl = tile("B", "W%d" % t)
+
+        def fl(e, B, inc):
+            for q in range(16):
+                inc(e.matmul(B(wl)[:, 0:32], B("mst8")[0:8, 15 - q:143 - q], B("lose")[0:8, q:P:16], q == 0, q == 15))
+        mm(16 * 64, fl, [R("mst8"), R("lose")], [R(wl)], "lose list")
+        tt("lt", wl, "dj", A.mult, 0, 32, 64, name="w")
+        tt("lo", "lt", "hf", A.max, 0, 32, 64, name="w")
+        cp("wu", "lo", 0, 32, 64, name="w")
+
+    def phase_d(t, c):
+        ch = "D%d_%d" % (t, c)
+        gather("vd", "rpu", c)
+        ds = dist("vd", c, [(p, p + 1, p) for p in range(15)], ch, True)
+        first_fail(ds, c, "sb2", "kb", "ind2", ch)
+        cls[0] = "N%d%d" % (t, c)
+        return dist("vd", c, [(p, p + 2, p + 1) for p in range(0, 14, 2)], ch + "n", False)
+
+    def phase_e(t, c, dn):
+        j0, j1, ch = c * CH, (c + 1) * CH, "E%d_%d" % (t, c)
+        s(lambda e, B, inc: inc(e.activation(B("sn")[:, j0:j1], B(dn)[:, 0:CH], F.Sign, scale=-1.0, bias=B("kf")[:, 3:4])), [R(dn), R("kf")], [R("sn", j0, j1)], CH, "near")
+        n1 = tile("B", ch + "n")
+
+        def f6(e, B, inc):
+            inc(e.matmul(B(n1)[:, 0:CH], B("qm")[:, :], B("rp")[:, j0:j1], True, True))
+            inc(e.matmul(B(n1)[:, CH:2 * CH], B("qp")[:, :], B("rp")[:, j0:j1], True, t < RO - 1))
+            if t == RO - 1:
+                inc(e.matmul(B(n1)[:, CH:2 * CH], B("ey")[:, :], B("c1536")[:, :], False, True))
+        mm(2 * CH, f6, [R("qm"), R("qp"), R("ey"), R("c1536"), R("rp", j0, j1), R("sn", j0, j1)], [R(n1)], "n1")
+        tt("t5", n1, "sn", A.mult, j0, j1, slo=0, name="t5")
+        out = "yrs" if t == RO - 1 else "rn%d" % t
+        tt(out, n1, "t5", A.add, j0, j1, slo=CH, name="rn")
+        if t == RO - 1:
+            op("Y", lambda e, B, inc: inc(e.dma_start(B("IN")["yr"][:, j0:j1], B("yrs")[:, j0:j1])), [R("yrs", j0, j1)], [("yr", j0, j1)], 2.5, "store yr", sem="oy%d" % c)
+        else:
+            op("G", ("send", t, c, j0, j1), [R(out, j0, j1)], [], 1.0, "send", sem="ls%d_%d" % (t + 1, c))
+            ops[-1]["sem2"] = "ar%d_%d" % (t + 1, c)
+            op("N", ("arrive", t + 1, c), [R(out, j0, j1)], [R("rf%d" % (t + 1), j0, j1)], 3.5, "arrive", sem="ar%d_%d" % (t + 1, c))
+            ops[-1]["after"] = len(ops) - 2
+        cls[0] = "S%d%d" % (t, c)
+        om = tile("B", ch)
+
+        def fom(e, B, inc):
+            inc(e.matmul(B(om)[:, 0:CH], B("ey")[:, :], B("ones")[:, 0:CH], True, False))
+            inc(e.matmul(B(om)[:, 0:CH], B("u15n")[:, :], B("ind2")[:, j0:j1], False, True))
+            inc(e.matmul(B(om)[:, CH:2 * CH], B("ey")[:, :], B("rp")[:, j0:j1], True, True))
+        mm(3 * CH, fom, [R("ey"), R("ones"), R("u15n"), R("ind2", j0, j1), R("rp", j0, j1)], [R(om)], "om")
+        tt("indr2", om, "ind2", A.mult, j0, j1, slo=CH, name="indr2")
+        tt("t4", om, "rp", A.mult, j0, j1, slo=0, name="t4")
+        sk = tile("B", ch)
+
+        def fsk(e, B, inc):
+            inc(e.matmul(B(sk)[:, 0:CH], B("ey")[:, :], B("c1536")[:, :], True, False))
+            inc(e.matmul(B(sk)[:, 0:CH], B("u15")[:, :], B("indr2")[:, j0:j1], False, True))
+        mm(2 * CH, fsk, [R("ey"), R("c1536"), R("u15"), R("indr2", j0, j1)], [R(sk)], "sk")
+        tt("st", sk, "t4", A.add, j0, j1, slo=0, name="st")
+        k0, k1 = c * NL, (c + 1) * NL
+        v(lambda e, B, inc: inc(e.tensor_copy(out=B("cache")[:, 0:H + P].indirect(B("wu")[:, k0:k1]), in_=B("st")[:, j0:j1])),
+          [R("wu", k0, k1), R("st", j0, j1)], [R("cache")], SCF * CH, "scatter")
+
+    for t in range(RO):
+        for c in range(NC):
+            cls[0] = "A%d%d" % (t, c)
+            phase_a(t, c)
+        for c in range(NC):
+            cls[0] = "B%d%d" % (t, c)
+            phase_b(t, c)
+            cls[0] = "H%d%d" % (t, c)
+            hrep(t, c)
+        cls[0] = "W%d0" % t
+        winners(t)
+        for c in range(NC):
+            cls[0] = "D%d%d" % (t, c)
+            dn = phase_d(t, c)
+            cls[0] = "E%d%d" % (t, c)
+            phase_e(t, c, dn)
+    op("Y", lambda e, B, inc: inc(e.dma_start(B("IN")["yc"][:, :], B("cache")[:, 0:H])), [R("cache", 0, H)], [("yc", 0, H)], 3.0, "store yc", sem="oc")
+    return ops, tiles
+
+
+def deps_of(ops, key, cross):
+    hist, out = {}, []
+    for o in ops:
+        d = {}
+        for rw, regs in (("r", o["r"]), ("w", o["w"])):
+            for (b, lo, hi) in regs:
+                for (lo2, hi2, rw2, o2) in hist.get(key(b), ()):
+                    if o2 is o or lo2 >= hi or hi2 <= lo:
+                        continue
+                    kind = rw2 + rw
+                    if kind == "rr" and not (cross(b) and o2["q"] != o["q"]):
+                        continue
+                    d.setdefault(o2["id"], set()).add((kind, cross(b)))
+        if "after" in o:
+            d.setdefault(o["after"], set()).add(("wr", False))
+        for rw, regs in (("r", o["r"]), ("w", o["w"])):
+            for (b, lo, hi) in regs:
+                h = hist.setdefault(key(b), [])
+                if rw == "w" and not cross(b):
+                    h[:] = [x for x in h if not (lo <= x[0] and x[1] <= hi)]
+                h.append((lo, hi, rw, o))
+        out.append(d)
+    return out
+
+
+PSUM = set(k for k in SCRATCH if SCRATCH[k][0] == "psum")
+
+
+def is_tile(b):
+    return b in PSUM
+
+
+def schedule():
+    ops, tiles = build_ops()
+    for o in ops:
+        o["q"] = o["qs"][0]
+        for b, lo, hi in o["r"] + o["w"]:
+            if isinstance(b, tuple):
+                tiles[b[1]]["users"] += 1
+    dep = deps_of(ops, lambda b: b, lambda b: isinstance(b, tuple) and tiles[b[1]]["pool"] != "AD")
+    n = len(ops)
+    succ = [[] for _ in range(n)]
+    left = [len(dep[i]) for i in range(n)]
+    for i in range(n):
+        for d in dep[i]:
+            succ[d].append(i)
+    rank = [0.0] * n
+    for i in range(n - 1, -1, -1):
+        rank[i] = ops[i]["dur"] + max([rank[j] + LAT for j in succ[i]] or [0.0])
+    for i in range(n):
+        rank[i] += BIAS.get(ops[i]["cls"], 0.0)
+    free = {q: 0.0 for q in "VSTGYAN"}
+    pool = {k: {b: 0.0 for b in v_} for k, v_ in POOLS.items()}
+    live, endt, order = {}, [0.0] * n, []
+    ready = [i for i in range(n) if left[i] == 0]
+    while ready:
+        cands = []
+        for i in ready:
+            o = ops[i]
+            est0 = max([endt[d] + (LAT if any(k != "rw" for k, _ in kk) or ops[d]["q"] != o["qs"][0] else 0.0) for d, kk in dep[i].items()] or [0.0])
+            okay = True
+            for b, lo, hi in o["w"]:
+                if isinstance(b, tuple) and tiles[b[1]]["buf"] is None:
+                    tl = tiles[b[1]]
+                    fr = pool[tl["pool"]]
+                    if not fr or (tl["pool"] == "B" and len(fr) < 2 and not live.get(tl["chain"], 0)):
+                        okay = False
+                    else:
+                        est0 = max(est0, min(fr.values()) + LAT)
+            if okay:
+                for q in o["qs"]:
+                    cands.append((max(est0, free[q] if q != "N" else 0.0), -rank[i], i, q))
+        assert cands, "no operation can go on"
+        t0 = min(c[0] for c in cands)
+        st, _, i, q = min([c for c in cands if c[0] <= t0 + 0.03], key=lambda c: (c[1], c[0]))
+        o = ops[i]
+        o["q"] = q
+        for b, lo, hi in o["w"]:
+            if isinstance(b, tuple) and tiles[b[1]]["buf"] is None:
+                tl = tiles[b[1]]
+                fr = pool[tl["pool"]]
+                bb = min(fr, key=lambda x: fr[x])
+                del fr[bb]
+                tl["buf"] = bb
+                live[tl["chain"]] = live.get(tl["chain"], 0) + 1
+        e = st + o["dur"]
+        endt[i], o["t0"], o["t1"] = e, st, e
+        free[q] = st + 0.1 if q in "YA" else e
+        if q == "A":
+            free["S"] = max(free["S"], 0.1)
+        for b, lo, hi in o["r"] + o["w"]:
+            if isinstance(b, tuple):
+                tl = tiles[b[1]]
+                tl["users"] -= 1
+                tl["end"] = max(tl.get("end", 0.0), e)
+                if tl["users"] == 0:
+                    pool[tl["pool"]][tl["buf"]] = tl["end"]
+                    live[tl["chain"]] -= 1
+        order.append(i)
+        ready.remove(i)
+        for j in succ[i]:
+            left[j] -= 1
+            if left[j] == 0:
+                ready.append(j)
+    assert len(order) == n
+    return [ops[i] for i in order], tiles, max(endt)
+
+
+PLAN = {}
+
+
+def plan():
+    if not PLAN:
+        seq, tiles, end = schedule()
+        key = lambda b: tiles[b[1]]["buf"] if isinstance(b, tuple) else b
+        PLAN["seq"], PLAN["tiles"], PLAN["end"] = seq, tiles, end
+        PLAN["dep"] = deps_of(seq, key, lambda b: is_tile(key(b)))
+    return PLAN
+
+
+def rank_program(g, core, T, topo):
+    rank = T.rank_of(core)
+    if rank is None:
+        return
+    pl = plan()
+    tiles = pl["tiles"]
+    dst = T.cores[(rank + ST) % len(T.cores)]
+    src = T.cores[(rank - ST) % len(T.cores)]
+    rid, pid, _ = topo.addr(dst)
+    emask, ne, ne_in = topo.mask(core, dst), len(topo.engines(core, dst)), len(topo.engines(src, core))
+    eng = {"V": g.vector, "S": g.scalar, "T": g.tensor, "G": g, "Y": g.sync, "A": g.scalar}
+    host = {"V": "V", "S": "S", "T": "T", "G": "G", "Y": "Y", "A": "S"}
+    ins = {"x": T.x, "r0": T.r0, "c0": T.c0, "yc": T.yc, "yr": T.yr}
+    cur = ["V"]
+
+    def B(name):
+        if name == "Q":
+            return cur[0]
+        if name == "IN":
+            return ins
+        return T[tiles[name[1]]["buf"]] if isinstance(name, tuple) else T[name]
+
+    cnt = {"V": 0, "S": 0, "T": 0, "G": 0}
+    known = {q: {} for q in "VSTGY"}
+    done, pend = {}, {}
+
+    def inc(x, q):
+        cnt[q] += 1
+        x.then_inc(T.sem["q" + q], 1)
+
+    for o, dep in zip(pl["seq"], pl["dep"]):
+        q = o["q"]
+        if q == "N":
+            done[o["id"]] = (o["sem"], ne_in, {})
+            pend[o["sem"]] = ne_in
+            continue
+        h = host[q]
+        kn, need = known[h], {}
+        for d, kinds in dep.items():
+            sem, c, imp = done[d]
+            if sem == "q" + h:
+                if (h == "T" and all(cr for _, cr in kinds)) or all(k == "rw" for k, _ in kinds):
+                    continue
+            if c > need.get(sem, (0, None))[0]:
+                need[sem] = (c, imp)
+        for sem in sorted(need, key=lambda x: -need[x][0]):
+            c, imp = need[sem]
+            if kn.get(sem, 0) >= c:
+                continue
+            eng[q].wait_ge(T.sem[sem], c)
+            kn[sem] = c
+            for s2, c2 in imp.items():
+                kn[s2] = max(kn.get(s2, 0), c2)
+        cur[0] = q
+        if isinstance(o["fn"], tuple):
+            _, t, c, j0, j1 = o["fn"]
+            g.remote_dma(T["rf%d" % (t + 1)][:, j0:j1], T["rn%d" % t][:, j0:j1], T.sem[o["sem2"]], T.sem[o["sem"]], pid, rid, emask)
+            done[o["id"]] = (o["sem"], ne, {})
+            pend[o["sem"]] = ne
+        elif o["sem"]:
+            o["fn"](eng[q], B, lambda x: x.then_inc(T.sem[o["sem"]], 16))
+            done[o["id"]] = (o["sem"], 16, dict(kn))
+            pend[o["sem"]] = 16
+        else:
+            o["fn"](eng[q], B, lambda x: inc(x, h))
+            imp = dict(kn)
+            imp["q" + h] = cnt[h]
+            done[o["id"]] = ("q" + h, cnt[h], imp)
+    for q in "VSTG":
+        g.wait_ge(T.sem["q" + q], cnt[q])
+    for sname in pend:
+        if known["G"].get(sname, 0) < pend[sname]:
+            g.wait_ge(T.sem[sname], pend[sname])

@@ -1,15 +1,16 @@
-from concourse.mybir import AluOpType as A, ActivationFunctionType as F
+from concourse.mybir import AluOpType as A, ActivationFunctionType as F, AxisListType as AX
 
 W, H, P, RO, ST = 3072, 1024, 512, 3, 2
 SH = 1536
 CH = 256
 NC = P // CH
 NL = CH // 16
+BL = 128
+NB = P // BL
 KG = 32
-NAD = 4
-W0 = 128
-RT = 1024 // W0
-KW = CH + 16
+SC = 128
+D0 = 16
+KA, KB = CH + 16, BL + 16
 
 SCRATCH = {}
 
@@ -19,43 +20,34 @@ def bufs(dtype, **sizes):
         SCRATCH[k] = ("sbuf", [128, sizes[k]], dtype)
 
 
-bufs("bfloat16", xs=W, va=16 * P, vd=16 * P, eqw=32 * P, eqp=2048 * NC, sb=P, ind=P, sf=P, ee=P, sm=P, sb2=P, ind2=P, sn=P, lose=P,
-     ka=NC * KW, kb=NC * KW, smask=CH)
-bufs("int32", r0i=P, c0i=H, pri=32, fi=32, si=32, hm=32, ki=8, kp=8, kd=8, ks=8, kw=8)
-bufs("float32", cache=H + P, t1=P, t2=P, t3=P, t4=P, st=P, t5=P, yrs=P, r15=32, rkk=32, djn=32, hf=32, lt=32, lo=32, kacc=8, kcol=8,
-     onesf=128, vt=16, ve=16, rio=16, kf=8, mb=8, dj=32)
-bufs("float16", rf0=P, rf1=P, rf2=P, rn0=P, rn1=P, r2=P, rp=P, indr=P, fr=P, indr2=P, hh=32, hrep=P)
-bufs("uint16", ru=P, rpu=P, hu=32, wu=32)
-bufs("bfloat16", ones=2048, c1536=CH, zero=8, bo=128, bo1=128, ey=128, ney=128, ux=128, u15=128, u15s=128, u15n=128, tl=128, tl2=128,
-     au=128, au16=128, boq=128, boqm=128, boqp=128, hey=128, b8a=8, b8=8, b15=8, mst=144, mstn=144, mst15=144, mst8=144, mqa=128, mq=128,
-     hq=2048, pa=1024, pb=1024, vm=240, qm=128, qp=128)
-for _i in range(NAD):
-    SCRATCH["ad%d" % _i] = ("sbuf", [128, 1024], "bfloat16")
-for _i in range(2):
-    SCRATCH["d%d" % _i] = ("psum", [128, 1024], "float32")
-for _i in range(4):
+bufs("bfloat16", xs=W, va=16 * P, vd=16 * P, mx=16 * P, md=16 * P, m2=8 * P, ka=NC * KA, kb=NB * KB, sn=NB * KB, nm=P, nq=P,
+     eqp=8 * P, eqh=256)
+bufs("float16", rf=P, indr=P, r2=P, hh=32)
+bufs("uint16", ru0=P, ru1=P, ru2=P, rn0=P, rn1=P, r2u=P, hu=32, wu=64)
+bufs("int32", r0i=P, c0i=H, pi=32, hm=32, ki=8, kp=8, ks=8, kt=8, ia=256, ib=256)
+bufs("float32", cache=D0 + H, t1=P, yp=P, y2=P, t5=P, st=P, yrs=P, r15=32, pri=32, kacc=8, kcol=8, col=16, rio=16, fa=16, fb=16, fc=16,
+     onesf=128, zerof=128, tri=128, tra=128, tro=128, trb=128, ioh=128, t15=128, kw=128)
+bufs("bfloat16", ones=CH, zero=256, ey=128, ney=128, b2=16, b2a=16, bm=16, bma=16, ci=256, ca=CH, nw=256, cap=CH, ms=432, c192=16, ni15=128,
+     c15=128, pq=256, pd=128, pb=1024, vw=480, dl=128)
+NPS = 8
+for _i in range(NPS):
     SCRATCH["p%d" % _i] = ("psum", [128, 512], "float32")
-SEMAPHORES = (["qV", "qS", "qT", "qG", "lr", "lx", "lc", "oc"] + ["oy%d" % c for c in range(NC)]
-              + ["ar%d_%d" % (t, c) for t in range(1, RO) for c in range(NC)]
-              + ["ls%d_%d" % (t, c) for t in range(1, RO) for c in range(NC)])
+SEMAPHORES = (["qV", "qS", "qT", "qG", "lr", "lx", "lc", "oc"] + ["oy%d" % b for b in range(NB)]
+              + ["ar%d_%d" % (t, b) for t in range(1, RO) for b in range(NB)]
+              + ["ls%d_%d" % (t, b) for t in range(1, RO) for b in range(NB)])
 
-CYC, TCYC, LAT = 0.00083, 0.00042, 0.12
-GF, SCF = 1.56, 3.8
-POOLS = {"AD": ["ad%d" % i for i in range(NAD)], "D": ["d0", "d1"], "B": ["p0", "p1", "p2", "p3"]}
-BIAS = {'B00': 19.2, 'P00': 65.9, 'D00': 1.6, 'N00': 36.2, 'E00': 19.2, 'S00': 31.8, 'A00': 3.7, 'H00': 18.5, 'B01': -42.6, 'P01': 11.0,
-        'D01': 18.9, 'N01': 11.2, 'E01': 2.5, 'S01': -15.0, 'A01': -5.5, 'H01': -15.8, 'W00': -20.7, 'B10': 19.0, 'P10': 37.7, 'D10': 8.5,
-        'N10': 13.8, 'E10': -1.6, 'S10': 40.8, 'A10': 0.6, 'H10': 30.5, 'B11': -19.2, 'P11': 26.7, 'D11': 7.0, 'N11': 24.6, 'E11': 6.7,
-        'S11': 56.7, 'A11': 8.6, 'H11': -69.5, 'W10': -0.9, 'B20': -14.7, 'P20': 43.9, 'D20': 2.5, 'N20': 13.2, 'E20': 29.0, 'S20': 5.9,
-        'A20': 1.3, 'H20': 5.4, 'B21': -0.6, 'P21': 1.2, 'D21': 0.6, 'N21': -12.4, 'E21': -14.3, 'S21': -8.9, 'A21': -47.2, 'H21': -0.4,
-        'W20': -2.2, 'C': 2.7}
-QG = {'A01': 'V', 'D11': 'V'}
+COST = {"CYC": 0.00083, "TCYC": 0.00042, "LAT": 0.12, "GF": 1.56, "SCF": 3.8, "HOP": 3.5}
+BIAS = {}
+VG = {"A0"}
+CQ, CLO, CHI, CSC, CBI, CNH, CW, C15, CSH = range(9)
 
 
-def build_ops():
+def build_ops(cost):
     ops, tiles, cls = [], [], ["C"]
+    CYC, TCYC, GF = cost["CYC"], cost["TCYC"], cost["GF"]
 
-    def tile(pool, chain):
-        tiles.append({"pool": pool, "chain": chain, "users": 0, "buf": None})
+    def tile():
+        tiles.append({"users": 0, "buf": None})
         return ("tile", len(tiles) - 1)
 
     def op(qs, fn, reads, writes, dur, name="", sem=None):
@@ -67,411 +59,339 @@ def build_ops():
         return (buf, lo, SCRATCH[buf][1][1] if hi is None else hi)
 
     def v(fn, reads, writes, cyc, name=""):
-        op("V", fn, reads, writes, 0.055 + CYC * cyc, name)
+        op("V", fn, reads, writes, 0.055 + CYC * max(cyc, 64), name)
 
     def s(fn, reads, writes, cyc, name=""):
-        op("S", fn, reads, writes, 0.065 + CYC * cyc, name)
+        op("S", fn, reads, writes, 0.065 + CYC * max(cyc, 64), name)
 
     def gp(fn, reads, writes, n, name=""):
         op("G", fn, reads, writes, 0.17 + 2 * CYC * n, name)
 
-    def mm(cols, fn, reads, writes, name=""):
-        op("T", fn, reads, writes, cols * TCYC + 0.03, name)
+    def mm(out, terms, reads, name, first=True, last=True):
+        def fn(e, B, inc):
+            for i, x in enumerate(terms):
+                a, z = (x[6], x[7]) if len(x) > 6 else (first and i == 0, last and i == len(terms) - 1)
+                inc(e.matmul(B(out)[:, x[0]], B(x[1])[x[2]], B(x[3])[x[4]], a, z))
+        op("T", fn, reads, [R(out)], sum(x[5] for x in terms) * TCYC + 0.03, name)
 
-    def ts(dst, src, s1, o1, s2=None, o2=None, lo=0, hi=1, cyc=64, slo=None, name="ts", extra=()):
+    def c(lo, hi, st=1, p=128):
+        return (slice(0, p), slice(lo, hi, st))
+
+    def ts(dst, src, s1, o1, s2=None, o2=None, lo=0, hi=1, cyc=64, slo=None, name="ts", dview=None):
         a, b = (lo, hi) if slo is None else (slo, slo + hi - lo)
+        w = slice(lo, hi) if dview is None else dview
         val = lambda B, x: B(x[0])[:, x[1]:x[1] + 1] if isinstance(x, tuple) else x
 
         def fn(e, B, inc):
             if o2 is None:
-                inc(e.tensor_scalar(out=B(dst)[:, lo:hi], in0=B(src)[:, a:b], scalar1=val(B, s1), scalar2=None, op0=o1))
+                inc(e.tensor_scalar(out=B(dst)[:, w], in0=B(src)[:, a:b], scalar1=val(B, s1), scalar2=None, op0=o1))
             else:
-                inc(e.tensor_scalar(out=B(dst)[:, lo:hi], in0=B(src)[:, a:b], scalar1=val(B, s1), scalar2=val(B, s2), op0=o1, op1=o2))
+                inc(e.tensor_scalar(out=B(dst)[:, w], in0=B(src)[:, a:b], scalar1=val(B, s1), scalar2=val(B, s2), op0=o1, op1=o2))
         cols = [R(x[0], x[1], x[1] + 1) for x in (s1, s2) if isinstance(x, tuple)]
-        v(fn, [R(src, a, b)] + cols, [R(dst, lo, hi)], cyc, name)
+        v(fn, [R(src, a, b)] + cols, [R(dst, w.start, w.stop)], cyc, name)
 
-    def tt(dst, in0, in1, o, lo, hi, cyc=None, slo=None, name="tt"):
+    def tt(dst, in0, in1, o, lo, hi, cyc=None, slo=None, name="tt", lo1=None):
         a, b = (lo, hi) if slo is None else (slo, slo + hi - lo)
-        v(lambda e, B, inc: inc(e.tensor_tensor(out=B(dst)[:, lo:hi], in0=B(in0)[:, a:b], in1=B(in1)[:, lo:hi], op=o)),
-          [R(in0, a, b), R(in1, lo, hi)], [R(dst, lo, hi)], (hi - lo) if cyc is None else cyc, name)
+        a1, b1 = (lo, hi) if lo1 is None else (lo1, lo1 + hi - lo)
+        v(lambda e, B, inc: inc(e.tensor_tensor(out=B(dst)[:, lo:hi], in0=B(in0)[:, a:b], in1=B(in1)[:, a1:b1], op=o)),
+          [R(in0, a, b), R(in1, a1, b1)], [R(dst, lo, hi)], (hi - lo) if cyc is None else cyc, name)
 
     def cp(dst, src, lo, hi, cyc, slo=None, name="cp"):
         a, b = (lo, hi) if slo is None else (slo, slo + hi - lo)
         v(lambda e, B, inc: inc(e.tensor_copy(out=B(dst)[:, lo:hi], in_=B(src)[:, a:b])), [R(src, a, b)], [R(dst, lo, hi)], cyc, name)
 
+    def scan(dst, dv, a, av, b, bv, init, o0, o1, cyc, name):
+        rng = lambda x, w: R(x, w.start, w.stop)
+        v(lambda e, B, inc: inc(e.tensor_tensor_scan(B(dst)[:, dv], B(a)[:, av], B(b)[:, bv], init, o0, o1)),
+          [rng(a, av), rng(b, bv)], [rng(dst, dv)], cyc, name)
+
     op("A", lambda e, B, inc: inc(e.dma_start(B("r0i")[:, :], B("IN")["r0"][:, :])), [], [R("r0i")], 2.5, "load r0", sem="lr")
     op("Y", lambda e, B, inc: inc(e.dma_start(B("xs")[:, :], B("IN")["x"][:, :])), [], [R("xs")], 5.0, "load x", sem="lx")
-    op("Y", lambda e, B, inc: inc(e.dma_start(B("c0i")[:, :], B("IN")["c0"][:, :])), [], [R("c0i")], 4.0, "load c0", sem="lc")
+    op("Y", lambda e, B, inc: inc(e.dma_start(B("c0i")[:, :], B("IN")["c0"][:, :])), [], [R("c0i")], 7.0, "load c0", sem="lc")
 
-    def fill(buf, val, n, lo=0):
-        v(lambda e, B, inc: inc(e.memset(B(buf)[:, lo:lo + n], val)), [], [R(buf, lo, lo + n)], n / 2)
+    def fill(buf, val, lo=0, hi=None, st=1):
+        hi = SCRATCH[buf][1][1] if hi is None else hi
+        v(lambda e, B, inc: inc(e.memset(B(buf)[:, lo:hi:st], val)), [], [R(buf, lo, hi)], (hi - lo) / st / 2, "fill")
 
-    def gsel(dst, src, pat, cmp, fillv, base, cm, n, view=None):
+    def sel(dst, src, pat, cmp, fillv, base, cm, view=None, sview=None):
+        n = 1
+        for x in pat:
+            n *= x[1]
         w = slice(0, n) if view is None else view
-        gp(lambda e, B, inc: inc(e.affine_select(out=B(dst)[:, w], in_=B(src)[:, w], pattern=pat, compare_op=cmp, fill=fillv, base=base, channel_multiplier=cm)),
+        u = w if sview is None else sview
+        gp(lambda e, B, inc: inc(e.affine_select(out=B(dst)[:, w], in_=B(src)[:, u], pattern=pat, compare_op=cmp, fill=fillv, base=base, channel_multiplier=cm)),
            [R(src)], [R(dst)], n, "sel " + dst)
 
-    def scale(dst, src, k):
-        n = SCRATCH[src][1][1]
-        ts(dst, src, float(k), A.mult, hi=n, cyc=n / 2)
+    def iota(dst, lo, hi, pat, base, cm, flt=False):
+        if flt:
+            gp(lambda e, B, inc: inc(e.iota(B(dst)[:, lo:hi], pat, base, cm, allow_small_or_imprecise_dtypes=True)), [], [R(dst, lo, hi)], hi - lo, "iota")
+        else:
+            gp(lambda e, B, inc: inc(e.iota(B(dst)[:, lo:hi], pat, base, cm)), [], [R(dst, lo, hi)], hi - lo, "iota")
 
-    fill("ones", 1.0, 2048)
-    gsel("ey", "ones", [[-1, 128]], A.is_equal, 0.0, 0, 1, 128)
-    gsel("b8a", "ones", [[-16, 8]], A.is_ge, 0.0, 0, 1, 8)
-    gsel("b8", "b8a", [[16, 8]], A.is_ge, 0.0, 15, -1, 8)
-    gsel("b15", "ones", [[-16, 8]], A.is_equal, 0.0, -15, 1, 8)
-    scale("ney", "ey", -1)
-    fill("mst", 0.0, 144)
-    fill("mst15", 0.0, 144)
-    for d_, s_ in (("mst", "b8"), ("mst15", "b15")):
-        v(lambda e, B, inc, d_=d_, s_=s_: inc(e.tensor_copy(out=B(d_)[:, 15:143:16], in_=B(s_)[:, 0:8])), [R(s_)], [R(d_)], 64)
-    scale("mstn", "mst", -1)
-    gsel("bo1", "ones", [[-16, 8], [0, 16]], A.is_ge, 0.0, 0, 1, 128)
-    gsel("bo", "bo1", [[16, 8], [0, 16]], A.is_ge, 0.0, 15, -1, 128)
-    gsel("ux", "bo", [[1, 128]], A.is_gt, 0.0, 0, -1, 128)
-    fill("smask", 1.0, CH)
-    v(lambda e, B, inc: inc(e.memset(B("smask")[:, 15:CH:16], 0.0)), [], [R("smask")], 64)
-    for c in range(NC):
-        fill("ka", 0.0, 16, c * KW)
-        fill("kb", 0.0, 16, c * KW)
-    gsel("u15", "ux", [[0, 8], [-1, 16]], A.is_gt, 0.0, 15, 0, 128)
-    scale("u15s", "u15", -SH)
-    scale("u15n", "u15", -1)
-    gp(lambda e, B, inc: inc(e.iota(B("ki")[:, 0:1], [[0, 1]], 0, 1)), [], [R("ki")], 8)
-    gp(lambda e, B, inc: inc(e.iota(B("rio")[:, 0:16], [[1, 16]], 0, 0, allow_small_or_imprecise_dtypes=True)), [], [R("rio")], 16)
-    gp(lambda e, B, inc: inc(e.iota(B("dj")[:, 0:32], [[16, 32]], H, 0, allow_small_or_imprecise_dtypes=True)), [], [R("dj")], 32)
+    NE, GE = A.not_equal, A.is_ge
+    fill("zero", 0.0)
+    fill("ones", 1.0)
+    for a, z, val in (("b2a", "b2", 2.0), ("bma", "bm", -1.0)):
+        sel(a, "zero", [[0, 2], [16, 8]], A.is_gt, val, 0, -1)
+        sel(z, a, [[0, 2], [16, 8]], GE, 0.0, 15, -1)
+    fill("ca", -5.0)
+    sel("cap", "ones", [[0, CH // 16], [1, 16]], NE, 0.0, -15, 0)
+    sel("ey", "zero", [[-1, 128]], NE, 1.0, 0, 1)
+    sel("ney", "zero", [[-1, 128]], NE, -1.0, 0, 1)
+    fill("ka", 0.0)
+    fill("ms", 0.0)
+    w8 = slice(0, 8)
+    sel("b2a", "ones", [[-16, 8]], GE, 0.0, 0, 1)
+    sel("ms", "b2a", [[16, 8]], GE, 0.0, 14, -1, slice(15, 143, 16), w8)
+    sel("ms", "zero", [[-16, 8]], NE, 1.0, -15, 1, slice(159, 287, 16), w8)
+    sel("ms", "zero", [[-16, 8]], NE, 0.125, -15, 1, slice(303, 431, 16), w8)
+    fill("c192", SH / 8.0)
+    iota("ki", 0, 1, [[0, 1]], 0, 1)
+    iota("ia", 0, 128, [[0, 8], [1, 16]], 128, -1)
+    iota("ia", 128, 256, [[1, 8], [1, 16]], 129, -1)
+    iota("rio", 0, 16, [[1, 16]], 0, 0, True)
+    sel("ni15", "ney", [[0, 8], [1, 16]], NE, 0.0, -15, 0)
     ts("kp", "ki", 15, A.bitwise_and)
-    ts("mb", "kp", 16.0, A.mult, -17.0, A.add)
-    ts("kd", "ki", 4, A.arith_shift_right)
-    tt("ks", "kp", "kd", A.add, 0, 1, 64)
-    ts("kw", "ks", 1.0, A.add)
-    v(lambda e, B, inc: inc(e.tensor_scalar(out=B("ks")[:, 2:3], in0=B("kw")[:, 0:1], scalar1=15, scalar2=None, op0=A.bitwise_and)), [R("kw")], [R("ks")], 64)
-    v(lambda e, B, inc: inc(e.tensor_tensor(out=B("kf")[:, 0:1], in0=B("kp")[:, 0:1], in1=B("ks")[:, 2:3], op=A.min)), [R("kp"), R("ks")], [R("kf", 0, 1)], 64)
-    cp("kf", "kp", 1, 2, 64, slo=0)
-    ts("dj", "dj", ("kf", 1), A.add, hi=32)
-    fill("vm", 0.0, 240)
-    ts("vt", "rio", ("kf", 0), A.is_gt, -100.0, A.mult, hi=16)
-    ts("ve", "rio", ("kf", 0), A.is_equal, hi=16)
-    v(lambda e, B, inc: inc(e.tensor_tensor(out=B("vm")[:, 112:128], in0=B("vt")[:, 0:16], in1=B("ve")[:, 0:16], op=A.add)), [R("vt"), R("ve")], [R("vm")], 64)
-    fill("pa", 0.0, 1024)
-    gsel("pb", "pa", [[-16, 8], [0, 8], [-1, 16]], A.not_equal, 1.0, 0, 1, 1024)
-    gsel("pa", "pb", [[-16, 8], [-1, 8], [-1, 16]], A.not_equal, -1.0, -1, 1, 1024)
-    gsel("pb", "pa", [[-16, 8], [-1, 8], [-1, 16]], A.not_equal, -1.0, 15, 1, 1024)
-    gsel("pa", "pb", [[-16, 8], [0, 128]], A.is_ge, 0.0, 0, 1, 1024)
-    gsel("pb", "pa", [[16, 8], [0, 128]], A.is_ge, 0.0, 15, -1, 1024)
-    scale("boq", "bo", 0.25)
-    scale("hey", "ey", 0.5)
-    tt("boqp", "boq", "hey", A.add, 0, 128, 256)
-    tt("boqm", "boq", "hey", A.subtract, 0, 128, 256)
-    gsel("tl", "bo", [[-1, 128]], A.is_ge, 0.0, 0, 1, 128)
-    scale("tl2", "tl", 2)
-    gsel("au", "bo", [[1, 128]], A.is_ge, 0.0, 0, -1, 128)
-    scale("au16", "au", 16)
-    gsel("hq", "ones", [[-1, 16], [-16, 8], [0, 16]], A.is_equal, 0.0, 0, 1, 2048)
-    gsel("mqa", "ones", [[0, 16], [-16, 8]], A.is_ge, 0.0, 0, 1, 128)
-    gsel("mq", "mqa", [[1, 16], [16, 8]], A.is_ge, 0.0, -1, -1, 128)
-    gsel("mst8", "ones", [[-1, 144]], A.is_equal, 0.0, 15, 16, 144)
-    fill("qm", 0.0, 128)
-    gsel("qm", "qm", [[-2, 64]], A.not_equal, 0.5, 0, 1, 64, slice(1, 128, 2))
-    gsel("qm", "qm", [[-2, 64]], A.not_equal, -0.5, -1, 1, 64, slice(1, 128, 2))
-    v(lambda e, B, inc: inc(e.memset(B("qm")[:, 15:128:16], 0.0)), [], [R("qm")], 64)
-    tt("qp", "qm", "ey", A.add, 0, 128, 256)
-    fill("c1536", float(SH), CH)
-    fill("onesf", 1.0, 128)
-    fill("zero", 0.0, 8)
-    fill("cache", 0.0, P, H)
-    cp("cache", "c0i", 0, H, H)
-    for i, val in ((2, -40.5), (3, 40.5), (4, -0.5)):
-        v(lambda e, B, inc, i=i, val=val: inc(e.memset(B("kf")[:, i:i + 1], val)), [], [R("kf", i, i + 1)], 64)
+    cp("col", "kp", CQ, CQ + 1, 64, slo=0)
+    ts("col", "kp", 15.0, A.is_equal, lo=C15, hi=C15 + 1, slo=0)
+    ts("col", "col", 10240.0, A.mult, 6144.0, A.add, lo=CSC, hi=CSC + 1, slo=C15)
+    ts("col", "col", -16896.0, A.mult, -7680.0, A.add, lo=CBI, hi=CBI + 1, slo=C15)
+    fill("c15", -960.0)
+    fill("c15", 0.0, 15, 128, 16)
+    fill("cache", 0.0, 0, D0)
+    cp("cache", "c0i", D0, D0 + H, H, slo=0)
+    ts("ib", "ia", 15, A.bitwise_and, hi=256, cyc=256)
+    ts("pq", "ib", 0.0, A.is_equal, hi=256, cyc=256)
+    tt("pd", "pq", "pq", A.subtract, 0, 128, 256, lo1=128)
+    for g in range(8):
+        ts("pb", "pd", ("bm", g), A.mult, lo=128 * g, hi=128 * g + 128, slo=0)
+    sel("dl", "ey", [[-1, 128]], NE, -1.0, 1, 1)
+    sel("dl", "ones", [[-16, 8]], A.is_equal, 0.0, 0, 1, slice(0, 128, 16), w8)
+    ts("ks", "ki", 4, A.arith_shift_right)
+    tt("kt", "ks", "kp", A.add, 0, 1, 64)
+    ts("ks", "kt", 1.0, A.add)
+    ts("kt", "ks", 15, A.bitwise_and)
+    tt("col", "kp", "kt", A.min, CLO, CLO + 1, 64, slo=0, lo1=0)
+    tt("col", "kp", "kt", A.max, CHI, CHI + 1, 64, slo=0, lo1=0)
+    fill("vw", 0.0)
+    ts("fa", "rio", ("col", CLO), A.is_gt, 2.0 ** -8, A.max, hi=16)
+    v(lambda e, B, inc: inc(e.tensor_reduce(B("col")[:, CW:CW + 1], B("fa")[:, 0:16], AX.X, A.mult)), [R("fa")], [R("col", CW, CW + 1)], 64, "red")
+    ts("fb", "rio", ("col", CLO), A.is_gt, 17.0 * 2.0 ** 60, A.mult, hi=16)
+    ts("fc", "rio", ("col", CHI), A.is_le, hi=16)
+    tt("fa", "fb", "fc", A.mult, 0, 16, 64)
+    ts("vw", "fa", -2.0 ** 60, A.add, ("col", CW), A.mult, lo=112, hi=128, slo=0)
+    ts("vw", "rio", ("col", CHI), A.is_equal, -4096.0, A.mult, lo=352, hi=368, slo=0)
+    fill("ci", -37.0, 0, 128)
+    fill("ci", -5.0, 128, 256, 2)
+    fill("ci", 27.0, 129, 256, 2)
+    sel("nw", "zero", [[-1, 128]], NE, 256.0, -1, 1)
+    sel("nw", "zero", [[-2, 64]], NE, 256.0, -2, 1, slice(128, 256, 2), slice(0, 64))
+    sel("nw", "zero", [[-2, 64]], NE, -256.0, -2, 1, slice(129, 256, 2), slice(0, 64))
+    fill("kb", 0.0)
+    fill("sn", 0.0)
+    fill("col", -0.5, CNH, CNH + 1)
+    fill("col", float(SH), CSH, CSH + 1)
+    iota("onesf", 0, 128, [[0, 128]], 1, 0, True)
+    iota("zerof", 0, 128, [[0, 128]], 0, 0, True)
+    sel("tra", "onesf", [[1, 128]], GE, 0.0, 0, -1)
+    sel("tri", "tra", [[-16, 8], [0, 16]], GE, 0.0, 0, 1)
+    odd = [[-2, 64], [-1001, 2]]
+    sel("tro", "tri", odd, NE, 0.0, 1000, 1)
+    sel("tro", "tri", [[0, 8]], GE, 0.0, 0, 0, slice(15, 128, 16))
+    sel("trb", "zerof", odd, NE, 0.5, 1000, 1)
+    sel("ioh", "trb", [[0, 8], [1, 16]], NE, 0.0, -15, 0)
+    sel("t15", "tri", [[0, 8], [1, 16]], NE, 0.0, -15, 0)
+    ts("kw", "onesf", ("col", C15), A.mult, 1.0 / 256, A.mult, hi=128, cyc=128)
 
-    def E(B, q, m="mst"):
-        return B(m)[:, 15 - q:143 - q]
+    al = c(0, 128)
 
-    def dist(vb, c, pairs, chain, flip):
-        ds = tile("B", chain)
-        for x in range(CH // W0):
-            for i0 in range(0, len(pairs), RT):
-                part = pairs[i0:i0 + RT]
-                lo, hi = 16 * (c * CH + x * W0), 16 * (c * CH + (x + 1) * W0)
-                d = tile("D", chain + "d")
-                ad = tile("AD", chain + "a")
-
-                def diff(e, B, inc, part=part, d=d, lo=lo, hi=hi):
-                    for i, (p, p2, row) in enumerate(part):
-                        o = B(d)[:, i * W0:(i + 1) * W0]
-                        inc(e.matmul(o, B("ey")[:, :], B(vb)[:, lo + p:hi:16], True, False))
-                        inc(e.matmul(o, B("ney")[:, :], B(vb)[:, lo + p2:hi:16], False, True))
-                mm(2 * W0 * len(part), diff, [R(vb, lo, hi), R("ey"), R("ney")], [R(d)], "diff")
-                w = W0 * len(part)
-                s(lambda e, B, inc, d=d, ad=ad, w=w: inc(e.activation(B(ad)[:, 0:w], B(d)[:, 0:w], F.Abs)), [R(d)], [R(ad)], w, "abs")
-
-                def summ(e, B, inc, part=part, ad=ad, i0=i0, x=x):
-                    for i, (p, p2, row) in enumerate(part):
-                        inc(e.matmul(B(ds)[:, x * W0:(x + 1) * W0], E(B, row), B(ad)[:, i * W0:(i + 1) * W0], i0 + i == 0, i0 + i == len(pairs) - 1))
-
-                def sumf(e, B, inc, part=part, ad=ad, x=x):
-                    b0 = x * W0
-                    for i, (p, p2, row) in enumerate(part):
-                        inc(e.matmul(B(ds)[:, b0 + row:b0 + 128:16], B(ad)[:, i * W0:i * W0 + 128], B("b8")[:, 0:8], True, True))
-                    if part[-1] == pairs[-1]:
-                        inc(e.matmul(B(ds)[:, b0 + 15:b0 + 128:16], B(ad)[:, 0:128], B("zero")[:, 0:8], True, True))
-                if flip:
-                    mm(W0 // 2 * len(part), sumf, [R(ad), R("b8"), R("zero")], [R(ds)], "sum")
-                else:
-                    mm(W0 * len(part), summ, [R(ad), R("mst")], [R(ds)], "sum")
-        return ds
-
-    def gather(vb, off, c):
-        for j in range(c * CH, (c + 1) * CH, KG):
+    def gather(vb, off, j0, j1):
+        for j in range(j0, j1, KG):
             def fn(e, B, inc, j=j):
                 o, w = B(vb)[:, 16 * j:16 * (j + KG)], B("xs")[:, 0:W].indirect(B(off)[:, j:j + KG])
                 if B("Q") == "V":
                     inc(e.tensor_copy(out=o, in_=w))
                 else:
                     inc(e.activation(o, w, F.Copy))
-            op(QG.get(cls[0], "VS"), fn, [R("xs"), R(off, j, j + KG)], [R(vb, 16 * j, 16 * (j + KG))], 0.06 + GF * CYC * 16 * KG, "gather")
+            op("SV" if cls[0] in VG else "S", fn, [R("xs"), R(off, j, j + KG)], [R(vb, 16 * j, 16 * (j + KG))], 0.065 + GF * CYC * 16 * KG, "gather")
 
-    def first_fail(ds, c, sbuf, kbuf, ibuf, chain, kacc=None):
-        j0, j1, i0 = c * CH, (c + 1) * CH, 16 + c * KW
-        s(lambda e, B, inc: inc(e.activation(B(sbuf)[:, j0:j1], B(ds)[:, 0:CH], F.Sign, bias=B("kf")[:, 2:3])), [R(ds), R("kf")], [R(sbuf, j0, j1)], CH, "bad")
-        v(lambda e, B, inc: inc(e.tensor_tensor_scan(B(kbuf)[:, i0:i0 + CH], B("smask")[:, 0:CH], B(sbuf)[:, j0:j1], 0.0, A.mult, A.max)),
-          [R("smask"), R(sbuf, j0, j1)], [R(kbuf, i0, i0 + CH)], CH / 2, "scan")
-        qt = tile("B", chain)
+    def maxima(dst, vb, j0, j1, d):
+        for j in range(j0, j1, SC):
+            lo, hi = 16 * j, 16 * (j + SC)
+            scan(dst, slice(lo // d, hi // d - 1), vb, slice(lo, hi - d, d), vb, slice(lo + d, hi, d), 16.0, A.min, A.max, 8 * SC / d, "max%d" % d)
 
-        def fq(e, B, inc):
-            for x in range(0, CH, 128):
-                inc(e.matmul(B(qt)[:, x:x + 128], B(kbuf)[:, i0 + x:i0 + x + 128], B("ey")[:, :], True, False))
-                inc(e.matmul(B(qt)[:, x:x + 128], B(kbuf)[:, i0 + x - 1:i0 + x + 127], B("ney")[:, :], False, True))
-        mm(2 * CH, fq, [R("ey"), R("ney"), R(kbuf, i0 - 1, i0 + CH)], [R(qt)], "q")
-        if kacc is None:
-            def fn(e, B, inc):
-                if B("Q") == "S":
-                    inc(e.activation(B(ibuf)[:, j0:j1], B(qt)[:, 0:CH], F.Relu))
-                else:
-                    inc(e.tensor_scalar(out=B(ibuf)[:, j0:j1], in0=B(qt)[:, 0:CH], scalar1=0.0, scalar2=None, op0=A.max))
-            op("SV", fn, [R(qt)], [R(ibuf, j0, j1)], 0.06 + CYC * CH, "ind")
-        else:
-            op("S", lambda e, B, inc: inc(e.activation(B(ibuf)[:, j0:j1], B(qt)[:, 0:CH], F.Relu, accum_out=B("kacc")[:, kacc:kacc + 1])),
-               [R(qt)], [R(ibuf, j0, j1), R("kacc", kacc, kacc + 1)], 0.2 + CYC * CH, "ind")
+    def rows(buf, j, p, k=16):
+        return c(k * j + p, k * (j + BL), k)
 
-    def phase_a(t, c):
-        j0, j1, rf, ch = c * CH, (c + 1) * CH, "rf%d" % t, "A%d_%d" % (t, c)
-        if t == 0:
-            cp("ru", "r0i", j0, j1, CH)
-            ts(rf, "r0i", float(-SH), A.add, lo=j0, hi=j1, cyc=CH)
-        else:
-            ts("ru", rf, float(SH), A.add, lo=j0, hi=j1, cyc=CH / 2)
-        gather("va", "ru", c)
-        l15 = tile("B", ch + "r")
+    def lists(out, o0, n, m0, src, j0, j1):
+        return [(slice(o0, o0 + n), "ms", c(m0 + 15 - q, m0 + 143 - q), src, c(j0 + q, j1, 16), 64) for q in range(16)]
 
-        def f15(e, B, inc):
-            for q in range(16):
-                inc(e.matmul(B(l15)[:, 0:NL], E(B, q, "mst15"), B(rf)[:, j0 + q:j1:16], q == 0, q == 15))
-        mm(16 * 64, f15, [R("mst15"), R(rf, j0, j1)], [R(l15)], "r15")
-        ts("r15", l15, float(SH), A.add, lo=c * NL, hi=(c + 1) * NL, slo=0, name="r15")
-        ds = dist("va", c, [(p, p + 1, p) for p in range(15)], ch, True)
-        first_fail(ds, c, "sb", "ka", "ind", ch, t * NC + c if t < RO - 1 else None)
+    def phase_a(t, ch):
+        j0, j1, ru, i0 = ch * CH, (ch + 1) * CH, "ru%d" % t, 16 + ch * KA
+        ds = tile()
+        first = True
+        for j in range(j1 - BL, j0 - 1, -BL):
+            if t == 0:
+                cp(ru, "r0i", j, j + BL, BL, name="ru")
+            ts("rf", ru, float(-SH), A.add, lo=j, hi=j + BL, cyc=BL / 2, name="rf")
+            gather("va", ru, j, j + BL)
+            maxima("mx", "va", j, j + BL, 1)
+            o = lambda p: slice(j - j0 + p, j - j0 + BL, 16)
+            va = [(o(p), "va", rows("va", j, p + e), "bm", c(0, 8), 64) for p in range(15) for e in (0, 1)]
+            init = [(slice(0, CH), "ones", c(0, 128, 1, 8), "ca", c(0, CH, 1, 8), CH)] if first else []
+            rd = [R("va", 16 * j, 16 * (j + BL)), R("bm"), R("ones"), R("ca")]
+            mm(ds, init + va[:15], rd, "sum a", first, False)
+            mm(ds, va[15:], rd, "sum a", False, False)
+            mm(ds, [(o(p), "mx", rows("mx", j, p), "b2", c(0, 8), 64) for p in range(15)], [R("mx", 16 * j, 16 * (j + BL)), R("b2")], "sum m", False, j == j0)
+            first = False
+        scan("ka", slice(i0, i0 + CH), ds, slice(0, CH), "cap", slice(0, CH), 0.0, A.max, A.min, CH, "ka")
+        cls[0] = "R%d" % t
+        l15 = tile()
+        mm(l15, lists(l15, 0, NL, 144, "rf", j0, j1), [R("ms"), R("rf", j0, j1)], "r15")
+        ts("r15", l15, float(SH + 64), A.add, lo=ch * NL, hi=(ch + 1) * NL, slo=0, name="r15")
 
-    def phase_b(t, c):
-        j0, j1, k0, k1 = c * CH, (c + 1) * CH, c * NL, (c + 1) * NL
-        rf, ch = "rf%d" % t, "B%d_%d" % (t, c)
-        wm = tile("B", ch)
+    def turn(o0, n, buf, i0, m, start=True, stop=True):
+        return [(slice(o0 + x, o0 + x + 128), buf, c(i0 + x, i0 + x + 128), m, al, 128, start, stop) for x in range(0, n, 128)]
 
-        def fwm(e, B, inc):
-            inc(e.matmul(B(wm)[:, 0:CH], B("ey")[:, :], B(rf)[:, j0:j1], True, False))
-            inc(e.matmul(B(wm)[:, 0:CH], B("u15s")[:, :], B("ind")[:, j0:j1], False, True))
-            inc(e.matmul(B(wm)[:, CH:2 * CH], B("u15")[:, :], B("ind")[:, j0:j1], True, True))
-        mm(3 * CH, fwm, [R("ey"), R("u15"), R("u15s"), R(rf, j0, j1), R("ind", j0, j1)]
-           + ([R("kcol", t, t + 1)] if t else []) + ([R("cache")] if t and c else []), [R(wm)], "wm")
-        tt("indr", wm, "ind", A.mult, j0, j1, slo=0, name="indr")
-        ll = tile("B", ch)
+    def phase_b(t, ch):
+        j0, j1, k0, k1, i0 = ch * CH, (ch + 1) * CH, ch * NL, (ch + 1) * NL, 16 + ch * KA
+        kr = [R("ka", i0 - 1, i0 + CH), R("ey"), R("ney")]
+        qt = tile()
+        a, b = turn(0, CH, "ka", i0, "ey", True, False), turn(0, CH, "ka", i0 - 1, "ney", False, True)
+        mm(qt, [x for ab in zip(a, b) for x in ab], kr + [R("rf", j0, j1)], "ind")
+        tt("indr", qt, "rf", A.mult, j0, j1, slo=0, name="indr")
+        qa = tile()
+        mm(qa, turn(0, CH, "ka", i0 - 1, "ey"), kr, "a")
+        kc = t * NC + ch
 
-        def ffl(e, B, inc):
-            for q in range(16):
-                inc(e.matmul(B(ll)[:, NL:2 * NL], E(B, q, "mstn"), B("ind")[:, j0 + q:j1:16], q == 0, False))
-            inc(e.matmul(B(ll)[:, NL:2 * NL], B("ey")[:, :], B("ones")[:, 0:NL], False, True))
-        mm(17 * 64, ffl, [R("mstn"), R("ey"), R("ones"), R("ind", j0, j1)], [R(ll)], "fail list")
-
-        def frk(e, B, inc):
-            for q in range(16):
-                inc(e.matmul(B(ll)[:, 0:NL], E(B, q), B("indr")[:, j0 + q:j1:16], q == 0, False))
-            inc(e.matmul(B(ll)[:, 0:NL], B("ey")[:, :], B("c1536")[:, 0:NL], False, True))
-        mm(17 * 64, frk, [R("mst"), R("ey"), R("c1536"), R("indr", j0, j1)], [R(ll)], "rk list")
-        tt("pri", ll, "r15", A.mult, k0, k1, 64, slo=0, name="l")
+        def fnm(e, B, inc):
+            sc, bi = B("col")[:, CSC:CSC + 1], B("col")[:, CBI:CBI + 1]
+            if t < RO - 1:
+                inc(e.activation(B("nm")[:, j0:j1], B(qa)[:, 0:CH], F.Identity, bias=bi, scale=sc, accum_out=B("kacc")[:, kc:kc + 1]))
+            else:
+                inc(e.activation(B("nm")[:, j0:j1], B(qa)[:, 0:CH], F.Identity, bias=bi, scale=sc))
+        s(fnm, [R(qa), R("col", CSC, CBI + 1)], [R("nm", j0, j1), R("kacc", kc, kc + 1)], CH + 24, "nm")
+        ll = tile()
+        mm(ll, lists(ll, 0, NL, 0, "indr", j0, j1) + [(slice(0, NL), "ones", c(0, 128, 1, 8), "c192", c(0, NL, 1, 8), 64)],
+           [R("ms"), R("ones"), R("c192"), R("indr", j0, j1), R("r15", k0, k1)], "rk")
         if t:
-            ts("rkk", ll, ("kcol", t), A.add, lo=k0, hi=k1, slo=0, name="l")
-        tt("djn", ll, "dj", A.mult, k0, k1, 64, slo=NL, name="l")
-        ts("fi", "pri", 6, A.arith_shift_right, lo=k0, hi=k1, name="l")
-        if t:
-            tt("si", "rkk", "fi", A.add, k0, k1, 64, name="l")
+            tt("pri", ll, "r15", A.mult, k0, k1, slo=0, name="l")
+            ts("pi", "pri", ("kcol", t), A.add, lo=k0, hi=k1, name="l")
         else:
-            tt("si", ll, "fi", A.add, k0, k1, 64, slo=0, name="l")
-        ts("hm", "si", H - 1, A.bitwise_and, lo=k0, hi=k1, name="l")
-        tt("hf", "hm", "djn", A.max, k0, k1, 64, name="l")
-        cp("hu", "hf", k0, k1, 64, name="hu")
-        cls[0] = "P%d%d" % (t, c)
-        v(lambda e, B, inc: inc(e.tensor_tensor(out=B("t1")[:, j0:j1], in0=B("cache")[:, 0:H + P].indirect(B("hu")[:, k0:k1]), in1=B(rf)[:, j0:j1], op=A.subtract)),
-          [R("cache"), R("hu", k0, k1), R(rf, j0, j1)], [R("t1", j0, j1)], GF * CH, "cache gather")
-        tt("t2", wm, "t1", A.mult, j0, j1, slo=CH, name="t2")
-        tt("r2", wm, "t2", A.add, j0, j1, slo=0, name="r2")
-        gpt, b0 = 1024 // CH, c * 2048
+            tt("pi", ll, "r15", A.mult, k0, k1, slo=0, name="l")
+        ts("hm", "pi", 6, A.arith_shift_right, H - 1, A.bitwise_and, lo=k0, hi=k1, name="l")
+        cp("hu", "hm", k0, k1, 64, name="l")
+        wm = tile()
+        mm(wm, [(slice(0, CH), "ey", al, "rf", c(j0, j1), CH), (slice(0, CH), "c15", c(0, 128, 1, 8), "ones", c(0, CH, 1, 8), CH),
+                (slice(0, CH), "ni15", al, "nm", c(j0, j1), CH)],
+           [R("ey"), R("c15"), R("ones"), R("ni15"), R("rf", j0, j1), R("nm", j0, j1), R("hm", k0, k1), R("cache")], "wm")
+        v(lambda e, B, inc: inc(e.tensor_tensor(out=B("t1")[:, j0:j1], in0=B("cache")[:, D0:D0 + H].indirect(B("hu")[:, k0:k1]), in1=B("nm")[:, j0:j1], op=A.add)),
+          [R("cache"), R("hu", k0, k1), R("nm", j0, j1)], [R("t1", j0, j1)], GF * CH, "cache gather")
+        tt("r2", wm, "t1", A.max, j0, j1, slo=0, name="r2")
+        ts("r2u", "r2", float(SH), A.add, lo=j0, hi=j1, cyc=CH / 2, name="r2u")
+        cls[0] = "P%d" % t
+        gpt, b0 = 512 // CH, 8 * j0
         for g0 in range(0, 8, gpt):
-            d = tile("D", ch + "p")
-
-            def fpr(e, B, inc, d=d, g0=g0):
-                for i in range(gpt):
-                    inc(e.matmul(B(d)[:, i * CH:(i + 1) * CH], B("pb")[:, 128 * (g0 + i):128 * (g0 + i + 1)], B("r2")[:, j0:j1], True, True))
-            mm(gpt * CH, fpr, [R("pb"), R("r2", j0, j1)], [R(d)], "pairs")
+            d = tile()
+            mm(d, [(slice(i * CH, (i + 1) * CH), "pb", c(128 * (g0 + i), 128 * (g0 + i + 1)), "r2", c(j0, j1), CH, True, True) for i in range(gpt)],
+               [R("pb"), R("r2", j0, j1)], "pairs")
             ts("eqp", d, 0.0, A.is_equal, lo=b0 + g0 * CH, hi=b0 + (g0 + gpt) * CH, cyc=gpt * CH, slo=0, name="eq")
-        vt = tile("B", ch)
-
-        def fv(e, B, inc):
-            for g in range(8):
-                inc(e.matmul(B(vt)[:, 0:CH], B("vm")[:, 112 - 16 * g:240 - 16 * g], B("eqp")[:, b0 + g * CH:b0 + (g + 1) * CH], g == 0, g == 7))
-        mm(8 * CH, fv, [R("vm"), R("eqp", b0, b0 + 8 * CH)], [R(vt)], "V")
-        s(lambda e, B, inc: inc(e.activation(B("sf")[:, j0:j1], B(vt)[:, 0:CH], F.Sign, bias=B("kf")[:, 4:5])), [R(vt), R("kf")], [R("sf", j0, j1)], CH, "f")
-        rc = tile("B", ch)
-        mm(CH, lambda e, B, inc: inc(e.matmul(B(rc)[:, 0:CH], B("ey")[:, :], B("r2")[:, j0:j1], True, True)), [R("ey"), R("r2", j0, j1)], [R(rc)], "copy r2")
-        tt("fr", rc, "sf", A.mult, j0, j1, slo=0, name="fr")
-        xm = tile("B", ch)
-
-        def fxm(e, B, inc):
-            inc(e.matmul(B(xm)[:, 0:CH], B("boqm")[:, :], B("r2")[:, j0:j1], True, False))
-            inc(e.matmul(B(xm)[:, 0:CH], B("boq")[:, :], B("fr")[:, j0:j1], False, True))
-        mm(2 * CH, fxm, [R("boqm"), R("boq"), R("r2", j0, j1), R("fr", j0, j1)], [R(xm)], "xm")
-        ts("ee", xm, 0.0, A.is_equal, lo=j0, hi=j1, cyc=CH, slo=0, name="E")
-        v2 = tile("B", ch)
-
-        def fv2(e, B, inc):
-            inc(e.matmul(B(v2)[:, 0:CH], B("au16")[:, :], B("sf")[:, j0:j1], True, False))
-            inc(e.matmul(B(v2)[:, 0:CH], B("tl2")[:, :], B("ee")[:, j0:j1], False, True))
-        mm(2 * CH, fv2, [R("au16"), R("tl2"), R("sf", j0, j1), R("ee", j0, j1)], [R(v2)], "v2")
-        s(lambda e, B, inc: inc(e.activation(B("sm")[:, j0:j1], B(v2)[:, 0:CH], F.Sign, bias=B("mb")[:, 0:1])), [R(v2), R("mb")], [R("sm", j0, j1)], CH, "M")
-        tt("t3", xm, "sm", A.mult, j0, j1, slo=0, name="t3")
-        xp = tile("B", ch)
-
-        def fxp(e, B, inc):
-            inc(e.matmul(B(xp)[:, 0:CH], B("boqp")[:, :], B("r2")[:, j0:j1], True, False))
-            inc(e.matmul(B(xp)[:, 0:CH], B("boq")[:, :], B("fr")[:, j0:j1], False, True))
-        mm(2 * CH, fxp, [R("boqp"), R("boq"), R("r2", j0, j1), R("fr", j0, j1), R("sm", j0, j1)], [R(xp)], "xp")
-        tt("rp", xp, "t3", A.add, j0, j1, slo=0, name="rp")
-        ts("rpu", "rp", float(SH), A.add, lo=j0, hi=j1, cyc=CH / 2, name="rpu")
-
-    def hrep(t, c):
-        j0, j1, k0, k1 = c * CH, (c + 1) * CH, c * NL, (c + 1) * NL
-        cp("hh", "hf", k0, k1, 64, name="hh")
-        hr = tile("B", "H%d_%d" % (t, c))
-
-        def fh(e, B, inc):
-            for q in range(16):
-                inc(e.matmul(B(hr)[:, q:CH:16], B("hq")[:, 128 * q:128 * (q + 1)], B("hh")[:, k0:k1], True, True))
-        mm(16 * 64, fh, [R("hq"), R("hh", k0, k1)], [R(hr)], "hrep")
-        cp("hrep", hr, j0, j1, CH, slo=0, name="hrep")
+        vt = tile()
+        for g0 in (0, 4):
+            mm(vt, [(slice(0, CH), "vw", c(112 - 16 * g, 240 - 16 * g), "eqp", c(b0 + g * CH, b0 + (g + 1) * CH), CH) for g in range(g0, g0 + 4)],
+               [R("vw"), R("eqp", b0 + g0 * CH, b0 + (g0 + 4) * CH)] + ([] if g0 else [R("eqp", b0 + 4 * CH, b0 + 6 * CH)]), "loop", g0 == 0, g0 == 4)
+        ts("nq", vt, 0.0, A.is_le, lo=j0, hi=j1, cyc=CH, slo=0, name="nq")
+        dt_ = tile()
+        mm(dt_, [(slice(0, CH), "dl", al, "r2", c(j0, j1), CH)], [R("dl"), R("r2", j0, j1), R("eqp", b0, b0 + 8 * CH)], "delta")
+        tt("yp", dt_, "nq", A.mult, j0, j1, slo=0, name="yp")
 
     def winners(t):
         if t < RO - 1:
-            kt = tile("B", "K%d" % t)
+            kt = tile()
+            mm(kt, [(slice(0, 1), "kw", al, "kacc", c(t * NC + x, t * NC + x + 1), 256) for x in range(NC)], [R("kw"), R("kacc", t * NC, t * NC + NC)], "K")
+            ts("kcol", kt, 96.0 * 8 * P, A.add, lo=t + 1, hi=t + 2, slo=0, name="K")
+        lf = tile()
+        mm(lf, lists(lf, 0, 32, 288, "nm", 0, P), [R("ms"), R("nm"), R("hm")], "fail")
+        tt("hh", lf, "hm", A.add, 0, 32, name="w")
+        pt = tile()
+        mm(pt, [(slice(32 * g, 32 * g + 32), "pb", c(128 * g, 128 * g + 128), "hh", c(0, 32), 64, True, True) for g in range(8)], [R("pb"), R("hh")], "h pairs")
+        ts("eqh", pt, 0.0, A.is_equal, hi=256, cyc=256, name="w")
+        z = tile()
+        mm(z, [(slice(0, 32), "vw", c(352 - 16 * g, 480 - 16 * g), "eqh", c(32 * g, 32 * g + 32), 64) for g in range(8)]
+           + [(slice(0, 32), "ey", al, "hh", c(0, 32), 64)], [R("vw"), R("eqh"), R("ey"), R("hh")], "lose")
+        ts("wu", z, float(H + D0), A.add, ("col", CQ), A.max, hi=32, name="w", dview=slice(0, 64, 2))
 
-            def fk(e, B, inc):
-                for c in range(NC):
-                    inc(e.matmul(B(kt)[:, 0:1], B("onesf")[:, :], B("kacc")[:, t * NC + c:t * NC + c + 1], c == 0, c == NC - 1))
-            mm(256 * NC, fk, [R("onesf"), R("kacc", t * NC, t * NC + NC)], [R(kt)], "K")
-            cp("kcol", kt, t + 1, t + 2, 64, slo=0, name="K")
-        for k in range(32):
-            n = P - 16 * k
-            v(lambda e, B, inc, k=k, n=n: inc(e.tensor_scalar(out=B("eqw")[:, P * k:P * k + n], in0=B("hrep")[:, 16 * k:P], scalar1=B("hf")[:, k:k + 1], scalar2=None, op0=A.is_equal)),
-              [R("hrep", 16 * k, P), R("hf", k, k + 1)], [R("eqw", P * k, P * k + n)], n / 2, "win")
-        z = tile("B", "W%d" % t)
-        for k0 in range(0, 32, 4):
-            def fz(e, B, inc, k0=k0):
-                if k0 == 0:
-                    inc(e.matmul(B(z)[0:8, 0:P], B("zero")[:, 0:8], B("eqw")[:, 0:P], True, False))
-                for k in range(k0, min(k0 + 4, 31)):
-                    inc(e.matmul(B(z)[0:8, 16 * (k + 1):P], B("b8")[:, 0:8], B("eqw")[:, P * k + 16:P * k + P - 16 * k], False, False))
-            mm(4 * (P - 16 * k0), fz, [R("zero"), R("b8"), R("eqw", P * k0, P * (k0 + 3) + P - 16 * (k0 + 3))], [R(z)], "Z")
-
-        def fzd(e, B, inc):
-            for q in range(16):
-                inc(e.matmul(B(z)[0:8, q:P:16], B("mq")[:, 8 * q:8 * q + 8], B("eqw")[:, q:32 * P:P], False, q == 15))
-        mm(16 * 32, fzd, [R("mq"), R("eqw")], [R(z)], "Zd")
-        s(lambda e, B, inc: inc(e.activation(B("lose")[0:8, 0:P], B(z)[0:8, 0:P], F.Sign)), [R(z)], [R("lose")], P, "lose")
-        wl = tile("B", "W%d" % t)
-
-        def fl(e, B, inc):
-            for q in range(16):
-                inc(e.matmul(B(wl)[:, 0:32], B("mst8")[0:8, 15 - q:143 - q], B("lose")[0:8, q:P:16], q == 0, q == 15))
-        mm(16 * 64, fl, [R("mst8"), R("lose")], [R(wl)], "lose list")
-        tt("lt", wl, "dj", A.mult, 0, 32, 64, name="w")
-        tt("lo", "lt", "hf", A.max, 0, 32, 64, name="w")
-        cp("wu", "lo", 0, 32, 64, name="w")
-
-    def phase_d(t, c):
-        ch = "D%d_%d" % (t, c)
-        gather("vd", "rpu", c)
-        ds = dist("vd", c, [(p, p + 1, p) for p in range(15)], ch, True)
-        first_fail(ds, c, "sb2", "kb", "ind2", ch)
-        cls[0] = "N%d%d" % (t, c)
-        return dist("vd", c, [(p, p + 2, p + 1) for p in range(0, 14, 2)], ch + "n", False)
-
-    def phase_e(t, c, dn):
-        j0, j1, ch = c * CH, (c + 1) * CH, "E%d_%d" % (t, c)
-        s(lambda e, B, inc: inc(e.activation(B("sn")[:, j0:j1], B(dn)[:, 0:CH], F.Sign, scale=-1.0, bias=B("kf")[:, 3:4])), [R(dn), R("kf")], [R("sn", j0, j1)], CH, "near")
-        n1 = tile("B", ch + "n")
-
-        def f6(e, B, inc):
-            inc(e.matmul(B(n1)[:, 0:CH], B("qm")[:, :], B("rp")[:, j0:j1], True, True))
-            inc(e.matmul(B(n1)[:, CH:2 * CH], B("qp")[:, :], B("rp")[:, j0:j1], True, t < RO - 1))
-            if t == RO - 1:
-                inc(e.matmul(B(n1)[:, CH:2 * CH], B("ey")[:, :], B("c1536")[:, :], False, True))
-        mm(2 * CH, f6, [R("qm"), R("qp"), R("ey"), R("c1536"), R("rp", j0, j1), R("sn", j0, j1)], [R(n1)], "n1")
-        tt("t5", n1, "sn", A.mult, j0, j1, slo=0, name="t5")
-        out = "yrs" if t == RO - 1 else "rn%d" % t
-        tt(out, n1, "t5", A.add, j0, j1, slo=CH, name="rn")
+    def phase_d(t, b):
+        j0, j1, i0 = b * BL, (b + 1) * BL, 16 + b * KB
+        gather("vd", "r2u", j0, j1)
+        maxima("md", "vd", j0, j1, 1)
+        maxima("m2", "vd", j0, j1, 2)
+        ds = tile()
+        both, lo, hi = (lambda p: slice(p, 256, 16)), (lambda p: slice(p, 128, 16)), (lambda p: slice(128 + p, 256, 16))
+        init = [(slice(0, 256), "nq", c(j0, j1), "nw", c(0, 256), 256), (slice(0, 256), "ones", c(0, 128, 1, 8), "ci", c(0, 256, 1, 8), 256)]
+        va = []
+        for p in range(15):
+            if p % 2 == 0:
+                va += [(both(p), "vd", rows("vd", j0, p + e), "bm", c(0, 16), 64) for e in (0, 1)]
+            else:
+                va += [(lo(p), "vd", rows("vd", j0, p), "bm", c(0, 8), 64), (both(p), "vd", rows("vd", j0, p + 1), "bm", c(0, 16), 64),
+                       (hi(p), "vd", rows("vd", j0, p - 1), "bm", c(0, 8), 64)]
+        rd = [R("vd", 16 * j0, 16 * j1), R("bm")]
+        mm(ds, init, [R("nq", j0, j1), R("yp", j0, j1), R("nw"), R("ones"), R("ci"), R("vd", 16 * j0, 16 * (j0 + KG))], "init d", True, False)
+        for x in range(0, len(va), 13):
+            mm(ds, va[x:x + 13], rd, "sum d", False, False)
+        mm(ds, [((lo, both)[1 - p % 2](p), "md", rows("md", j0, p), "b2", c(0, 16 - 8 * (p % 2)), 64) for p in range(15)],
+           [R("md", 16 * j0, 16 * j1), R("b2")], "sum m", False, False)
+        mm(ds, [(hi(2 * p + 1), "m2", rows("m2", j0, p, 8), "b2", c(0, 8), 64) for p in range(7)], [R("m2", 8 * j0, 8 * j1), R("b2")], "sum m", False, True)
+        cls[0] = "E%d" % t
+        s(lambda e, B, inc: inc(e.activation(B("sn")[:, i0:i0 + BL], B(ds)[:, 128:256], F.Sign, bias=B("col")[:, CNH:CNH + 1])),
+          [R(ds), R("col", CNH, CNH + 1)], [R("sn", i0, i0 + BL)], BL, "near")
+        cls[0] = "S%d" % t
+        scan("kb", slice(i0, i0 + BL), ds, slice(0, BL), "cap", slice(0, BL), 0.0, A.max, A.min, BL, "kb")
+        cls[0] = "E%d" % t
+        nt = tile()
+        mm(nt, turn(0, BL, "sn", i0, "ey", True, False) + turn(0, BL, "sn", i0 - 1, "ey", False, True), [R("sn", i0 - 1, i0 + BL), R("ey")], "near")
+        tt("t5", nt, "yp", A.mult, j0, j1, slo=0, name="t5")
+        rt = tile()
+        mm(rt, [(slice(0, BL), "tro", al, "yp", c(j0, j1), 4 * BL)], [R("tro"), R("yp", j0, j1), R("sn", i0, i0 + BL)], "rn", True, False)
+        mm(rt, [(slice(0, BL), "ioh", al, "t5", c(j0, j1), 4 * BL)], [R("ioh"), R("t5", j0, j1)], "rn", False, True)
         if t == RO - 1:
-            op("Y", lambda e, B, inc: inc(e.dma_start(B("IN")["yr"][:, j0:j1], B("yrs")[:, j0:j1])), [R("yrs", j0, j1)], [("yr", j0, j1)], 2.5, "store yr", sem="oy%d" % c)
+            s(lambda e, B, inc: inc(e.activation(B("yrs")[:, j0:j1], B(rt)[:, 0:BL], F.Identity, bias=B("col")[:, CSH:CSH + 1])),
+              [R(rt), R("col", CSH, CSH + 1)], [R("yrs", j0, j1)], BL, "rn")
+            op("Y", lambda e, B, inc: inc(e.dma_start(B("IN")["yr"][:, j0:j1], B("yrs")[:, j0:j1])), [R("yrs", j0, j1)], [("yr", j0, j1)], 2.5, "store yr", sem="oy%d" % b)
         else:
-            op("G", ("send", t, c, j0, j1), [R(out, j0, j1)], [], 1.0, "send", sem="ls%d_%d" % (t + 1, c))
-            ops[-1]["sem2"] = "ar%d_%d" % (t + 1, c)
-            op("N", ("arrive", t + 1, c), [R(out, j0, j1)], [R("rf%d" % (t + 1), j0, j1)], 3.5, "arrive", sem="ar%d_%d" % (t + 1, c))
+            out = "rn%d" % t
+            ts(out, rt, float(SH), A.add, lo=j0, hi=j1, cyc=BL, slo=0, name="rn")
+            op("G", ("send", t, j0, j1), [R(out, j0, j1)], [], 1.0, "send", sem="ls%d_%d" % (t + 1, b))
+            ops[-1]["sem2"] = "ar%d_%d" % (t + 1, b)
+            op("N", None, [R(out, j0, j1)], [R("ru%d" % (t + 1), j0, j1)], cost["HOP"], "arrive", sem="ar%d_%d" % (t + 1, b))
             ops[-1]["after"] = len(ops) - 2
-        cls[0] = "S%d%d" % (t, c)
-        om = tile("B", ch)
-
-        def fom(e, B, inc):
-            inc(e.matmul(B(om)[:, 0:CH], B("ey")[:, :], B("ones")[:, 0:CH], True, False))
-            inc(e.matmul(B(om)[:, 0:CH], B("u15n")[:, :], B("ind2")[:, j0:j1], False, True))
-            inc(e.matmul(B(om)[:, CH:2 * CH], B("ey")[:, :], B("rp")[:, j0:j1], True, True))
-        mm(3 * CH, fom, [R("ey"), R("ones"), R("u15n"), R("ind2", j0, j1), R("rp", j0, j1)], [R(om)], "om")
-        tt("indr2", om, "ind2", A.mult, j0, j1, slo=CH, name="indr2")
-        tt("t4", om, "rp", A.mult, j0, j1, slo=0, name="t4")
-        sk = tile("B", ch)
-
-        def fsk(e, B, inc):
-            inc(e.matmul(B(sk)[:, 0:CH], B("ey")[:, :], B("c1536")[:, :], True, False))
-            inc(e.matmul(B(sk)[:, 0:CH], B("u15")[:, :], B("indr2")[:, j0:j1], False, True))
-        mm(2 * CH, fsk, [R("ey"), R("c1536"), R("u15"), R("indr2", j0, j1)], [R(sk)], "sk")
-        tt("st", sk, "t4", A.add, j0, j1, slo=0, name="st")
-        k0, k1 = c * NL, (c + 1) * NL
-        v(lambda e, B, inc: inc(e.tensor_copy(out=B("cache")[:, 0:H + P].indirect(B("wu")[:, k0:k1]), in_=B("st")[:, j0:j1])),
-          [R("wu", k0, k1), R("st", j0, j1)], [R("cache")], SCF * CH, "scatter")
+        cls[0] = "S%d" % t
+        at = tile()
+        mm(at, turn(0, BL, "kb", i0 - 1, "ney"), [R("kb", i0 - 1, i0 + BL), R("ney")], "a2")
+        tt("y2", at, "yp", A.mult, j0, j1, slo=0, name="y2")
+        sk = tile()
+        mm(sk, [(slice(0, BL), "tri", al, "yp", c(j0, j1), 4 * BL)], [R("tri"), R("yp", j0, j1), R("kb", i0, i0 + BL)], "st", True, False)
+        mm(sk, [(slice(0, BL), "t15", al, "y2", c(j0, j1), 4 * BL)], [R("t15"), R("y2", j0, j1)], "st", False, True)
+        s(lambda e, B, inc: inc(e.activation(B("st")[:, j0:j1], B(sk)[:, 0:BL], F.Identity, bias=B("col")[:, CSH:CSH + 1])),
+          [R(sk), R("col", CSH, CSH + 1)], [R("st", j0, j1)], BL, "st")
+        for k in range(j1 // 16 - 1, j0 // 16 - 1, -1):
+            op("V", lambda e, B, inc, k=k: inc(e.tensor_copy(out=B("cache")[:, 0:D0 + H].indirect(B("wu")[:, 2 * k:2 * k + 1]), in_=B("st")[:, 16 * k:16 * k + 16])),
+               [R("wu"), R("st", j0, j1)], [R("cache")], 0.05 + max(cost["SCF"] * 16, 64) * CYC, "scatter")
 
     for t in range(RO):
-        for c in range(NC):
-            cls[0] = "A%d%d" % (t, c)
-            phase_a(t, c)
-        for c in range(NC):
-            cls[0] = "B%d%d" % (t, c)
-            phase_b(t, c)
-            cls[0] = "H%d%d" % (t, c)
-            hrep(t, c)
-        cls[0] = "W%d0" % t
+        for ch in range(NC - 1, -1, -1):
+            cls[0] = "A%d" % t
+            phase_a(t, ch)
+        for ch in range(NC - 1, -1, -1):
+            cls[0] = "B%d" % t
+            phase_b(t, ch)
+        cls[0] = "W%d" % t
         winners(t)
-        for c in range(NC):
-            cls[0] = "D%d%d" % (t, c)
-            dn = phase_d(t, c)
-            cls[0] = "E%d%d" % (t, c)
-            phase_e(t, c, dn)
-    op("Y", lambda e, B, inc: inc(e.dma_start(B("IN")["yc"][:, :], B("cache")[:, 0:H])), [R("cache", 0, H)], [("yc", 0, H)], 3.0, "store yc", sem="oc")
+        for b in range(NB - 1, -1, -1):
+            cls[0] = "D%d" % t
+            phase_d(t, b)
+    op("Y", lambda e, B, inc: inc(e.dma_start(B("IN")["yc"][:, :], B("cache")[:, D0:D0 + H])), [R("cache")], [("yc", 0, H)], 3.5, "store yc", sem="oc")
     return ops, tiles
 
 
@@ -493,28 +413,26 @@ def deps_of(ops, key, cross):
         for rw, regs in (("r", o["r"]), ("w", o["w"])):
             for (b, lo, hi) in regs:
                 h = hist.setdefault(key(b), [])
-                if rw == "w" and not cross(b):
+                if rw == "w":
                     h[:] = [x for x in h if not (lo <= x[0] and x[1] <= hi)]
                 h.append((lo, hi, rw, o))
         out.append(d)
     return out
 
 
-PSUM = set(k for k in SCRATCH if SCRATCH[k][0] == "psum")
+def free_of_wait(o, o2, kinds):
+    return o["q"] == o2["q"] == "T" and all(cr for _, cr in kinds)
 
 
-def is_tile(b):
-    return b in PSUM
-
-
-def schedule():
-    ops, tiles = build_ops()
+def schedule(cost=COST, bias=BIAS):
+    ops, tiles = build_ops(cost)
+    LAT = cost["LAT"]
     for o in ops:
         o["q"] = o["qs"][0]
         for b, lo, hi in o["r"] + o["w"]:
             if isinstance(b, tuple):
                 tiles[b[1]]["users"] += 1
-    dep = deps_of(ops, lambda b: b, lambda b: isinstance(b, tuple) and tiles[b[1]]["pool"] != "AD")
+    dep = deps_of(ops, lambda b: b, lambda b: isinstance(b, tuple))
     n = len(ops)
     succ = [[] for _ in range(n)]
     left = [len(dep[i]) for i in range(n)]
@@ -525,41 +443,35 @@ def schedule():
     for i in range(n - 1, -1, -1):
         rank[i] = ops[i]["dur"] + max([rank[j] + LAT for j in succ[i]] or [0.0])
     for i in range(n):
-        rank[i] += BIAS.get(ops[i]["cls"], 0.0)
+        rank[i] += bias.get(ops[i]["cls"], bias.get(ops[i]["cls"][0], 0.0))
     free = {q: 0.0 for q in "VSTGYAN"}
-    pool = {k: {b: 0.0 for b in v_} for k, v_ in POOLS.items()}
-    live, endt, order = {}, [0.0] * n, []
+    pool = {"p%d" % i: 0.0 for i in range(NPS)}
+    endt, order, est = [0.0] * n, [], {}
     ready = [i for i in range(n) if left[i] == 0]
     while ready:
         cands = []
         for i in ready:
             o = ops[i]
-            est0 = max([endt[d] + (LAT if any(k != "rw" for k, _ in kk) or ops[d]["q"] != o["qs"][0] else 0.0) for d, kk in dep[i].items()] or [0.0])
-            okay = True
-            for b, lo, hi in o["w"]:
-                if isinstance(b, tuple) and tiles[b[1]]["buf"] is None:
-                    tl = tiles[b[1]]
-                    fr = pool[tl["pool"]]
-                    if not fr or (tl["pool"] == "B" and len(fr) < 2 and not live.get(tl["chain"], 0)):
-                        okay = False
-                    else:
-                        est0 = max(est0, min(fr.values()) + LAT)
-            if okay:
-                for q in o["qs"]:
-                    cands.append((max(est0, free[q] if q != "N" else 0.0), -rank[i], i, q))
+            if i not in est:
+                est[i] = max([endt[d] + (0.0 if free_of_wait(o, ops[d], kk) else LAT) for d, kk in dep[i].items()] or [0.0])
+            e0 = est[i]
+            new = [b for b, lo, hi in o["w"] if isinstance(b, tuple) and tiles[b[1]]["buf"] is None]
+            if new:
+                if len(pool) < 1 + (o["name"] in ("sum a", "init d", "rn", "st")):
+                    continue
+                e0 = max(e0, min(pool.values()) + LAT)
+            for q in o["qs"]:
+                cands.append((max(e0, free[q] if q != "N" else 0.0), -rank[i], i, q))
         assert cands, "no operation can go on"
-        t0 = min(c[0] for c in cands)
-        st, _, i, q = min([c for c in cands if c[0] <= t0 + 0.03], key=lambda c: (c[1], c[0]))
+        t0 = min(x[0] for x in cands)
+        st, _, i, q = min([x for x in cands if x[0] <= t0 + 0.03], key=lambda x: (x[1], x[0]))
         o = ops[i]
         o["q"] = q
         for b, lo, hi in o["w"]:
             if isinstance(b, tuple) and tiles[b[1]]["buf"] is None:
-                tl = tiles[b[1]]
-                fr = pool[tl["pool"]]
-                bb = min(fr, key=lambda x: fr[x])
-                del fr[bb]
-                tl["buf"] = bb
-                live[tl["chain"]] = live.get(tl["chain"], 0) + 1
+                bb = min(pool, key=lambda x: pool[x])
+                del pool[bb]
+                tiles[b[1]]["buf"] = bb
         e = st + o["dur"]
         endt[i], o["t0"], o["t1"] = e, st, e
         free[q] = st + 0.1 if q in "YA" else e
@@ -571,8 +483,7 @@ def schedule():
                 tl["users"] -= 1
                 tl["end"] = max(tl.get("end", 0.0), e)
                 if tl["users"] == 0:
-                    pool[tl["pool"]][tl["buf"]] = tl["end"]
-                    live[tl["chain"]] -= 1
+                    pool[tl["buf"]] = tl["end"]
         order.append(i)
         ready.remove(i)
         for j in succ[i]:
@@ -590,8 +501,8 @@ def plan():
     if not PLAN:
         seq, tiles, end = schedule()
         key = lambda b: tiles[b[1]]["buf"] if isinstance(b, tuple) else b
-        PLAN["seq"], PLAN["tiles"], PLAN["end"] = seq, tiles, end
-        PLAN["dep"] = deps_of(seq, key, lambda b: is_tile(key(b)))
+        PLAN["seq"], PLAN["tiles"] = seq, tiles
+        PLAN["dep"] = deps_of(seq, key, lambda b: isinstance(b, tuple))
     return PLAN
 
 
@@ -601,6 +512,7 @@ def rank_program(g, core, T, topo):
         return
     pl = plan()
     tiles = pl["tiles"]
+    byid = {o["id"]: o for o in pl["seq"]}
     dst = T.cores[(rank + ST) % len(T.cores)]
     src = T.cores[(rank - ST) % len(T.cores)]
     rid, pid, _ = topo.addr(dst)
@@ -634,24 +546,23 @@ def rank_program(g, core, T, topo):
         h = host[q]
         kn, need = known[h], {}
         for d, kinds in dep.items():
-            sem, c, imp = done[d]
-            if sem == "q" + h:
-                if (h == "T" and all(cr for _, cr in kinds)) or all(k == "rw" for k, _ in kinds):
-                    continue
-            if c > need.get(sem, (0, None))[0]:
-                need[sem] = (c, imp)
-        for sem in sorted(need, key=lambda x: -need[x][0]):
-            c, imp = need[sem]
-            if kn.get(sem, 0) >= c:
+            sem, n, imp = done[d]
+            if free_of_wait(o, byid[d], kinds):
                 continue
-            eng[q].wait_ge(T.sem[sem], c)
-            kn[sem] = c
+            if n > need.get(sem, (0, None))[0]:
+                need[sem] = (n, imp)
+        for sem in sorted(need, key=lambda x: -need[x][0]):
+            n, imp = need[sem]
+            if kn.get(sem, 0) >= n:
+                continue
+            eng[q].wait_ge(T.sem[sem], n)
+            kn[sem] = n
             for s2, c2 in imp.items():
                 kn[s2] = max(kn.get(s2, 0), c2)
         cur[0] = q
         if isinstance(o["fn"], tuple):
-            _, t, c, j0, j1 = o["fn"]
-            g.remote_dma(T["rf%d" % (t + 1)][:, j0:j1], T["rn%d" % t][:, j0:j1], T.sem[o["sem2"]], T.sem[o["sem"]], pid, rid, emask)
+            _, t, j0, j1 = o["fn"]
+            g.remote_dma(T["ru%d" % (t + 1)][:, j0:j1], T["rn%d" % t][:, j0:j1], T.sem[o["sem2"]], T.sem[o["sem"]], pid, rid, emask)
             done[o["id"]] = (o["sem"], ne, {})
             pend[o["sem"]] = ne
         elif o["sem"]:

@@ -9,7 +9,7 @@ BL = 128
 NB = P // BL
 KG = 32
 SC = 128
-D0 = 16
+D0 = 32
 KA, KB = CH + 16, BL + 16
 
 SCRATCH = {}
@@ -20,30 +20,51 @@ def bufs(dtype, **sizes):
         SCRATCH[k] = ("sbuf", [128, sizes[k]], dtype)
 
 
-bufs("bfloat16", xs=W, va=16 * P, vd=16 * P, mx=16 * P, md=16 * P, m2=8 * P, ka=NC * KA, kb=NB * KB, sn=NB * KB, nm=P, nq=P,
-     eqp=8 * P, eqh=256)
-bufs("float16", rf=P, indr=P, r2=P, hh=32)
-bufs("uint16", ru0=P, ru1=P, ru2=P, rn0=P, rn1=P, r2u=P, hu=32, wu=64)
+bufs("bfloat16", xs=W, va=16 * P, vd=16 * P, mx=16 * P, md=16 * P, m2=8 * P, ka=NC * KA, kb=NB * KB, sn=3 * P, sa=P, nm=P, nq=P,
+     eqp=8 * P, eqh=512)
+bufs("float16", rf0=P, rf1=P, rf2=P, rn0=P, rn1=P, indr=P, r2=P, hh=32)
+bufs("uint16", ru=P, r2u=P, hu=32, wu=32)
 bufs("int32", r0i=P, c0i=H, pi=32, hm=32, ki=8, kp=8, ks=8, kt=8, ia=256, ib=256)
 bufs("float32", cache=D0 + H, t1=P, yp=P, y2=P, t5=P, st=P, yrs=P, r15=32, pri=32, kacc=8, kcol=8, col=16, rio=16, fa=16, fb=16, fc=16,
-     onesf=128, zerof=128, tri=128, tra=128, tro=128, trb=128, ioh=128, t15=128, kw=128)
-bufs("bfloat16", ones=CH, zero=256, ey=128, ney=128, b2=16, b2a=16, bm=16, bma=16, ci=256, ca=CH, nw=256, cap=CH, ms=432, c192=16, ni15=128,
-     c15=128, pq=256, pd=128, pb=1024, vw=480, dl=128)
+     onesf=128, tri=128, tra=128, t15=128, kw=128, bmf=8)
+bufs("bfloat16", ones=CH, zero=2048, pe=1024, po=2048, lw=248, lwa=8, ey=128, ney=128, hey=128, e15=128, cap2=128, b2=8, b2a=8, bm=8, bma=8, cm8=128, ca=CH, nw=384, cap=CH, ms=432, c192=128,
+     ni15=128, c15=128, pq=256, pd=128, pb=1024, vw=480, dl=128)
 NPS = 8
 for _i in range(NPS):
-    SCRATCH["p%d" % _i] = ("psum", [128, 512], "float32")
-SEMAPHORES = (["qV", "qS", "qT", "qG", "lr", "lx", "lc", "oc"] + ["oy%d" % b for b in range(NB)]
+    SCRATCH["p%d" % _i] = ("psum", [128, 4, 8, 16], "float32")
+SCRATCH["we"] = ("sbuf", [128, 3, 8, 3], "bfloat16")
+SCRATCH["wo"] = ("sbuf", [128, 2, 8, 2], "bfloat16")
+SCRATCH["wx"] = ("sbuf", [128, 2, 8, 2], "bfloat16")
+ALL = slice(None)
+
+
+def bank_view(w):
+    if isinstance(w, tuple):
+        return (ALL, w[0], ALL, w[1]) if len(w) == 2 else (ALL,) + w
+    a, b = w.start, w.stop
+    if a % 128 == 0 and b % 128 == 0:
+        return (ALL, slice(a // 128, b // 128), ALL, ALL)
+    if a % 16 == 0 and b % 16 == 0:
+        return (ALL, a // 128, slice(a % 128 // 16, (b - 1) % 128 // 16 + 1), ALL)
+    return (ALL, a // 128, a % 128 // 16, slice(a % 16, (b - 1) % 16 + 1))
+
+
+SEMAPHORES = (["qV", "qS", "qT", "qG", "lr", "lq", "lx", "lc", "oc"] + ["oy%d" % b for b in range(NB)]
               + ["ar%d_%d" % (t, b) for t in range(1, RO) for b in range(NB)]
               + ["ls%d_%d" % (t, b) for t in range(1, RO) for b in range(NB)])
 
 COST = {"CYC": 0.00083, "TCYC": 0.00042, "LAT": 0.12, "GF": 1.56, "SCF": 3.8, "HOP": 3.5}
-BIAS = {}
-VG = {"A0"}
-CQ, CLO, CHI, CSC, CBI, CNH, CW, C15, CSH = range(9)
+BIAS = {"load x": 99}
+URGENT = dict({"load x": 99}, **{k: 50 for k in ("bad", "nm", "st", "near")},
+              **{k: 3 for k in ("ka", "indr", "l", "cache gather", "r2", "r2u", "ru", "t5", "rn")})
+WAIT = {}
+QBAD = "S"
+VG = {"A0", "A1", "A2"}
+CQ, CQ2, CLO, CHI, CSC, CBI, CNH, CW, C15, CSH = range(10)
 
 
 def build_ops(cost):
-    ops, tiles, cls = [], [], ["C"]
+    ops, tiles, cls = [], [], ["C", 0]
     CYC, TCYC, GF = cost["CYC"], cost["TCYC"], cost["GF"]
 
     def tile():
@@ -51,10 +72,10 @@ def build_ops(cost):
         return ("tile", len(tiles) - 1)
 
     def op(qs, fn, reads, writes, dur, name="", sem=None):
-        ops.append({"qs": qs, "fn": fn, "r": reads, "w": writes, "dur": dur, "name": name, "sem": sem, "id": len(ops), "cls": cls[0]})
+        ops.append({"qs": qs, "fn": fn, "r": reads, "w": writes, "dur": dur, "name": name, "sem": sem, "id": len(ops), "cls": cls[0], "part": cls[1]})
 
     def R(buf, lo=0, hi=None):
-        if isinstance(buf, tuple):
+        if isinstance(buf, tuple) or len(SCRATCH[buf][1]) > 2:
             return (buf, 0, 512)
         return (buf, lo, SCRATCH[buf][1][1] if hi is None else hi)
 
@@ -71,7 +92,7 @@ def build_ops(cost):
         def fn(e, B, inc):
             for i, x in enumerate(terms):
                 a, z = (x[6], x[7]) if len(x) > 6 else (first and i == 0, last and i == len(terms) - 1)
-                inc(e.matmul(B(out)[:, x[0]], B(x[1])[x[2]], B(x[3])[x[4]], a, z))
+                inc(e.matmul(B(out, x[0]), B(x[1])[x[2]], B(x[3])[x[4]], a, z))
         op("T", fn, reads, [R(out)], sum(x[5] for x in terms) * TCYC + 0.03, name)
 
     def c(lo, hi, st=1, p=128):
@@ -84,16 +105,16 @@ def build_ops(cost):
 
         def fn(e, B, inc):
             if o2 is None:
-                inc(e.tensor_scalar(out=B(dst)[:, w], in0=B(src)[:, a:b], scalar1=val(B, s1), scalar2=None, op0=o1))
+                inc(e.tensor_scalar(out=B(dst)[:, w], in0=B(src, slice(a, b)), scalar1=val(B, s1), scalar2=None, op0=o1))
             else:
-                inc(e.tensor_scalar(out=B(dst)[:, w], in0=B(src)[:, a:b], scalar1=val(B, s1), scalar2=val(B, s2), op0=o1, op1=o2))
+                inc(e.tensor_scalar(out=B(dst)[:, w], in0=B(src, slice(a, b)), scalar1=val(B, s1), scalar2=val(B, s2), op0=o1, op1=o2))
         cols = [R(x[0], x[1], x[1] + 1) for x in (s1, s2) if isinstance(x, tuple)]
         v(fn, [R(src, a, b)] + cols, [R(dst, w.start, w.stop)], cyc, name)
 
     def tt(dst, in0, in1, o, lo, hi, cyc=None, slo=None, name="tt", lo1=None):
         a, b = (lo, hi) if slo is None else (slo, slo + hi - lo)
         a1, b1 = (lo, hi) if lo1 is None else (lo1, lo1 + hi - lo)
-        v(lambda e, B, inc: inc(e.tensor_tensor(out=B(dst)[:, lo:hi], in0=B(in0)[:, a:b], in1=B(in1)[:, a1:b1], op=o)),
+        v(lambda e, B, inc: inc(e.tensor_tensor(out=B(dst)[:, lo:hi], in0=B(in0, slice(a, b)), in1=B(in1)[:, a1:b1], op=o)),
           [R(in0, a, b), R(in1, a1, b1)], [R(dst, lo, hi)], (hi - lo) if cyc is None else cyc, name)
 
     def cp(dst, src, lo, hi, cyc, slo=None, name="cp"):
@@ -102,16 +123,22 @@ def build_ops(cost):
 
     def scan(dst, dv, a, av, b, bv, init, o0, o1, cyc, name):
         rng = lambda x, w: R(x, w.start, w.stop)
-        v(lambda e, B, inc: inc(e.tensor_tensor_scan(B(dst)[:, dv], B(a)[:, av], B(b)[:, bv], init, o0, o1)),
+        v(lambda e, B, inc: inc(e.tensor_tensor_scan(B(dst)[:, dv], B(a, av), B(b)[:, bv], init, o0, o1)),
           [rng(a, av), rng(b, bv)], [rng(dst, dv)], cyc, name)
 
-    op("A", lambda e, B, inc: inc(e.dma_start(B("r0i")[:, :], B("IN")["r0"][:, :])), [], [R("r0i")], 2.5, "load r0", sem="lr")
+    op("A", lambda e, B, inc: inc(e.dma_start(B("r0i")[:, CH:P], B("IN")["r0"][:, CH:P])), [], [R("r0i", CH, P)], 2.5, "load r0", sem="lr")
     op("Y", lambda e, B, inc: inc(e.dma_start(B("xs")[:, :], B("IN")["x"][:, :])), [], [R("xs")], 5.0, "load x", sem="lx")
+    op("Y", lambda e, B, inc: inc(e.dma_start(B("r0i")[:, 0:CH], B("IN")["r0"][:, 0:CH])), [], [R("r0i", 0, CH)], 5.4, "load r0", sem="lq")
     op("Y", lambda e, B, inc: inc(e.dma_start(B("c0i")[:, :], B("IN")["c0"][:, :])), [], [R("c0i")], 7.0, "load c0", sem="lc")
 
     def fill(buf, val, lo=0, hi=None, st=1):
         hi = SCRATCH[buf][1][1] if hi is None else hi
         v(lambda e, B, inc: inc(e.memset(B(buf)[:, lo:hi:st], val)), [], [R(buf, lo, hi)], (hi - lo) / st / 2, "fill")
+
+    def sfill(buf, val, lo=0, hi=None, st=1):
+        hi = SCRATCH[buf][1][1] if hi is None else hi
+        n, src = len(range(lo, hi, st)), "ones" if val else "zero"
+        s(lambda e, B, inc: inc(e.activation(B(buf)[:, lo:hi:st], B(src)[:, 0:n], F.Copy, scale=val)), [R(src, 0, n)], [R(buf, lo, hi)], n, "fill")
 
     def sel(dst, src, pat, cmp, fillv, base, cm, view=None, sview=None):
         n = 1
@@ -120,7 +147,7 @@ def build_ops(cost):
         w = slice(0, n) if view is None else view
         u = w if sview is None else sview
         gp(lambda e, B, inc: inc(e.affine_select(out=B(dst)[:, w], in_=B(src)[:, u], pattern=pat, compare_op=cmp, fill=fillv, base=base, channel_multiplier=cm)),
-           [R(src)], [R(dst)], n, "sel " + dst)
+           [R(src, u.start, u.stop)], [R(dst)], n, "sel " + dst)
 
     def iota(dst, lo, hi, pat, base, cm, flt=False):
         if flt:
@@ -128,27 +155,33 @@ def build_ops(cost):
         else:
             gp(lambda e, B, inc: inc(e.iota(B(dst)[:, lo:hi], pat, base, cm)), [], [R(dst, lo, hi)], hi - lo, "iota")
 
+    def weights(dst, parts):
+        for x, y, src in parts:
+            gp(lambda e, B, inc, x=x, y=y, src=src: inc(e.affine_select(out=B(dst)[:, x, :, y], in_=B(src)[:, 0:8], pattern=[[0, 8]], compare_op=A.is_ge,
+                                                                        fill=0.0, base=0, channel_multiplier=0)),
+               [R(src, 0, 8)], [(dst, 3 * x + y, 3 * x + y + 1)], 8, "sel " + dst)
+
     NE, GE = A.not_equal, A.is_ge
-    fill("zero", 0.0)
+    fill("zero", 0.0, 0, 512)
     fill("ones", 1.0)
-    for a, z, val in (("b2a", "b2", 2.0), ("bma", "bm", -1.0)):
-        sel(a, "zero", [[0, 2], [16, 8]], A.is_gt, val, 0, -1)
-        sel(z, a, [[0, 2], [16, 8]], GE, 0.0, 15, -1)
-    fill("ca", -5.0)
+    fill("zero", 0.0, 512)
+    for a, z, val in (("bma", "bm", -1.0), ("b2a", "b2", 2.0)):
+        sel(a, "zero", [[16, 8]], A.is_gt, val, 0, -1)
+        sel(z, a, [[16, 8]], GE, 0.0, 15, -1)
+    weights("wo", [(0, 0, "bm"), (0, 1, "bm")])
+    sfill("ca", -5.0)
     sel("cap", "ones", [[0, CH // 16], [1, 16]], NE, 0.0, -15, 0)
     sel("ey", "zero", [[-1, 128]], NE, 1.0, 0, 1)
     sel("ney", "zero", [[-1, 128]], NE, -1.0, 0, 1)
-    fill("ka", 0.0)
-    fill("ms", 0.0)
+    sfill("ka", 0.0, 15, NC * KA, KA)
+    sfill("ms", 0.0)
     w8 = slice(0, 8)
     sel("b2a", "ones", [[-16, 8]], GE, 0.0, 0, 1)
     sel("ms", "b2a", [[16, 8]], GE, 0.0, 14, -1, slice(15, 143, 16), w8)
     sel("ms", "zero", [[-16, 8]], NE, 1.0, -15, 1, slice(159, 287, 16), w8)
     sel("ms", "zero", [[-16, 8]], NE, 0.125, -15, 1, slice(303, 431, 16), w8)
-    fill("c192", SH / 8.0)
+    sfill("c192", SH / 8.0)
     iota("ki", 0, 1, [[0, 1]], 0, 1)
-    iota("ia", 0, 128, [[0, 8], [1, 16]], 128, -1)
-    iota("ia", 128, 256, [[1, 8], [1, 16]], 129, -1)
     iota("rio", 0, 16, [[1, 16]], 0, 0, True)
     sel("ni15", "ney", [[0, 8], [1, 16]], NE, 0.0, -15, 0)
     ts("kp", "ki", 15, A.bitwise_and)
@@ -156,15 +189,22 @@ def build_ops(cost):
     ts("col", "kp", 15.0, A.is_equal, lo=C15, hi=C15 + 1, slo=0)
     ts("col", "col", 10240.0, A.mult, 6144.0, A.add, lo=CSC, hi=CSC + 1, slo=C15)
     ts("col", "col", -16896.0, A.mult, -7680.0, A.add, lo=CBI, hi=CBI + 1, slo=C15)
-    fill("c15", -960.0)
-    fill("c15", 0.0, 15, 128, 16)
-    fill("cache", 0.0, 0, D0)
+    ts("col", "kp", 16.0, A.add, lo=CQ2, hi=CQ2 + 1, slo=0)
+    sfill("c15", -960.0)
+    sfill("c15", 0.0, 15, 128, 16)
+    sfill("cache", 0.0, 0, D0)
     cp("cache", "c0i", D0, D0 + H, H, slo=0)
+    cls[0] = "K0"
+    iota("ia", 0, 128, [[0, 8], [1, 16]], 128, -1)
+    iota("ia", 128, 256, [[1, 8], [1, 16]], 129, -1)
     ts("ib", "ia", 15, A.bitwise_and, hi=256, cyc=256)
     ts("pq", "ib", 0.0, A.is_equal, hi=256, cyc=256)
     tt("pd", "pq", "pq", A.subtract, 0, 128, 256, lo1=128)
+    sel("bmf", "bm", [[0, 8]], GE, 0.0, 0, 0)
     for g in range(8):
-        ts("pb", "pd", ("bm", g), A.mult, lo=128 * g, hi=128 * g + 128, slo=0)
+        s(lambda e, B, inc, g=g: inc(e.activation(B("pb")[:, 128 * g:128 * g + 128], B("pd")[:, 0:128], F.Copy, scale=B("bmf")[:, g:g + 1])),
+          [R("pd"), R("bmf")], [R("pb", 128 * g, 128 * g + 128)], 128, "pb")
+    cls[0] = "C0"
     sel("dl", "ey", [[-1, 128]], NE, -1.0, 1, 1)
     sel("dl", "ones", [[-16, 8]], A.is_equal, 0.0, 0, 1, slice(0, 128, 16), w8)
     ts("ks", "ki", 4, A.arith_shift_right)
@@ -173,7 +213,7 @@ def build_ops(cost):
     ts("kt", "ks", 15, A.bitwise_and)
     tt("col", "kp", "kt", A.min, CLO, CLO + 1, 64, slo=0, lo1=0)
     tt("col", "kp", "kt", A.max, CHI, CHI + 1, 64, slo=0, lo1=0)
-    fill("vw", 0.0)
+    sfill("vw", 0.0)
     ts("fa", "rio", ("col", CLO), A.is_gt, 2.0 ** -8, A.max, hi=16)
     v(lambda e, B, inc: inc(e.tensor_reduce(B("col")[:, CW:CW + 1], B("fa")[:, 0:16], AX.X, A.mult)), [R("fa")], [R("col", CW, CW + 1)], 64, "red")
     ts("fb", "rio", ("col", CLO), A.is_gt, 17.0 * 2.0 ** 60, A.mult, hi=16)
@@ -181,25 +221,31 @@ def build_ops(cost):
     tt("fa", "fb", "fc", A.mult, 0, 16, 64)
     ts("vw", "fa", -2.0 ** 60, A.add, ("col", CW), A.mult, lo=112, hi=128, slo=0)
     ts("vw", "rio", ("col", CHI), A.is_equal, -4096.0, A.mult, lo=352, hi=368, slo=0)
-    fill("ci", -37.0, 0, 128)
-    fill("ci", -5.0, 128, 256, 2)
-    fill("ci", 27.0, 129, 256, 2)
     sel("nw", "zero", [[-1, 128]], NE, 256.0, -1, 1)
-    sel("nw", "zero", [[-2, 64]], NE, 256.0, -2, 1, slice(128, 256, 2), slice(0, 64))
-    sel("nw", "zero", [[-2, 64]], NE, -256.0, -2, 1, slice(129, 256, 2), slice(0, 64))
-    fill("kb", 0.0)
-    fill("sn", 0.0)
-    fill("col", -0.5, CNH, CNH + 1)
-    fill("col", float(SH), CSH, CSH + 1)
+    sel("nw", "nw", [[-16, 8], [0, 16]], NE, -296.0, 0, 1)
+    sel("nw", "zero", [[0, 2], [-16, 8], [0, 16]], NE, 216.0, 0, 1, slice(128, 384), slice(0, 256))
+    sel("nw", "nw", [[-2, 64]], NE, -256.0, -2, 1, slice(129, 256, 2))
+    sel("nw", "nw", [[-2, 64]], NE, 256.0, -2, 1, slice(257, 384, 2))
+    sel("nw", "nw", [[-16, 8], [0, 8]], NE, -40.0, 0, 1, slice(257, 384, 2))
+    sel("nw", "zero", [[0, 2], [-16, 8]], NE, 216.0, 0, 1, slice(143, 384, 16), slice(0, 16))
+    weights("wo", [(1, 0, "zero"), (1, 1, "bm")])
+    weights("we", [(x, y, "bm" if k else "zero") for x, ks in enumerate(((1, 1, 0), (1, 0, 1), (0, 0, 1))) for y, k in enumerate(ks)])
+    weights("wx", [(x, y, "b2" if x == y else "zero") for x in (0, 1) for y in (0, 1)])
+    sel("hey", "zero", [[-1, 128]], NE, -0.5, 0, 1)
+    sel("e15", "ey", [[0, 8], [1, 16]], A.is_equal, 0.0, -15, 0)
+    sel("cap2", "zero", [[0, 8], [1, 16]], NE, 1.0, -15, 0)
+    sfill("cm8", -0.125)
+    sfill("kb", 1.0, 15, NB * KB, KB)
+    sfill("col", 0.5, CNH, CNH + 1)
+    sfill("col", float(SH), CSH, CSH + 1)
+    sel("pe", "zero", [[-16, 8], [0, 8], [-1, 16]], NE, 1.0, 0, 1)
+    sel("po", "zero", [[-1, 128], [0, 16]], NE, -1.0, 0, 1)
+    sfill("lw", 0.0)
+    sel("lwa", "zero", [[16, 8]], A.is_gt, -4096.0, 0, -1)
+    sel("lw", "lwa", [[16, 8]], GE, 0.0, 15, -1, slice(120, 128), w8)
     iota("onesf", 0, 128, [[0, 128]], 1, 0, True)
-    iota("zerof", 0, 128, [[0, 128]], 0, 0, True)
     sel("tra", "onesf", [[1, 128]], GE, 0.0, 0, -1)
     sel("tri", "tra", [[-16, 8], [0, 16]], GE, 0.0, 0, 1)
-    odd = [[-2, 64], [-1001, 2]]
-    sel("tro", "tri", odd, NE, 0.0, 1000, 1)
-    sel("tro", "tri", [[0, 8]], GE, 0.0, 0, 0, slice(15, 128, 16))
-    sel("trb", "zerof", odd, NE, 0.5, 1000, 1)
-    sel("ioh", "trb", [[0, 8], [1, 16]], NE, 0.0, -15, 0)
     sel("t15", "tri", [[0, 8], [1, 16]], NE, 0.0, -15, 0)
     ts("kw", "onesf", ("col", C15), A.mult, 1.0 / 256, A.mult, hi=128, cyc=128)
 
@@ -227,27 +273,34 @@ def build_ops(cost):
         return [(slice(o0, o0 + n), "ms", c(m0 + 15 - q, m0 + 143 - q), src, c(j0 + q, j1, 16), 64) for q in range(16)]
 
     def phase_a(t, ch):
-        j0, j1, ru, i0 = ch * CH, (ch + 1) * CH, "ru%d" % t, 16 + ch * KA
+        j0, j1, rf, i0 = ch * CH, (ch + 1) * CH, "rf%d" % t, 16 + ch * KA
         ds = tile()
         first = True
         for j in range(j1 - BL, j0 - 1, -BL):
             if t == 0:
-                cp(ru, "r0i", j, j + BL, BL, name="ru")
-            ts("rf", ru, float(-SH), A.add, lo=j, hi=j + BL, cyc=BL / 2, name="rf")
-            gather("va", ru, j, j + BL)
+                cp("ru", "r0i", j, j + BL, BL, name="ru")
+                ts(rf, "ru", float(-SH), A.add, lo=j, hi=j + BL, cyc=BL / 2, name="rf")
+            else:
+                ts("ru", rf, float(SH), A.add, lo=j, hi=j + BL, cyc=BL / 2, name="ru")
+            gather("va", "ru", j, j + BL)
             maxima("mx", "va", j, j + BL, 1)
-            o = lambda p: slice(j - j0 + p, j - j0 + BL, 16)
-            va = [(o(p), "va", rows("va", j, p + e), "bm", c(0, 8), 64) for p in range(15) for e in (0, 1)]
+            x = (j - j0) // BL
+            va = [((x, slice(max(p - 1, 0), min(p + 1, 15))), "va", rows("va", j, p), "wo", (ALL, 0, ALL, slice(0, 1 + (0 < p < 15))), 64) for p in range(16)]
             init = [(slice(0, CH), "ones", c(0, 128, 1, 8), "ca", c(0, CH, 1, 8), CH)] if first else []
-            rd = [R("va", 16 * j, 16 * (j + BL)), R("bm"), R("ones"), R("ca")]
-            mm(ds, init + va[:15], rd, "sum a", first, False)
-            mm(ds, va[15:], rd, "sum a", False, False)
-            mm(ds, [(o(p), "mx", rows("mx", j, p), "b2", c(0, 8), 64) for p in range(15)], [R("mx", 16 * j, 16 * (j + BL)), R("b2")], "sum m", False, j == j0)
+            mm(ds, init + va, [R("va", 16 * j, 16 * (j + BL)), ("wo", 0, 2), R("ones"), R("ca")], "sum a", first, False)
+            mm(ds, [((x, p), "mx", rows("mx", j, p), "b2", c(0, 8), 64) for p in range(15)], [R("mx", 16 * j, 16 * (j + BL)), R("b2")], "sum m", False, j == j0)
             first = False
-        scan("ka", slice(i0, i0 + CH), ds, slice(0, CH), "cap", slice(0, CH), 0.0, A.max, A.min, CH, "ka")
+
+        def bad(e, B, inc):
+            if B("Q") == "S":
+                inc(e.activation(B("sa")[:, j0:j1], B(ds, slice(0, CH)), F.Sign))
+            else:
+                inc(e.tensor_scalar(out=B("sa")[:, j0:j1], in0=B(ds, slice(0, CH)), scalar1=0.0, scalar2=None, op0=A.is_gt))
+        op(QBAD, bad, [R(ds)], [R("sa", j0, j1)], 0.06 + CYC * CH, "bad")
+        scan("ka", slice(i0, i0 + CH), "sa", slice(j0, j1), "cap", slice(0, CH), 0.0, A.max, A.min, CH / 2, "ka")
         cls[0] = "R%d" % t
         l15 = tile()
-        mm(l15, lists(l15, 0, NL, 144, "rf", j0, j1), [R("ms"), R("rf", j0, j1)], "r15")
+        mm(l15, lists(l15, 0, NL, 144, rf, j0, j1), [R("ms"), R(rf, j0, j1)], "r15")
         ts("r15", l15, float(SH + 64), A.add, lo=ch * NL, hi=(ch + 1) * NL, slo=0, name="r15")
 
     def turn(o0, n, buf, i0, m, start=True, stop=True):
@@ -255,11 +308,11 @@ def build_ops(cost):
 
     def phase_b(t, ch):
         j0, j1, k0, k1, i0 = ch * CH, (ch + 1) * CH, ch * NL, (ch + 1) * NL, 16 + ch * KA
-        kr = [R("ka", i0 - 1, i0 + CH), R("ey"), R("ney")]
+        kr, rf = [R("ka", i0 - 1, i0 + CH), R("ey"), R("ney")], "rf%d" % t
         qt = tile()
         a, b = turn(0, CH, "ka", i0, "ey", True, False), turn(0, CH, "ka", i0 - 1, "ney", False, True)
-        mm(qt, [x for ab in zip(a, b) for x in ab], kr + [R("rf", j0, j1)], "ind")
-        tt("indr", qt, "rf", A.mult, j0, j1, slo=0, name="indr")
+        mm(qt, [x for ab in zip(a, b) for x in ab], kr + [R(rf, j0, j1)], "ind")
+        tt("indr", qt, rf, A.mult, j0, j1, slo=0, name="indr")
         qa = tile()
         mm(qa, turn(0, CH, "ka", i0 - 1, "ey"), kr, "a")
         kc = t * NC + ch
@@ -267,9 +320,9 @@ def build_ops(cost):
         def fnm(e, B, inc):
             sc, bi = B("col")[:, CSC:CSC + 1], B("col")[:, CBI:CBI + 1]
             if t < RO - 1:
-                inc(e.activation(B("nm")[:, j0:j1], B(qa)[:, 0:CH], F.Identity, bias=bi, scale=sc, accum_out=B("kacc")[:, kc:kc + 1]))
+                inc(e.activation(B("nm")[:, j0:j1], B(qa, slice(0, CH)), F.Identity, bias=bi, scale=sc, accum_out=B("kacc")[:, kc:kc + 1]))
             else:
-                inc(e.activation(B("nm")[:, j0:j1], B(qa)[:, 0:CH], F.Identity, bias=bi, scale=sc))
+                inc(e.activation(B("nm")[:, j0:j1], B(qa, slice(0, CH)), F.Identity, bias=bi, scale=sc))
         s(fnm, [R(qa), R("col", CSC, CBI + 1)], [R("nm", j0, j1), R("kacc", kc, kc + 1)], CH + 24, "nm")
         ll = tile()
         mm(ll, lists(ll, 0, NL, 0, "indr", j0, j1) + [(slice(0, NL), "ones", c(0, 128, 1, 8), "c192", c(0, NL, 1, 8), 64)],
@@ -282,9 +335,9 @@ def build_ops(cost):
         ts("hm", "pi", 6, A.arith_shift_right, H - 1, A.bitwise_and, lo=k0, hi=k1, name="l")
         cp("hu", "hm", k0, k1, 64, name="l")
         wm = tile()
-        mm(wm, [(slice(0, CH), "ey", al, "rf", c(j0, j1), CH), (slice(0, CH), "c15", c(0, 128, 1, 8), "ones", c(0, CH, 1, 8), CH),
+        mm(wm, [(slice(0, CH), "ey", al, rf, c(j0, j1), CH), (slice(0, CH), "c15", c(0, 128, 1, 8), "ones", c(0, CH, 1, 8), CH),
                 (slice(0, CH), "ni15", al, "nm", c(j0, j1), CH)],
-           [R("ey"), R("c15"), R("ones"), R("ni15"), R("rf", j0, j1), R("nm", j0, j1), R("hm", k0, k1), R("cache")], "wm")
+           [R("ey"), R("c15"), R("ones"), R("ni15"), R(rf, j0, j1), R("nm", j0, j1), R("hm", k0, k1), R("cache")], "wm")
         v(lambda e, B, inc: inc(e.tensor_tensor(out=B("t1")[:, j0:j1], in0=B("cache")[:, D0:D0 + H].indirect(B("hu")[:, k0:k1]), in1=B("nm")[:, j0:j1], op=A.add)),
           [R("cache"), R("hu", k0, k1), R("nm", j0, j1)], [R("t1", j0, j1)], GF * CH, "cache gather")
         tt("r2", wm, "t1", A.max, j0, j1, slo=0, name="r2")
@@ -315,11 +368,20 @@ def build_ops(cost):
         tt("hh", lf, "hm", A.add, 0, 32, name="w")
         pt = tile()
         mm(pt, [(slice(32 * g, 32 * g + 32), "pb", c(128 * g, 128 * g + 128), "hh", c(0, 32), 64, True, True) for g in range(8)], [R("pb"), R("hh")], "h pairs")
-        ts("eqh", pt, 0.0, A.is_equal, hi=256, cyc=256, name="w")
+        for x0 in (0, 8):
+            mm(pt, [y for x in range(x0, x0 + 8) for y in
+                    ((slice(256 + 16 * x, 272 + 16 * x), "pe", c(128 * (x // 2), 128 * (x // 2 + 1)), "hh", c(0, 32, 2), 64, True, False),
+                     (slice(256 + 16 * x, 272 + 16 * x), "po", c(128 * x, 128 * x + 128), "hh", c(1, 32, 2), 64, False, True))],
+               [R("pe"), R("po"), R("hh")], "h pairs")
+        ts("eqh", pt, 0.0, A.is_equal, hi=512, cyc=512, name="w")
         z = tile()
         mm(z, [(slice(0, 32), "vw", c(352 - 16 * g, 480 - 16 * g), "eqh", c(32 * g, 32 * g + 32), 64) for g in range(8)]
-           + [(slice(0, 32), "ey", al, "hh", c(0, 32), 64)], [R("vw"), R("eqh"), R("ey"), R("hh")], "lose")
-        ts("wu", z, float(H + D0), A.add, ("col", CQ), A.max, hi=32, name="w", dview=slice(0, 64, 2))
+           + [((0, slice(0, 2), slice(1, 16, 2)), "lw", c(120 - 8 * x, 248 - 8 * x), "eqh", c(256 + 16 * x, 272 + 16 * x), 64) for x in range(16)]
+           + [(slice(0, 32), "ey", al, "hh", c(0, 32), 64)], [R("vw"), R("lw"), R("eqh"), R("ey"), R("hh")], "lose")
+        for x in (0, 1):
+            v(lambda e, B, inc, x=x: inc(e.tensor_scalar(out=B("wu")[:, x:32:2], in0=B(z, (0, slice(0, 2), slice(x, 16, 2))), scalar1=float(H + D0),
+                                                         scalar2=B("col")[:, CQ + x:CQ + x + 1], op0=A.add, op1=A.max)),
+              [R(z), R("col", CQ, CQ + 2)], [("wu", x, x + 1)], 64, "w")
 
     def phase_d(t, b):
         j0, j1, i0 = b * BL, (b + 1) * BL, 16 + b * KB
@@ -327,69 +389,69 @@ def build_ops(cost):
         maxima("md", "vd", j0, j1, 1)
         maxima("m2", "vd", j0, j1, 2)
         ds = tile()
-        both, lo, hi = (lambda p: slice(p, 256, 16)), (lambda p: slice(p, 128, 16)), (lambda p: slice(128 + p, 256, 16))
-        init = [(slice(0, 256), "nq", c(j0, j1), "nw", c(0, 256), 256), (slice(0, 256), "ones", c(0, 128, 1, 8), "ci", c(0, 256, 1, 8), 256)]
+        s02, n0, last = slice(0, 3, 2), 3 * BL * b + BL, t == RO - 1
         va = []
         for p in range(15):
-            if p % 2 == 0:
-                va += [(both(p), "vd", rows("vd", j0, p + e), "bm", c(0, 16), 64) for e in (0, 1)]
+            if p % 2:
+                va.append(((s02, slice(p - 1, p + 1)), "vd", rows("vd", j0, p), "wo", (ALL, ALL, ALL, ALL), 64))
             else:
-                va += [(lo(p), "vd", rows("vd", j0, p), "bm", c(0, 8), 64), (both(p), "vd", rows("vd", j0, p + 1), "bm", c(0, 16), 64),
-                       (hi(p), "vd", rows("vd", j0, p - 1), "bm", c(0, 8), 64)]
-        rd = [R("vd", 16 * j0, 16 * j1), R("bm")]
-        mm(ds, init, [R("nq", j0, j1), R("yp", j0, j1), R("nw"), R("ones"), R("ci"), R("vd", 16 * j0, 16 * (j0 + KG))], "init d", True, False)
-        for x in range(0, len(va), 13):
-            mm(ds, va[x:x + 13], rd, "sum d", False, False)
-        mm(ds, [((lo, both)[1 - p % 2](p), "md", rows("md", j0, p), "b2", c(0, 16 - 8 * (p % 2)), 64) for p in range(15)],
-           [R("md", 16 * j0, 16 * j1), R("b2")], "sum m", False, False)
-        mm(ds, [(hi(2 * p + 1), "m2", rows("m2", j0, p, 8), "b2", c(0, 8), 64) for p in range(7)], [R("m2", 8 * j0, 8 * j1), R("b2")], "sum m", False, True)
+                lo, hi = max(p - 1, 0), min(p + 2, 15)
+                va.append(((slice(0, 3), slice(lo, hi)), "vd", rows("vd", j0, p), "we", (ALL, ALL, ALL, slice(lo - p + 1, hi - p + 1)), max(64, 24 * (hi - lo))))
+        va.append(((0, 14), "vd", rows("vd", j0, 15), "bm", c(0, 8), 64))
+        mx = [((s02, slice(p, p + 2)), "md", rows("md", j0, p), "wx", (ALL, ALL, ALL, ALL), 64) if p % 2 == 0 and p < 14 else
+              ((0, p), "md", rows("md", j0, p), "b2", c(0, 8), 64) for p in range(15)]
+        mm(ds, [(slice(0, 384), "nq", c(j0, j1), "nw", c(0, 384), 384)], [R("nq", j0, j1), R("yp", j0, j1), R("nw"), R("vd", 16 * j0, 16 * (j0 + KG))], "init d", True, False)
+        mm(ds, va, [R("vd", 16 * j0, 16 * j1), R("bm"), R("we"), R("wo")], "sum d", False, False)
+        mm(ds, mx, [R("md", 16 * j0, 16 * j1), R("b2"), R("wx")], "sum m", False, False)
+        mm(ds, [((1, 2 * p + 1), "m2", rows("m2", j0, p, 8), "b2", c(0, 8), 64) for p in range(7)], [R("m2", 8 * j0, 8 * j1), R("b2")], "sum m", False, True)
         cls[0] = "E%d" % t
-        s(lambda e, B, inc: inc(e.activation(B("sn")[:, i0:i0 + BL], B(ds)[:, 128:256], F.Sign, bias=B("col")[:, CNH:CNH + 1])),
-          [R(ds), R("col", CNH, CNH + 1)], [R("sn", i0, i0 + BL)], BL, "near")
+        s(lambda e, B, inc: inc(e.activation(B("sn")[:, n0 - BL:n0 + 2 * BL], B(ds, slice(0, 384)), F.Sign, bias=B("col")[:, CNH:CNH + 1], scale=-1.0)),
+          [R(ds), R("col", CNH, CNH + 1)], [R("sn", n0 - BL, n0 + 2 * BL)], 3 * BL, "near")
         cls[0] = "S%d" % t
-        scan("kb", slice(i0, i0 + BL), ds, slice(0, BL), "cap", slice(0, BL), 0.0, A.max, A.min, BL, "kb")
+        scan("kb", slice(i0, i0 + BL), "sn", slice(n0 - BL, n0), "cap2", slice(0, BL), 1.0, A.min, A.max, BL / 2, "kb")
         cls[0] = "E%d" % t
         nt = tile()
-        mm(nt, turn(0, BL, "sn", i0, "ey", True, False) + turn(0, BL, "sn", i0 - 1, "ey", False, True), [R("sn", i0 - 1, i0 + BL), R("ey")], "near")
+        mm(nt, [(slice(0, BL), "ones", c(0, 128, 1, 8), "cm8", c(0, BL, 1, 8), BL, True, False)] + turn(0, BL, "sn", n0, "hey", False, False)
+           + turn(0, BL, "sn", n0 + BL, "hey", False, True), [R("sn", n0, n0 + 2 * BL), R("hey"), R("ones"), R("cm8")], "near")
         tt("t5", nt, "yp", A.mult, j0, j1, slo=0, name="t5")
         rt = tile()
-        mm(rt, [(slice(0, BL), "tro", al, "yp", c(j0, j1), 4 * BL)], [R("tro"), R("yp", j0, j1), R("sn", i0, i0 + BL)], "rn", True, False)
-        mm(rt, [(slice(0, BL), "ioh", al, "t5", c(j0, j1), 4 * BL)], [R("ioh"), R("t5", j0, j1)], "rn", False, True)
-        if t == RO - 1:
-            s(lambda e, B, inc: inc(e.activation(B("yrs")[:, j0:j1], B(rt)[:, 0:BL], F.Identity, bias=B("col")[:, CSH:CSH + 1])),
-              [R(rt), R("col", CSH, CSH + 1)], [R("yrs", j0, j1)], BL, "rn")
+        whole = [(slice(0, BL), "tri", al, "yp", c(j0, j1), 4 * BL)]
+        if last:
+            whole.append((slice(0, BL), "ones", c(0, 128, 1, 8), "c192", c(0, BL, 1, 8), BL))
+        mm(rt, whole, [R("tri"), R("ones"), R("c192"), R("yp", j0, j1), R("sn", n0, n0 + 2 * BL)], "rn")
+        tt("yrs" if last else "rn%d" % t, rt, "t5", A.add, j0, j1, slo=0, name="rn")
+        if last:
             op("Y", lambda e, B, inc: inc(e.dma_start(B("IN")["yr"][:, j0:j1], B("yrs")[:, j0:j1])), [R("yrs", j0, j1)], [("yr", j0, j1)], 2.5, "store yr", sem="oy%d" % b)
         else:
             out = "rn%d" % t
-            ts(out, rt, float(SH), A.add, lo=j0, hi=j1, cyc=BL, slo=0, name="rn")
             op("G", ("send", t, j0, j1), [R(out, j0, j1)], [], 1.0, "send", sem="ls%d_%d" % (t + 1, b))
             ops[-1]["sem2"] = "ar%d_%d" % (t + 1, b)
-            op("N", None, [R(out, j0, j1)], [R("ru%d" % (t + 1), j0, j1)], cost["HOP"], "arrive", sem="ar%d_%d" % (t + 1, b))
+            op("N", None, [R(out, j0, j1)], [R("rf%d" % (t + 1), j0, j1)], cost["HOP"], "arrive", sem="ar%d_%d" % (t + 1, b))
             ops[-1]["after"] = len(ops) - 2
         cls[0] = "S%d" % t
         at = tile()
-        mm(at, turn(0, BL, "kb", i0 - 1, "ney"), [R("kb", i0 - 1, i0 + BL), R("ney")], "a2")
+        mm(at, turn(0, BL, "kb", i0 - 1, "ey"), [R("kb", i0 - 1, i0 + BL), R("ey")], "a2")
         tt("y2", at, "yp", A.mult, j0, j1, slo=0, name="y2")
         sk = tile()
-        mm(sk, [(slice(0, BL), "tri", al, "yp", c(j0, j1), 4 * BL)], [R("tri"), R("yp", j0, j1), R("kb", i0, i0 + BL)], "st", True, False)
-        mm(sk, [(slice(0, BL), "t15", al, "y2", c(j0, j1), 4 * BL)], [R("t15"), R("y2", j0, j1)], "st", False, True)
-        s(lambda e, B, inc: inc(e.activation(B("st")[:, j0:j1], B(sk)[:, 0:BL], F.Identity, bias=B("col")[:, CSH:CSH + 1])),
+        mm(sk, [(slice(0, BL), "e15", al, "r2", c(j0, j1), BL), (slice(0, BL), "t15", al, "y2", c(j0, j1), 4 * BL)],
+           [R("t15"), R("e15"), R("r2", j0, j1), R("y2", j0, j1)], "st")
+        s(lambda e, B, inc: inc(e.activation(B("st")[:, j0:j1], B(sk, slice(0, BL)), F.Identity, bias=B("col")[:, CSH:CSH + 1])),
           [R(sk), R("col", CSH, CSH + 1)], [R("st", j0, j1)], BL, "st")
-        for k in range(j1 // 16 - 1, j0 // 16 - 1, -1):
-            op("V", lambda e, B, inc, k=k: inc(e.tensor_copy(out=B("cache")[:, 0:D0 + H].indirect(B("wu")[:, 2 * k:2 * k + 1]), in_=B("st")[:, 16 * k:16 * k + 16])),
-               [R("wu"), R("st", j0, j1)], [R("cache")], 0.05 + max(cost["SCF"] * 16, 64) * CYC, "scatter")
+        for k in range(j1 // 16 - 2, j0 // 16 - 1, -2):
+            op("V", lambda e, B, inc, k=k: inc(e.tensor_copy(out=B("cache")[:, 0:D0 + H].indirect(B("wu")[:, k:k + 2]), in_=B("st")[:, 16 * k:16 * k + 32])),
+               [R("wu"), R("st", j0, j1)], [R("cache")], 0.05 + cost["SCF"] * 32 * CYC, "scatter")
 
     for t in range(RO):
         for ch in range(NC - 1, -1, -1):
-            cls[0] = "A%d" % t
+            cls[0], cls[1] = "A%d" % t, NC - 1 - ch
             phase_a(t, ch)
         for ch in range(NC - 1, -1, -1):
-            cls[0] = "B%d" % t
+            cls[0], cls[1] = "B%d" % t, NC - 1 - ch
             phase_b(t, ch)
-        cls[0] = "W%d" % t
+        cls[0], cls[1] = "W%d" % t, 0
         winners(t)
         for b in range(NB - 1, -1, -1):
-            cls[0] = "D%d" % t
+            cls[0], cls[1] = "D%d" % t, NB - 1 - b
             phase_d(t, b)
     op("Y", lambda e, B, inc: inc(e.dma_start(B("IN")["yc"][:, :], B("cache")[:, D0:D0 + H])), [R("cache")], [("yc", 0, H)], 3.5, "store yc", sem="oc")
     return ops, tiles
@@ -443,7 +505,9 @@ def schedule(cost=COST, bias=BIAS):
     for i in range(n - 1, -1, -1):
         rank[i] = ops[i]["dur"] + max([rank[j] + LAT for j in succ[i]] or [0.0])
     for i in range(n):
-        rank[i] += bias.get(ops[i]["cls"], bias.get(ops[i]["cls"][0], 0.0))
+        k = ops[i]["cls"]
+        rank[i] += bias.get(k, 0.0) + bias.get(k[0], 0.0) + bias.get(k[0] + "+", 0.0) * ops[i]["part"] + bias.get(ops[i]["name"], 0.0)
+    rank = bias.get("rank", rank)
     free = {q: 0.0 for q in "VSTGYAN"}
     pool = {"p%d" % i: 0.0 for i in range(NPS)}
     endt, order, est = [0.0] * n, [], {}
@@ -464,7 +528,8 @@ def schedule(cost=COST, bias=BIAS):
                 cands.append((max(e0, free[q] if q != "N" else 0.0), -rank[i], i, q))
         assert cands, "no operation can go on"
         t0 = min(x[0] for x in cands)
-        st, _, i, q = min([x for x in cands if x[0] <= t0 + 0.03], key=lambda x: (x[1], x[0]))
+        q0 = min(cands)[3]
+        st, _, i, q = min([x for x in cands if x[3] == q0 and x[0] <= t0 + 0.01 * bias.get("wait" + q0, 3)], key=lambda x: (x[1], x[0]))
         o = ops[i]
         o["q"] = q
         for b, lo, hi in o["w"]:
@@ -494,12 +559,51 @@ def schedule(cost=COST, bias=BIAS):
     return [ops[i] for i in order], tiles, max(endt)
 
 
+def backward(seq, cost):
+    n, ops = len(seq), sorted(seq, key=lambda o: o["id"])
+    dep = deps_of(ops, lambda b: b, lambda b: isinstance(b, tuple))
+    later, left = [[] for _ in range(n)], [0] * n
+    for i in range(n):
+        for d, kk in dep[i].items():
+            later[d].append((i, 0.0 if free_of_wait(ops[i], ops[d], kk) else cost["LAT"]))
+            left[d] += 1
+    free, end, est = {q: 0.0 for q in "VSTGYAN"}, [0.0] * n, {}
+    ready = [i for i in range(n) if left[i] == 0]
+    while ready:
+        cands = []
+        for i in ready:
+            if i not in est:
+                est[i] = max([end[j] + w for j, w in later[i]] or [0.0])
+            q = ops[i]["q"]
+            cands.append((est[i] if q in "NYA" else max(est[i], free[q]), -ops[i]["t1"], i, q))
+        m = min(cands)
+        st, _, i, q = min([x for x in cands if x[3] == m[3] and x[0] <= m[0] + 0.03], key=lambda x: (x[1], x[0]))
+        end[i] = free[q] = st + ops[i]["dur"]
+        ready.remove(i)
+        for d in dep[i]:
+            left[d] -= 1
+            if left[d] == 0:
+                ready.append(d)
+    return end
+
+
+def best_order(cost=COST, passes=6):
+    bias, best = BIAS, None
+    for _ in range(passes):
+        got = schedule(cost, bias)
+        if best is None or got[2] < best[2]:
+            best = got
+        rank = backward(got[0], cost)
+        bias = dict(WAIT, rank=[rank[o["id"]] + URGENT.get(o["name"], 0.0) for o in sorted(got[0], key=lambda o: o["id"])])
+    return best
+
+
 PLAN = {}
 
 
 def plan():
     if not PLAN:
-        seq, tiles, end = schedule()
+        seq, tiles, end = best_order()
         key = lambda b: tiles[b[1]]["buf"] if isinstance(b, tuple) else b
         PLAN["seq"], PLAN["tiles"] = seq, tiles
         PLAN["dep"] = deps_of(seq, key, lambda b: isinstance(b, tuple))
@@ -522,11 +626,13 @@ def rank_program(g, core, T, topo):
     ins = {"x": T.x, "r0": T.r0, "c0": T.c0, "yc": T.yc, "yr": T.yr}
     cur = ["V"]
 
-    def B(name):
+    def B(name, cols=None):
         if name == "Q":
             return cur[0]
         if name == "IN":
             return ins
+        if cols is not None:
+            return B(name)[bank_view(cols) if isinstance(name, tuple) else (slice(0, 128), cols)]
         return T[tiles[name[1]]["buf"]] if isinstance(name, tuple) else T[name]
 
     cnt = {"V": 0, "S": 0, "T": 0, "G": 0}
@@ -562,7 +668,7 @@ def rank_program(g, core, T, topo):
         cur[0] = q
         if isinstance(o["fn"], tuple):
             _, t, j0, j1 = o["fn"]
-            g.remote_dma(T["ru%d" % (t + 1)][:, j0:j1], T["rn%d" % t][:, j0:j1], T.sem[o["sem2"]], T.sem[o["sem"]], pid, rid, emask)
+            g.remote_dma(T["rf%d" % (t + 1)][:, j0:j1], T["rn%d" % t][:, j0:j1], T.sem[o["sem2"]], T.sem[o["sem"]], pid, rid, emask)
             done[o["id"]] = (o["sem"], ne, {})
             pend[o["sem"]] = ne
         elif o["sem"]:

@@ -1,16 +1,20 @@
+import math
+import numpy as np
 from concourse.mybir import AluOpType as A, ActivationFunctionType as F, AxisListType as AX
 
 W, H, P, RO, ST = 3072, 1024, 512, 3, 2
 SH = 1536
 CH = 256
-NC = P // CH
-NL = CH // 16
+PARTS = [(128, 128, 256), (256, 256), (256, 256)]
+LOOPS = PARTS
+DISTS = [(128, 128, 128, 128)] * RO
+SENDS = [(128, 128, 128, 128)] * RO
+COPIES = [(256, 256), (256, 256), (256, 128, 128)]
 BL = 128
 NB = P // BL
 KG = 32
-SC = 128
 D0 = 32
-KA, KB = CH + 16, BL + 16
+KA = CH + 16
 
 SCRATCH = {}
 
@@ -20,20 +24,21 @@ def bufs(dtype, **sizes):
         SCRATCH[k] = ("sbuf", [128, sizes[k]], dtype)
 
 
-bufs("bfloat16", xs=W, va=16 * P, vd=16 * P, mx=16 * P, md=16 * P, m2=8 * P, ka=NC * KA, kb=NB * KB, sn=3 * P, sa=P, nm=P, nq=P,
+bufs("bfloat16", xs=W, va=16 * P, vd=16 * P, mx=16 * P, md=16 * P, m2=8 * P, ka=NB * KA, kb=NB * KA, sa=P, nm=P, nq=P,
      eqp=8 * P, eqh=512)
 bufs("float16", rf0=P, rf1=P, rf2=P, rn0=P, rn1=P, indr=P, r2=P, hh=32)
 bufs("uint16", ru=P, r2u=P, hu=32, wu=32)
 bufs("int32", r0i=P, c0i=H, pi=32, hm=32, ki=8, kp=8, ks=8, kt=8, ia=256, ib=256)
-bufs("float32", cache=D0 + H, t1=P, yp=P, y2=P, t5=P, st=P, yrs=P, r15=32, pri=32, kacc=8, kcol=8, col=16, rio=16, fa=16, fb=16, fc=16,
+bufs("float32", cache=D0 + H, t1=P, yp=P, y2=P, t5=P, st=P, yrs=P, r150=32, r151=32, r152=32, eyf=128, pri=32, kacc=16, kcol=8, col=16, rio=16, fa=16, fb=16, fc=16,
      onesf=128, tri=128, tra=128, t15=128, kw=128, bmf=8)
-bufs("bfloat16", ones=CH, zero=2048, pe=1024, po=2048, lw=248, lwa=8, ey=128, ney=128, hey=128, e15=128, cap2=128, b2=8, b2a=8, bm=8, bma=8, cm8=128, ca=CH, nw=384, cap=CH, ms=432, c192=128,
+bufs("bfloat16", ones=CH, zero=512, pe=1024, po=2048, lw=248, lwa=8, ey=128, ney=128, hey=128, e15=128, cap2=CH, b2=8, b2a=8, bm=8, bma=8, nw=384, cap=CH, ms=432, c192=16,
      ni15=128, c15=128, pq=256, pd=128, pb=1024, vw=480, dl=128)
 NPS = 8
 for _i in range(NPS):
     SCRATCH["p%d" % _i] = ("psum", [128, 4, 8, 16], "float32")
+SCRATCH["sn"] = ("sbuf", [128, 3, P], "bfloat16")
 SCRATCH["we"] = ("sbuf", [128, 3, 8, 3], "bfloat16")
-SCRATCH["wo"] = ("sbuf", [128, 2, 8, 2], "bfloat16")
+SCRATCH["wo"] = ("sbuf", [128, 3, 8, 2], "bfloat16")
 SCRATCH["wx"] = ("sbuf", [128, 2, 8, 2], "bfloat16")
 ALL = slice(None)
 
@@ -49,18 +54,25 @@ def bank_view(w):
     return (ALL, a // 128, a % 128 // 16, slice(a % 16, (b - 1) % 16 + 1))
 
 
-SEMAPHORES = (["qV", "qS", "qT", "qG", "lr", "lq", "lx", "lc", "oc"] + ["oy%d" % b for b in range(NB)]
+SEMAPHORES = (["qV", "qS", "qT", "qG", "lr", "lx", "ad1", "ad2", "ld1", "ld2", "lc", "oc"] + ["oy%d" % b for b in range(NB)]
               + ["ar%d_%d" % (t, b) for t in range(1, RO) for b in range(NB)]
               + ["ls%d_%d" % (t, b) for t in range(1, RO) for b in range(NB)])
 
-COST = {"CYC": 0.00083, "TCYC": 0.00042, "LAT": 0.12, "GF": 1.56, "SCF": 3.8, "HOP": 3.5}
-BIAS = {"load x": 99}
-URGENT = dict({"load x": 99}, **{k: 50 for k in ("bad", "nm", "st", "near")},
-              **{k: 3 for k in ("ka", "indr", "l", "cache gather", "r2", "r2u", "ru", "t5", "rn")})
-WAIT = {}
-QBAD = "S"
-VG = {"A0", "A1", "A2"}
-CQ, CQ2, CLO, CHI, CSC, CBI, CNH, CW, C15, CSH = range(10)
+COST = {"CYC": 0.00083, "TCYC": 0.00042, "LAT": 0.12, "GF": 1.56, "SCF": 3.8, "HOP": 3.0, "LX": 4.3, "SEND": 1.0}
+BIAS = {'beat': 143, 'gap': 12, 'wait': 8, 'B0': 60, 'B1': 161, 'B2': 34, 'S3': 79, 'sum a': 54, 'S2': -35, 'w': 46, 'D0': -4, 'E1': -21, 'sum d': 30,
+        'sum m': -12, 'E2': 250, 'A1': -15, 'R0': -16, 'S1': 22, 'loop': 160, 'P2': 9, 'A0': -16, 'pairs': -3, 'A2': -203, 'scatter': 26, 'E0': 51,
+        'eq': -14, 'max2': 8, 'D2': -15, 'P0': 9, 'C0': -72, 'gather': 1, 'l': -53, 'D3': -44, 'max1': 1, 'S0': -5, 'D1': 1, 'ru': -12, 'P1': 4,
+        'W0': 6, 'E3': -2}
+STEPS = 36000
+CASES = [{}, {"GF": 1.08, "SCF": 2.2, "HOP": 2.5, "LX": 3.6}, {"GF": 1.25, "SCF": 4.0, "HOP": 3.8, "SEND": 1.3}]
+KGS = {"D1": 64, "D2": 64, "A1": 64}
+VG = {"A0": (0, 1, 4, 8), "A1": (4,), "A2": (4,)}
+CQ, CQ2, CLO, CHI, CSC, CBI, CNH, CW, C15, CSH, CTH = range(11)
+
+
+def spans(sizes):
+    ends = [P - sum(sizes[:i]) for i in range(len(sizes) + 1)]
+    return list(zip(ends[1:], ends[:-1]))
 
 
 def build_ops(cost):
@@ -86,7 +98,7 @@ def build_ops(cost):
         op("S", fn, reads, writes, 0.065 + CYC * max(cyc, 64), name)
 
     def gp(fn, reads, writes, n, name=""):
-        op("G", fn, reads, writes, 0.17 + 2 * CYC * n, name)
+        op("G", fn, reads, writes, (0.17 * CYC / 0.00083 + 2 * CYC * n) * cost.get("GX", 1.0), name)
 
     def mm(out, terms, reads, name, first=True, last=True):
         def fn(e, B, inc):
@@ -126,10 +138,9 @@ def build_ops(cost):
         v(lambda e, B, inc: inc(e.tensor_tensor_scan(B(dst)[:, dv], B(a, av), B(b)[:, bv], init, o0, o1)),
           [rng(a, av), rng(b, bv)], [rng(dst, dv)], cyc, name)
 
-    op("A", lambda e, B, inc: inc(e.dma_start(B("r0i")[:, CH:P], B("IN")["r0"][:, CH:P])), [], [R("r0i", CH, P)], 2.5, "load r0", sem="lr")
-    op("Y", lambda e, B, inc: inc(e.dma_start(B("xs")[:, :], B("IN")["x"][:, :])), [], [R("xs")], 5.0, "load x", sem="lx")
-    op("Y", lambda e, B, inc: inc(e.dma_start(B("r0i")[:, 0:CH], B("IN")["r0"][:, 0:CH])), [], [R("r0i", 0, CH)], 5.4, "load r0", sem="lq")
-    op("Y", lambda e, B, inc: inc(e.dma_start(B("c0i")[:, :], B("IN")["c0"][:, :])), [], [R("c0i")], 7.0, "load c0", sem="lc")
+    op("A", lambda e, B, inc: inc(e.dma_start(B("r0i")[:, :], B("IN")["r0"][:, :])), [], [R("r0i")], 0.55 * cost["LX"], "load r0", sem="lr")
+    op("Y", lambda e, B, inc: inc(e.dma_start(B("xs")[:, :], B("IN")["x"][:, :])), [], [R("xs")], cost["LX"], "load x", sem="lx")
+    op("Y", lambda e, B, inc: inc(e.dma_start(B("c0i")[:, :], B("IN")["c0"][:, :])), [], [R("c0i")], 1.4 * cost["LX"], "load c0", sem="lc")
 
     def fill(buf, val, lo=0, hi=None, st=1):
         hi = SCRATCH[buf][1][1] if hi is None else hi
@@ -147,13 +158,13 @@ def build_ops(cost):
         w = slice(0, n) if view is None else view
         u = w if sview is None else sview
         gp(lambda e, B, inc: inc(e.affine_select(out=B(dst)[:, w], in_=B(src)[:, u], pattern=pat, compare_op=cmp, fill=fillv, base=base, channel_multiplier=cm)),
-           [R(src, u.start, u.stop)], [R(dst)], n, "sel " + dst)
+           [R(src, u.start, u.stop)], [R(dst, w.start, w.stop)], n, "sel " + dst)
 
     def iota(dst, lo, hi, pat, base, cm, flt=False):
         if flt:
-            gp(lambda e, B, inc: inc(e.iota(B(dst)[:, lo:hi], pat, base, cm, allow_small_or_imprecise_dtypes=True)), [], [R(dst, lo, hi)], hi - lo, "iota")
+            gp(lambda e, B, inc: inc(e.iota(B(dst)[:, lo:hi], pat, base, cm, allow_small_or_imprecise_dtypes=True)), [], [R(dst, lo, hi)], hi - lo, "iota0")
         else:
-            gp(lambda e, B, inc: inc(e.iota(B(dst)[:, lo:hi], pat, base, cm)), [], [R(dst, lo, hi)], hi - lo, "iota")
+            gp(lambda e, B, inc: inc(e.iota(B(dst)[:, lo:hi], pat, base, cm)), [], [R(dst, lo, hi)], hi - lo, "iota0")
 
     def weights(dst, parts):
         for x, y, src in parts:
@@ -162,18 +173,19 @@ def build_ops(cost):
                [R(src, 0, 8)], [(dst, 3 * x + y, 3 * x + y + 1)], 8, "sel " + dst)
 
     NE, GE = A.not_equal, A.is_ge
-    fill("zero", 0.0, 0, 512)
+    fill("zero", 0.0)
     fill("ones", 1.0)
-    fill("zero", 0.0, 512)
     for a, z, val in (("bma", "bm", -1.0), ("b2a", "b2", 2.0)):
         sel(a, "zero", [[16, 8]], A.is_gt, val, 0, -1)
         sel(z, a, [[16, 8]], GE, 0.0, 15, -1)
+    for x in ("wo", "we", "wx"):
+        v(lambda e, B, inc, x=x: inc(e.memset(B(x)[:, :, :, :], 0.0)), [], [R(x)], 64, "fill")
     weights("wo", [(0, 0, "bm"), (0, 1, "bm")])
-    sfill("ca", -5.0)
+    sfill("col", -40.5, CTH, CTH + 1)
     sel("cap", "ones", [[0, CH // 16], [1, 16]], NE, 0.0, -15, 0)
     sel("ey", "zero", [[-1, 128]], NE, 1.0, 0, 1)
     sel("ney", "zero", [[-1, 128]], NE, -1.0, 0, 1)
-    sfill("ka", 0.0, 15, NC * KA, KA)
+    sfill("ka", 0.0, 15, NB * KA, KA)
     sfill("ms", 0.0)
     w8 = slice(0, 8)
     sel("b2a", "ones", [[-16, 8]], GE, 0.0, 0, 1)
@@ -183,17 +195,18 @@ def build_ops(cost):
     sfill("c192", SH / 8.0)
     iota("ki", 0, 1, [[0, 1]], 0, 1)
     iota("rio", 0, 16, [[1, 16]], 0, 0, True)
-    sel("ni15", "ney", [[0, 8], [1, 16]], NE, 0.0, -15, 0)
+    sel("c15", "ney", [[-16, 8], [0, 16]], NE, 1.0, 0, 1)
+    sel("c15", "zero", [[0, 8]], GE, 0.0, 0, 0, slice(0, 128, 16), w8)
+    sel("ni15", "c15", [[0, 8], [1, 16]], NE, 0.0, -15, 0)
     ts("kp", "ki", 15, A.bitwise_and)
     cp("col", "kp", CQ, CQ + 1, 64, slo=0)
     ts("col", "kp", 15.0, A.is_equal, lo=C15, hi=C15 + 1, slo=0)
     ts("col", "col", 10240.0, A.mult, 6144.0, A.add, lo=CSC, hi=CSC + 1, slo=C15)
     ts("col", "col", -16896.0, A.mult, -7680.0, A.add, lo=CBI, hi=CBI + 1, slo=C15)
     ts("col", "kp", 16.0, A.add, lo=CQ2, hi=CQ2 + 1, slo=0)
-    sfill("c15", -960.0)
-    sfill("c15", 0.0, 15, 128, 16)
     sfill("cache", 0.0, 0, D0)
-    cp("cache", "c0i", D0, D0 + H, H, slo=0)
+    gp(lambda e, B, inc: inc(e.affine_select(out=B("cache")[:, D0:D0 + H], in_=B("c0i")[:, 0:H], pattern=[[0, H]], compare_op=GE, fill=0.0, base=0,
+                                             channel_multiplier=0)), [R("c0i")], [R("cache", D0, D0 + H)], H, "cache")
     cls[0] = "K0"
     iota("ia", 0, 128, [[0, 8], [1, 16]], 128, -1)
     iota("ia", 128, 256, [[1, 8], [1, 16]], 129, -1)
@@ -227,31 +240,35 @@ def build_ops(cost):
     sel("nw", "nw", [[-2, 64]], NE, -256.0, -2, 1, slice(129, 256, 2))
     sel("nw", "nw", [[-2, 64]], NE, 256.0, -2, 1, slice(257, 384, 2))
     sel("nw", "nw", [[-16, 8], [0, 8]], NE, -40.0, 0, 1, slice(257, 384, 2))
-    sel("nw", "zero", [[0, 2], [-16, 8]], NE, 216.0, 0, 1, slice(143, 384, 16), slice(0, 16))
-    weights("wo", [(1, 0, "zero"), (1, 1, "bm")])
-    weights("we", [(x, y, "bm" if k else "zero") for x, ks in enumerate(((1, 1, 0), (1, 0, 1), (0, 0, 1))) for y, k in enumerate(ks)])
-    weights("wx", [(x, y, "b2" if x == y else "zero") for x in (0, 1) for y in (0, 1)])
+    sel("nw", "zero", [[0, 2], [-16, 8]], NE, 512.0, 0, 1, slice(143, 384, 16), slice(0, 16))
+    weights("wo", [(2, 1, "bm")])
+    weights("we", [(x, y, "bm") for x, y in ((0, 0), (0, 1), (1, 0), (1, 2), (2, 2))])
+    weights("wx", [(x, x, "b2") for x in (0, 1)])
     sel("hey", "zero", [[-1, 128]], NE, -0.5, 0, 1)
+    sel("cap2", "zero", [[0, CH // 16], [1, 16]], NE, 1.0, -15, 0)
     sel("e15", "ey", [[0, 8], [1, 16]], A.is_equal, 0.0, -15, 0)
-    sel("cap2", "zero", [[0, 8], [1, 16]], NE, 1.0, -15, 0)
-    sfill("cm8", -0.125)
-    sfill("kb", 1.0, 15, NB * KB, KB)
+    sfill("kb", 1.0, 15, NB * KA, KA)
     sfill("col", 0.5, CNH, CNH + 1)
     sfill("col", float(SH), CSH, CSH + 1)
-    sel("pe", "zero", [[-16, 8], [0, 8], [-1, 16]], NE, 1.0, 0, 1)
-    sel("po", "zero", [[-1, 128], [0, 16]], NE, -1.0, 0, 1)
+    for x in range(2):
+        sel("pe", "zero", [[-16, 4], [0, 8], [-1, 16]], NE, 1.0, -64 * x, 1, slice(512 * x, 512 * x + 512), slice(0, 512))
+    for x in range(4):
+        sel("po", "zero", [[-1, 32], [0, 16]], NE, -1.0, -32 * x, 1, slice(512 * x, 512 * x + 512), slice(0, 512))
     sfill("lw", 0.0)
     sel("lwa", "zero", [[16, 8]], A.is_gt, -4096.0, 0, -1)
     sel("lw", "lwa", [[16, 8]], GE, 0.0, 15, -1, slice(120, 128), w8)
     iota("onesf", 0, 128, [[0, 128]], 1, 0, True)
-    sel("tra", "onesf", [[1, 128]], GE, 0.0, 0, -1)
-    sel("tri", "tra", [[-16, 8], [0, 16]], GE, 0.0, 0, 1)
-    sel("t15", "tri", [[0, 8], [1, 16]], NE, 0.0, -15, 0)
+    sel("tri", "onesf", [[1, 128]], GE, 0.0, 0, -1)
+    sel("tra", "tri", [[-16, 8], [0, 16]], GE, 0.0, 0, 1)
+    sel("tri", "tra", [[-1, 128]], NE, 0.0, 0, 1)
+    sel("eyf", "onesf", [[-1, 128]], A.is_equal, 0.0, 0, 1)
+    sel("t15", "tra", [[0, 8], [1, 16]], NE, 0.0, -15, 0)
     ts("kw", "onesf", ("col", C15), A.mult, 1.0 / 256, A.mult, hi=128, cyc=128)
 
     al = c(0, 128)
 
     def gather(vb, off, j0, j1):
+        KG = KGS.get(cls[0][0] + str(cls[1]), 32)
         for j in range(j0, j1, KG):
             def fn(e, B, inc, j=j):
                 o, w = B(vb)[:, 16 * j:16 * (j + KG)], B("xs")[:, 0:W].indirect(B(off)[:, j:j + KG])
@@ -259,12 +276,11 @@ def build_ops(cost):
                     inc(e.tensor_copy(out=o, in_=w))
                 else:
                     inc(e.activation(o, w, F.Copy))
-            op("SV" if cls[0] in VG else "S", fn, [R("xs"), R(off, j, j + KG)], [R(vb, 16 * j, 16 * (j + KG))], 0.065 + GF * CYC * 16 * KG, "gather")
+            op("V" if (P - KG - j) // 32 in VG.get(cls[0], ()) else "S", fn, [R("xs"), R(off, j, j + KG)], [R(vb, 16 * j, 16 * (j + KG))], 0.065 + GF * CYC * 16 * KG, "gather")
 
     def maxima(dst, vb, j0, j1, d):
-        for j in range(j0, j1, SC):
-            lo, hi = 16 * j, 16 * (j + SC)
-            scan(dst, slice(lo // d, hi // d - 1), vb, slice(lo, hi - d, d), vb, slice(lo + d, hi, d), 16.0, A.min, A.max, 8 * SC / d, "max%d" % d)
+        lo, hi = 16 * j0, 16 * j1
+        scan(dst, slice(lo // d, hi // d - 1), vb, slice(lo, hi - d, d), vb, slice(lo + d, hi, d), 16.0, A.min, A.max, 8 * (j1 - j0) / d, "max%d" % d)
 
     def rows(buf, j, p, k=16):
         return c(k * j + p, k * (j + BL), k)
@@ -272,50 +288,50 @@ def build_ops(cost):
     def lists(out, o0, n, m0, src, j0, j1):
         return [(slice(o0, o0 + n), "ms", c(m0 + 15 - q, m0 + 143 - q), src, c(j0 + q, j1, 16), 64) for q in range(16)]
 
-    def phase_a(t, ch):
-        j0, j1, rf, i0 = ch * CH, (ch + 1) * CH, "rf%d" % t, 16 + ch * KA
+    def phase_a(t, ch, j0, j1):
+        CH, NL, rf, i0 = j1 - j0, (j1 - j0) // 16, "rf%d" % t, 16 + ch * KA
         ds = tile()
         first = True
         for j in range(j1 - BL, j0 - 1, -BL):
-            if t == 0:
-                cp("ru", "r0i", j, j + BL, BL, name="ru")
-                ts(rf, "ru", float(-SH), A.add, lo=j, hi=j + BL, cyc=BL / 2, name="rf")
-            else:
-                ts("ru", rf, float(SH), A.add, lo=j, hi=j + BL, cyc=BL / 2, name="ru")
             gather("va", "ru", j, j + BL)
             maxima("mx", "va", j, j + BL, 1)
             x = (j - j0) // BL
-            va = [((x, slice(max(p - 1, 0), min(p + 1, 15))), "va", rows("va", j, p), "wo", (ALL, 0, ALL, slice(0, 1 + (0 < p < 15))), 64) for p in range(16)]
-            init = [(slice(0, CH), "ones", c(0, 128, 1, 8), "ca", c(0, CH, 1, 8), CH)] if first else []
-            mm(ds, init + va, [R("va", 16 * j, 16 * (j + BL)), ("wo", 0, 2), R("ones"), R("ca")], "sum a", first, False)
+            va = [((x, slice(max(p - 1, 0), p + 1)), "va", rows("va", j, p), "wo", (ALL, 0, ALL, slice(0, 1 + (p > 0))), 64)
+                  for p in list(range(1, 16, 2)) + list(range(0, 16, 2))]
+            mm(ds, va, [R("va", 16 * j, 16 * (j + BL)), ("wo", 0, 2)], "sum a", first, False)
             mm(ds, [((x, p), "mx", rows("mx", j, p), "b2", c(0, 8), 64) for p in range(15)], [R("mx", 16 * j, 16 * (j + BL)), R("b2")], "sum m", False, j == j0)
             first = False
-
-        def bad(e, B, inc):
-            if B("Q") == "S":
-                inc(e.activation(B("sa")[:, j0:j1], B(ds, slice(0, CH)), F.Sign))
-            else:
-                inc(e.tensor_scalar(out=B("sa")[:, j0:j1], in0=B(ds, slice(0, CH)), scalar1=0.0, scalar2=None, op0=A.is_gt))
-        op(QBAD, bad, [R(ds)], [R("sa", j0, j1)], 0.06 + CYC * CH, "bad")
+        s(lambda e, B, inc: inc(e.activation(B("sa")[:, j0:j1], B(ds, slice(0, CH)), F.Sign, bias=B("col")[:, CTH:CTH + 1])),
+          [R(ds), R("col", CTH, CTH + 1)], [R("sa", j0, j1)], CH, "bad")
         scan("ka", slice(i0, i0 + CH), "sa", slice(j0, j1), "cap", slice(0, CH), 0.0, A.max, A.min, CH / 2, "ka")
-        cls[0] = "R%d" % t
-        l15 = tile()
-        mm(l15, lists(l15, 0, NL, 144, rf, j0, j1), [R("ms"), R(rf, j0, j1)], "r15")
-        ts("r15", l15, float(SH + 64), A.add, lo=ch * NL, hi=(ch + 1) * NL, slo=0, name="r15")
+
+    def send(src, dst, j0, j1, gone, come):
+        op("G", ("send", src, dst, j0, j1), [R(src, j0, j1)], [], cost["SEND"], "send", sem=gone)
+        ops[-1]["sem2"] = come
+        op("N", None, [R(src, j0, j1)], [R(dst, j0, j1)], cost["HOP"], "arrive", sem=come)
+        ops[-1]["after"] = len(ops) - 2
+
+    def ends(t):
+        if t == 0:
+            l15 = tile()
+            mm(l15, lists(l15, 0, 32, 144, "rf0", 0, P), [R("ms"), R("rf0")], "r15")
+            ts("r150", l15, float(SH + 64), A.add, hi=32, name="r15")
+        if t < RO - 1:
+            send("r15%d" % t, "r15%d" % (t + 1), 0, 32, "ld%d" % (t + 1), "ad%d" % (t + 1))
 
     def turn(o0, n, buf, i0, m, start=True, stop=True):
         return [(slice(o0 + x, o0 + x + 128), buf, c(i0 + x, i0 + x + 128), m, al, 128, start, stop) for x in range(0, n, 128)]
 
-    def phase_b(t, ch):
-        j0, j1, k0, k1, i0 = ch * CH, (ch + 1) * CH, ch * NL, (ch + 1) * NL, 16 + ch * KA
-        kr, rf = [R("ka", i0 - 1, i0 + CH), R("ey"), R("ney")], "rf%d" % t
+    def phase_b(t, ch, j0, j1):
+        CH, NL, k0, k1, i0 = j1 - j0, (j1 - j0) // 16, j0 // 16, j1 // 16, 16 + ch * KA
+        kr, rf, r15 = [R("ka", i0 - 1, i0 + CH), R("ey"), R("ney")], "rf%d" % t, "r15%d" % t
         qt = tile()
         a, b = turn(0, CH, "ka", i0, "ey", True, False), turn(0, CH, "ka", i0 - 1, "ney", False, True)
         mm(qt, [x for ab in zip(a, b) for x in ab], kr + [R(rf, j0, j1)], "ind")
         tt("indr", qt, rf, A.mult, j0, j1, slo=0, name="indr")
         qa = tile()
         mm(qa, turn(0, CH, "ka", i0 - 1, "ey"), kr, "a")
-        kc = t * NC + ch
+        kc = t * NB + ch
 
         def fnm(e, B, inc):
             sc, bi = B("col")[:, CSC:CSC + 1], B("col")[:, CBI:CBI + 1]
@@ -326,23 +342,24 @@ def build_ops(cost):
         s(fnm, [R(qa), R("col", CSC, CBI + 1)], [R("nm", j0, j1), R("kacc", kc, kc + 1)], CH + 24, "nm")
         ll = tile()
         mm(ll, lists(ll, 0, NL, 0, "indr", j0, j1) + [(slice(0, NL), "ones", c(0, 128, 1, 8), "c192", c(0, NL, 1, 8), 64)],
-           [R("ms"), R("ones"), R("c192"), R("indr", j0, j1), R("r15", k0, k1)], "rk")
+           [R("ms"), R("ones"), R("c192"), R("indr", j0, j1), R(r15)], "rk")
         if t:
-            tt("pri", ll, "r15", A.mult, k0, k1, slo=0, name="l")
+            tt("pri", ll, r15, A.mult, k0, k1, slo=0, name="l")
             ts("pi", "pri", ("kcol", t), A.add, lo=k0, hi=k1, name="l")
         else:
-            tt("pi", ll, "r15", A.mult, k0, k1, slo=0, name="l")
+            tt("pi", ll, r15, A.mult, k0, k1, slo=0, name="l")
         ts("hm", "pi", 6, A.arith_shift_right, H - 1, A.bitwise_and, lo=k0, hi=k1, name="l")
         cp("hu", "hm", k0, k1, 64, name="l")
         wm = tile()
-        mm(wm, [(slice(0, CH), "ey", al, rf, c(j0, j1), CH), (slice(0, CH), "c15", c(0, 128, 1, 8), "ones", c(0, CH, 1, 8), CH),
-                (slice(0, CH), "ni15", al, "nm", c(j0, j1), CH)],
-           [R("ey"), R("c15"), R("ones"), R("ni15"), R(rf, j0, j1), R("nm", j0, j1), R("hm", k0, k1), R("cache")], "wm")
+        mm(wm, [(slice(0, CH), "ey", al, rf, c(j0, j1), CH), (slice(0, CH), "ni15", al, "nm", c(j0, j1), CH)],
+           [R("ey"), R("ni15"), R(rf, j0, j1), R("nm", j0, j1), R("hm", k0, k1), R("cache")], "wm")
         v(lambda e, B, inc: inc(e.tensor_tensor(out=B("t1")[:, j0:j1], in0=B("cache")[:, D0:D0 + H].indirect(B("hu")[:, k0:k1]), in1=B("nm")[:, j0:j1], op=A.add)),
           [R("cache"), R("hu", k0, k1), R("nm", j0, j1)], [R("t1", j0, j1)], GF * CH, "cache gather")
         tt("r2", wm, "t1", A.max, j0, j1, slo=0, name="r2")
         ts("r2u", "r2", float(SH), A.add, lo=j0, hi=j1, cyc=CH / 2, name="r2u")
-        cls[0] = "P%d" % t
+
+    def phase_p(j0, j1):
+        CH = j1 - j0
         gpt, b0 = 512 // CH, 8 * j0
         for g0 in range(0, 8, gpt):
             d = tile()
@@ -361,7 +378,8 @@ def build_ops(cost):
     def winners(t):
         if t < RO - 1:
             kt = tile()
-            mm(kt, [(slice(0, 1), "kw", al, "kacc", c(t * NC + x, t * NC + x + 1), 256) for x in range(NC)], [R("kw"), R("kacc", t * NC, t * NC + NC)], "K")
+            mm(kt, [(slice(0, 1), "kw", al, "kacc", c(t * NB + x, t * NB + x + 1), 256) for x in range(len(PARTS[t]))],
+               [R("kw"), R("kacc", t * NB, t * NB + NB)], "K")
             ts("kcol", kt, 96.0 * 8 * P, A.add, lo=t + 1, hi=t + 2, slo=0, name="K")
         lf = tile()
         mm(lf, lists(lf, 0, 32, 288, "nm", 0, P), [R("ms"), R("nm"), R("hm")], "fail")
@@ -383,52 +401,44 @@ def build_ops(cost):
                                                          scalar2=B("col")[:, CQ + x:CQ + x + 1], op0=A.add, op1=A.max)),
               [R(z), R("col", CQ, CQ + 2)], [("wu", x, x + 1)], 64, "w")
 
-    def phase_d(t, b):
-        j0, j1, i0 = b * BL, (b + 1) * BL, 16 + b * KB
-        gather("vd", "r2u", j0, j1)
-        maxima("md", "vd", j0, j1, 1)
-        maxima("m2", "vd", j0, j1, 2)
+    def phase_d(t, j0, j1):
         ds = tile()
-        s02, n0, last = slice(0, 3, 2), 3 * BL * b + BL, t == RO - 1
-        va = []
-        for p in range(15):
-            if p % 2:
-                va.append(((s02, slice(p - 1, p + 1)), "vd", rows("vd", j0, p), "wo", (ALL, ALL, ALL, ALL), 64))
-            else:
-                lo, hi = max(p - 1, 0), min(p + 2, 15)
-                va.append(((slice(0, 3), slice(lo, hi)), "vd", rows("vd", j0, p), "we", (ALL, ALL, ALL, slice(lo - p + 1, hi - p + 1)), max(64, 24 * (hi - lo))))
-        va.append(((0, 14), "vd", rows("vd", j0, 15), "bm", c(0, 8), 64))
+        s02 = slice(0, 3, 2)
+        va = [((slice(0, 3), slice(p - 1, p + 1)), "vd", rows("vd", j0, p), "wo", (ALL, ALL, ALL, ALL), 64) for p in range(1, 16, 2)]
+        for p in range(0, 15, 2):
+            lo, hi = max(p - 1, 0), min(p + 2, 15)
+            va.append(((slice(0, 3), slice(lo, hi)), "vd", rows("vd", j0, p), "we", (ALL, ALL, ALL, slice(lo - p + 1, hi - p + 1)), max(64, 24 * (hi - lo))))
         mx = [((s02, slice(p, p + 2)), "md", rows("md", j0, p), "wx", (ALL, ALL, ALL, ALL), 64) if p % 2 == 0 and p < 14 else
               ((0, p), "md", rows("md", j0, p), "b2", c(0, 8), 64) for p in range(15)]
-        mm(ds, [(slice(0, 384), "nq", c(j0, j1), "nw", c(0, 384), 384)], [R("nq", j0, j1), R("yp", j0, j1), R("nw"), R("vd", 16 * j0, 16 * (j0 + KG))], "init d", True, False)
-        mm(ds, va, [R("vd", 16 * j0, 16 * j1), R("bm"), R("we"), R("wo")], "sum d", False, False)
+        mm(ds, va, [R("vd", 16 * j0, 16 * j1), R("we"), R("wo")], "sum d", True, False)
         mm(ds, mx, [R("md", 16 * j0, 16 * j1), R("b2"), R("wx")], "sum m", False, False)
-        mm(ds, [((1, 2 * p + 1), "m2", rows("m2", j0, p, 8), "b2", c(0, 8), 64) for p in range(7)], [R("m2", 8 * j0, 8 * j1), R("b2")], "sum m", False, True)
-        cls[0] = "E%d" % t
-        s(lambda e, B, inc: inc(e.activation(B("sn")[:, n0 - BL:n0 + 2 * BL], B(ds, slice(0, 384)), F.Sign, bias=B("col")[:, CNH:CNH + 1], scale=-1.0)),
-          [R(ds), R("col", CNH, CNH + 1)], [R("sn", n0 - BL, n0 + 2 * BL)], 3 * BL, "near")
-        cls[0] = "S%d" % t
-        scan("kb", slice(i0, i0 + BL), "sn", slice(n0 - BL, n0), "cap2", slice(0, BL), 1.0, A.min, A.max, BL / 2, "kb")
-        cls[0] = "E%d" % t
+        mm(ds, [((1, 2 * p + 1), "m2", rows("m2", j0, p, 8), "b2", c(0, 8), 64) for p in range(7)], [R("m2", 8 * j0, 8 * j1), R("b2")], "sum m", False, False)
+        mm(ds, [(slice(0, 384), "nq", c(j0, j1), "nw", c(0, 384), 384)], [R("nq", j0, j1), R("yp", j0, j1), R("nw")], "loop d", False, True)
+        s(lambda e, B, inc: inc(e.activation(B("sn")[:, :, j0:j1], B(ds, slice(0, 384)), F.Sign, bias=B("col")[:, CNH:CNH + 1], scale=-1.0)),
+          [R(ds), R("col", CNH, CNH + 1)], [("sn", j0, j1), ("sn", P + j0, P + j1)], 3 * BL, "near")
+
+    def phase_e(t, b, j0, j1):
+        BL, last = j1 - j0, t == RO - 1
         nt = tile()
-        mm(nt, [(slice(0, BL), "ones", c(0, 128, 1, 8), "cm8", c(0, BL, 1, 8), BL, True, False)] + turn(0, BL, "sn", n0, "hey", False, False)
-           + turn(0, BL, "sn", n0 + BL, "hey", False, True), [R("sn", n0, n0 + 2 * BL), R("hey"), R("ones"), R("cm8")], "near")
+        mm(nt, [(slice(x, x + 128), "sn", (ALL, y, slice(j0 + x, j0 + x + 128)), "hey", al, 128, y == 1, y == 2) for x in range(0, BL, 128) for y in (1, 2)],
+           [("sn", j0, j1), R("hey")], "near")
         tt("t5", nt, "yp", A.mult, j0, j1, slo=0, name="t5")
         rt = tile()
         whole = [(slice(0, BL), "tri", al, "yp", c(j0, j1), 4 * BL)]
         if last:
-            whole.append((slice(0, BL), "ones", c(0, 128, 1, 8), "c192", c(0, BL, 1, 8), BL))
-        mm(rt, whole, [R("tri"), R("ones"), R("c192"), R("yp", j0, j1), R("sn", n0, n0 + 2 * BL)], "rn")
-        tt("yrs" if last else "rn%d" % t, rt, "t5", A.add, j0, j1, slo=0, name="rn")
-        if last:
-            op("Y", lambda e, B, inc: inc(e.dma_start(B("IN")["yr"][:, j0:j1], B("yrs")[:, j0:j1])), [R("yrs", j0, j1)], [("yr", j0, j1)], 2.5, "store yr", sem="oy%d" % b)
+            mm(rt, whole + [(slice(0, BL), "eyf", al, "t5", c(j0, j1), 4 * BL)], [R("tri"), R("eyf"), R("yp", j0, j1), R("t5", j0, j1)], "rn")
+            s(lambda e, B, inc: inc(e.activation(B("yrs")[:, j0:j1], B(rt, slice(0, BL)), F.Identity, bias=B("col")[:, CSH:CSH + 1])),
+              [R(rt), R("col", CSH, CSH + 1)], [R("yrs", j0, j1)], BL, "yr")
+            op("Y", lambda e, B, inc: inc(e.dma_start(B("IN")["yr"][:, j0:j1], B("yrs")[:, j0:j1])), [R("yrs", j0, j1)], [("yr", j0, j1)], 0.5 * cost["LX"], "store yr", sem="oy%d" % b)
         else:
-            out = "rn%d" % t
-            op("G", ("send", t, j0, j1), [R(out, j0, j1)], [], 1.0, "send", sem="ls%d_%d" % (t + 1, b))
-            ops[-1]["sem2"] = "ar%d_%d" % (t + 1, b)
-            op("N", None, [R(out, j0, j1)], [R("rf%d" % (t + 1), j0, j1)], cost["HOP"], "arrive", sem="ar%d_%d" % (t + 1, b))
-            ops[-1]["after"] = len(ops) - 2
-        cls[0] = "S%d" % t
+            mm(rt, whole, [R("tri"), R("yp", j0, j1), ("sn", j0, j1)], "rn")
+            tt("rn%d" % t, rt, "t5", A.add, j0, j1, slo=0, name="rn")
+            send("rn%d" % t, "rf%d" % (t + 1), j0, j1, "ls%d_%d" % (t + 1, b), "ar%d_%d" % (t + 1, b))
+
+    def phase_s(t, b, j0, j1):
+        BL, i0 = j1 - j0, 16 + b * KA
+        v(lambda e, B, inc: inc(e.tensor_tensor_scan(B("kb")[:, i0:i0 + BL], B("sn")[:, 0, j0:j1], B("cap2")[:, 0:BL], 1.0, A.min, A.max)),
+          [("sn", P + j0, P + j1), R("cap2")], [R("kb", i0, i0 + BL)], BL / 2, "kb")
         at = tile()
         mm(at, turn(0, BL, "kb", i0 - 1, "ey"), [R("kb", i0 - 1, i0 + BL), R("ey")], "a2")
         tt("y2", at, "yp", A.mult, j0, j1, slo=0, name="y2")
@@ -442,18 +452,39 @@ def build_ops(cost):
                [R("wu"), R("st", j0, j1)], [R("cache")], 0.05 + cost["SCF"] * 32 * CYC, "scatter")
 
     for t in range(RO):
-        for ch in range(NC - 1, -1, -1):
-            cls[0], cls[1] = "A%d" % t, NC - 1 - ch
-            phase_a(t, ch)
-        for ch in range(NC - 1, -1, -1):
-            cls[0], cls[1] = "B%d" % t, NC - 1 - ch
-            phase_b(t, ch)
+        for j0, j1 in spans(SENDS[t - 1] if t else (P,)):
+            cls[0], cls[1] = "A%d" % t, (P - j1) // CH
+            if t:
+                ts("ru", "rf%d" % t, float(SH), A.add, lo=j0, hi=j1, cyc=(j1 - j0) / 2, name="ru")
+            else:
+                cp("ru", "r0i", j0, j1, P, name="ru")
+                ts("rf0", "ru", float(-SH), A.add, lo=j0, hi=j1, cyc=P / 2, name="rf")
+        for ch, (j0, j1) in enumerate(spans(PARTS[t])):
+            cls[0], cls[1] = "A%d" % t, ch
+            phase_a(t, ch, j0, j1)
+        cls[0], cls[1] = "R%d" % t, 0
+        ends(t)
+        for ch, (j0, j1) in enumerate(spans(PARTS[t])):
+            cls[0], cls[1] = "B%d" % t, ch
+            phase_b(t, ch, j0, j1)
+        for ch, (j0, j1) in enumerate(spans(LOOPS[t])):
+            cls[0], cls[1] = "P%d" % t, ch
+            phase_p(j0, j1)
         cls[0], cls[1] = "W%d" % t, 0
         winners(t)
-        for b in range(NB - 1, -1, -1):
-            cls[0], cls[1] = "D%d" % t, NB - 1 - b
-            phase_d(t, b)
-    op("Y", lambda e, B, inc: inc(e.dma_start(B("IN")["yc"][:, :], B("cache")[:, D0:D0 + H])), [R("cache")], [("yc", 0, H)], 3.5, "store yc", sem="oc")
+        for j0, j1 in spans(DISTS[t]):
+            cls[0], cls[1] = "D%d" % t, (P - j1) // BL
+            gather("vd", "r2u", j0, j1)
+            maxima("md", "vd", j0, j1, 1)
+            maxima("m2", "vd", j0, j1, 2)
+            for j in range(j1 - BL, j0 - 1, -BL):
+                cls[1] = (P - BL - j) // BL
+                phase_d(t, j, j + BL)
+        for name, phase, sizes in (("E", phase_e, SENDS[t]), ("S", phase_s, COPIES[t])):
+            for b, (j0, j1) in enumerate(spans(sizes)):
+                cls[0], cls[1] = "%s%d" % (name, t), (P - j1) // BL
+                phase(t, b, j0, j1)
+    op("Y", lambda e, B, inc: inc(e.dma_start(B("IN")["yc"][:, :], B("cache")[:, D0:D0 + H])), [R("cache")], [("yc", 0, H)], 0.7 * cost["LX"], "store yc", sem="oc")
     return ops, tiles
 
 
@@ -501,12 +532,18 @@ def schedule(cost=COST, bias=BIAS):
     for i in range(n):
         for d in dep[i]:
             succ[d].append(i)
+    beat, due = cost["LX"], {}
+    for i, o in enumerate(ops):
+        if o["name"] == "gather" and o["q"] == "S":
+            beat += o["dur"] * bias["beat"] / 100
+            due[i] = beat
     rank = [0.0] * n
     for i in range(n - 1, -1, -1):
-        rank[i] = ops[i]["dur"] + max([rank[j] + LAT for j in succ[i]] or [0.0])
-    for i in range(n):
-        k = ops[i]["cls"]
-        rank[i] += bias.get(k, 0.0) + bias.get(k[0], 0.0) + bias.get(k[0] + "+", 0.0) * ops[i]["part"] + bias.get(ops[i]["name"], 0.0)
+        rank[i] = ops[i]["dur"] + max([rank[j] + LAT * bias["gap"] / 10 for j in succ[i]] + [-due.get(i, beat + 0.1 * bias.get("tail", 80))])
+    for i, o in enumerate(ops):
+        early = o["cls"][0] == "K" or o["name"] in ("load x", "iota0") or (o["cls"][0] == "C" and o["q"] in "VS")
+        short = o["q"] == "S" and o["name"] in ("bad", "nm", "st", "near")
+        rank[i] += 30 * early + 50 * short + 0.1 * (bias.get(o["cls"][0] + str(o["part"]), 0) + bias.get(o["name"], 0))
     rank = bias.get("rank", rank)
     free = {q: 0.0 for q in "VSTGYAN"}
     pool = {"p%d" % i: 0.0 for i in range(NPS)}
@@ -521,7 +558,7 @@ def schedule(cost=COST, bias=BIAS):
             e0 = est[i]
             new = [b for b, lo, hi in o["w"] if isinstance(b, tuple) and tiles[b[1]]["buf"] is None]
             if new:
-                if len(pool) < 1 + (o["name"] in ("sum a", "init d", "rn", "st")):
+                if len(pool) < 1 + (o["name"] in ("sum a", "sum d", "init d", "rn", "st")):
                     continue
                 e0 = max(e0, min(pool.values()) + LAT)
             for q in o["qs"]:
@@ -529,7 +566,7 @@ def schedule(cost=COST, bias=BIAS):
         assert cands, "no operation can go on"
         t0 = min(x[0] for x in cands)
         q0 = min(cands)[3]
-        st, _, i, q = min([x for x in cands if x[3] == q0 and x[0] <= t0 + 0.01 * bias.get("wait" + q0, 3)], key=lambda x: (x[1], x[0]))
+        st, _, i, q = min([x for x in cands if x[3] == q0 and x[0] <= t0 + 0.01 * max(bias["wait"], 0)], key=lambda x: (x[1], x[0]))
         o = ops[i]
         o["q"] = q
         for b, lo, hi in o["w"]:
@@ -559,43 +596,71 @@ def schedule(cost=COST, bias=BIAS):
     return [ops[i] for i in order], tiles, max(endt)
 
 
-def backward(seq, cost):
-    n, ops = len(seq), sorted(seq, key=lambda o: o["id"])
-    dep = deps_of(ops, lambda b: b, lambda b: isinstance(b, tuple))
-    later, left = [[] for _ in range(n)], [0] * n
-    for i in range(n):
-        for d, kk in dep[i].items():
-            later[d].append((i, 0.0 if free_of_wait(ops[i], ops[d], kk) else cost["LAT"]))
-            left[d] += 1
-    free, end, est = {q: 0.0 for q in "VSTGYAN"}, [0.0] * n, {}
-    ready = [i for i in range(n) if left[i] == 0]
-    while ready:
-        cands = []
-        for i in ready:
-            if i not in est:
-                est[i] = max([end[j] + w for j, w in later[i]] or [0.0])
-            q = ops[i]["q"]
-            cands.append((est[i] if q in "NYA" else max(est[i], free[q]), -ops[i]["t1"], i, q))
-        m = min(cands)
-        st, _, i, q = min([x for x in cands if x[3] == m[3] and x[0] <= m[0] + 0.03], key=lambda x: (x[1], x[0]))
-        end[i] = free[q] = st + ops[i]["dur"]
-        ready.remove(i)
-        for d in dep[i]:
-            left[d] -= 1
-            if left[d] == 0:
-                ready.append(d)
-    return end
+def tighten(seq, dep, costs, steps):
+    n, byid, rng = len(seq), {o["id"]: o for o in seq}, np.random.RandomState(0)
+    need, succ = [None] * n, [[] for _ in range(n)]
+    for o, d in zip(seq, dep):
+        need[o["id"]] = [(i, not free_of_wait(o, byid[i], kk)) for i, kk in d.items()]
+        for i in d:
+            succ[i].append(o["id"])
+    queues = {q: [o["id"] for o in seq if o["q"] == q] for q in "VSTG"}
+    cases = [([o["dur"] for o in build_ops(x)[0]], x["LAT"]) for x in costs]
 
+    def times():
+        before, after = [None] * n, [None] * n
+        for line in queues.values():
+            for a, b in zip(line, line[1:]):
+                before[b], after[a] = a, b
+        left = [len(need[i]) + (before[i] is not None) for i in range(n)]
+        order = [i for i in range(n) if not left[i]]
+        for i in order:
+            for j in succ[i] + ([after[i]] if after[i] is not None else []):
+                left[j] -= 1
+                if not left[j]:
+                    order.append(j)
+        if len(order) < n:
+            return (1e9,)
+        ends, whys = [], []
+        for dur, lat in cases:
+            end, why = [0.0] * n, [None] * n
+            for i in order:
+                w = before[i]
+                m = 0.0 if w is None else end[w]
+                for d, wait in need[i]:
+                    e = end[d] + lat if wait else end[d]
+                    if e > m:
+                        m, w = e, d
+                end[i], why[i] = m + dur[i], w
+            ends.append(end)
+            whys.append(why)
+        return sum(max(e) for e in ends) / len(ends), ends, whys, before
 
-def best_order(cost=COST, passes=6):
-    bias, best = BIAS, None
-    for _ in range(passes):
-        got = schedule(cost, bias)
-        if best is None or got[2] < best[2]:
-            best = got
-        rank = backward(got[0], cost)
-        bias = dict(WAIT, rank=[rank[o["id"]] + URGENT.get(o["name"], 0.0) for o in sorted(got[0], key=lambda o: o["id"])])
-    return best
+    cur = best = times()
+    for step in range(steps):
+        case = rng.randint(len(cases))
+        end, why = cur[1][case], cur[2][case]
+        i, path = end.index(max(end)), []
+        while i is not None:
+            if why[i] is not None and why[i] == cur[3][i] and i not in succ[why[i]]:
+                path.append(i)
+            i = why[i]
+        u = path[rng.randint(len(path))]
+        q, k = byid[u]["q"], (1, 1, 2, 3, 5, 8)[rng.randint(6)]
+        line = queues[q]
+        p = line.index(u)
+        if rng.randint(2):
+            queues[q] = line[:max(p - k, 0)] + [u] + line[max(p - k, 0):p] + line[p + 1:]
+        else:
+            queues[q] = line[:p - 1] + line[p:p + k] + [line[p - 1]] + line[p + k:]
+        new = times()
+        if new[0] - cur[0] <= -math.log(1.0 - rng.rand()) * 0.15 * (1.0 - step / steps):
+            cur = new
+            best = min(best, cur, key=lambda x: x[0])
+        else:
+            queues[q] = line
+    for o in seq:
+        o["t0"], o["t1"] = best[1][0][o["id"]] - cases[0][0][o["id"]], best[1][0][o["id"]]
+    return sorted(seq, key=lambda o: o["t0"])
 
 
 PLAN = {}
@@ -603,8 +668,9 @@ PLAN = {}
 
 def plan():
     if not PLAN:
-        seq, tiles, end = best_order()
+        seq, tiles, end = schedule()
         key = lambda b: tiles[b[1]]["buf"] if isinstance(b, tuple) else b
+        seq = tighten(seq, deps_of(seq, key, lambda b: isinstance(b, tuple)), [dict(COST, **x) for x in CASES], STEPS)
         PLAN["seq"], PLAN["tiles"] = seq, tiles
         PLAN["dep"] = deps_of(seq, key, lambda b: isinstance(b, tuple))
     return PLAN
@@ -667,8 +733,8 @@ def rank_program(g, core, T, topo):
                 kn[s2] = max(kn.get(s2, 0), c2)
         cur[0] = q
         if isinstance(o["fn"], tuple):
-            _, t, j0, j1 = o["fn"]
-            g.remote_dma(T["rf%d" % (t + 1)][:, j0:j1], T["rn%d" % t][:, j0:j1], T.sem[o["sem2"]], T.sem[o["sem"]], pid, rid, emask)
+            _, a, z, j0, j1 = o["fn"]
+            g.remote_dma(T[z][:, j0:j1], T[a][:, j0:j1], T.sem[o["sem2"]], T.sem[o["sem"]], pid, rid, emask)
             done[o["id"]] = (o["sem"], ne, {})
             pend[o["sem"]] = ne
         elif o["sem"]:

import math
import numpy as np
from concourse.mybir import AluOpType as A, ActivationFunctionType as F, AxisListType as AX

W, H, P, RO, ST = 3072, 1024, 512, 3, 2
SH = 1536
CH = 256
PARTS = [(128, 128, 256), (256, 256), (256, 256)]
LOOPS = PARTS
DISTS = [(128, 128, 128, 128)] * RO
SENDS = [(128, 128, 128, 128)] * RO
COPIES = [(256, 256), (256, 256), (256, 128, 128)]
BL = 128
NB = P // BL
KG = 32
D0 = 32
KA = CH + 16

SCRATCH = {}


def bufs(dtype, **sizes):
    for k in sizes:
        SCRATCH[k] = ("sbuf", [128, sizes[k]], dtype)


bufs("bfloat16", xs=W, va=16 * P, vd=16 * P, mx=16 * P, md=16 * P, m2=8 * P, ka=NB * KA, kb=NB * KA, sa=P, nm=P, nq=P,
     eqp=8 * P, eqh=512)
bufs("float16", rf0=P, rf1=P, rf2=P, rn0=P, rn1=P, indr=P, r2=P, hh=32)
bufs("uint16", ru=P, r2u=P, hu=32, wu=32)
bufs("int32", r0i=P, c0i=H, pi=32, hm=32, ki=8, kp=8, ks=8, kt=8, ia=256, ib=256)
bufs("float32", cache=D0 + H, t1=P, yp=P, y2=P, t5=P, st=P, yrs=P, r150=32, r151=32, r152=32, eyf=128, pri=32, kacc=16, kcol=8, col=16, rio=16, fa=16, fb=16, fc=16,
     onesf=128, tri=128, tra=128, t15=128, kw=128, bmf=8)
bufs("bfloat16", ones=CH, zero=512, pe=1024, po=2048, lw=248, lwa=8, ey=128, ney=128, hey=128, e15=128, cap2=CH, b2=8, b2a=8, bm=8, bma=8, nw=384, cap=CH, ms=432, c192=16,
     ni15=128, c15=128, pq=256, pd=128, pb=1024, vw=480, dl=128)
NPS = 8
for _i in range(NPS):
    SCRATCH["p%d" % _i] = ("psum", [128, 4, 8, 16], "float32")
SCRATCH["sn"] = ("sbuf", [128, 3, P], "bfloat16")
SCRATCH["we"] = ("sbuf", [128, 3, 8, 3], "bfloat16")
SCRATCH["wo"] = ("sbuf", [128, 3, 8, 2], "bfloat16")
SCRATCH["wx"] = ("sbuf", [128, 2, 8, 2], "bfloat16")
ALL = slice(None)


def bank_view(w):
    if isinstance(w, tuple):
        return (ALL, w[0], ALL, w[1]) if len(w) == 2 else (ALL,) + w
    a, b = w.start, w.stop
    if a % 128 == 0 and b % 128 == 0:
        return (ALL, slice(a // 128, b // 128), ALL, ALL)
    if a % 16 == 0 and b % 16 == 0:
        return (ALL, a // 128, slice(a % 128 // 16, (b - 1) % 128 // 16 + 1), ALL)
    return (ALL, a // 128, a % 128 // 16, slice(a % 16, (b - 1) % 16 + 1))


SEMAPHORES = (["qV", "qS", "qT", "qG", "lr", "lx", "ad1", "ad2", "ld1", "ld2", "lc", "oc"] + ["oy%d" % b for b in range(NB)]
              + ["ar%d_%d" % (t, b) for t in range(1, RO) for b in range(NB)]
              + ["ls%d_%d" % (t, b) for t in range(1, RO) for b in range(NB)])

COST = {"CYC": 0.00083, "TCYC": 0.00042, "LAT": 0.12, "GF": 1.56, "SCF": 3.8, "HOP": 3.0, "LX": 4.3, "SEND": 1.0}
BIAS = {'beat': 143, 'gap': 12, 'wait': 8, 'B0': 60, 'B1': 161, 'B2': 34, 'S3': 79, 'sum a': 54, 'S2': -35, 'w': 46, 'D0': -4, 'E1': -21, 'sum d': 30,
        'sum m': -12, 'E2': 250, 'A1': -15, 'R0': -16, 'S1': 22, 'loop': 160, 'P2': 9, 'A0': -16, 'pairs': -3, 'A2': -203, 'scatter': 26, 'E0': 51,
        'eq': -14, 'max2': 8, 'D2': -15, 'P0': 9, 'C0': -72, 'gather': 1, 'l': -53, 'D3': -44, 'max1': 1, 'S0': -5, 'D1': 1, 'ru': -12, 'P1': 4,
        'W0': 6, 'E3': -2}
STEPS = 36000
CASES = [{}, {"GF": 1.08, "SCF": 2.2, "HOP": 2.5, "LX": 3.6}, {"GF": 1.25, "SCF": 4.0, "HOP": 3.8, "SEND": 1.3}]
KGS = {"D1": 64, "D2": 64, "A1": 64}
VG = {"A0": (0, 1, 4, 8), "A1": (4,), "A2": (4,)}
CQ, CQ2, CLO, CHI, CSC, CBI, CNH, CW, C15, CSH, CTH = range(11)


def spans(sizes):
    ends = [P - sum(sizes[:i]) for i in range(len(sizes) + 1)]
    return list(zip(ends[1:], ends[:-1]))


def build_ops(cost):
    ops, tiles, cls = [], [], ["C", 0]
    CYC, TCYC, GF = cost["CYC"], cost["TCYC"], cost["GF"]

    def tile():
        tiles.append({"users": 0, "buf": None})
        return ("tile", len(tiles) - 1)

    def op(qs, fn, reads, writes, dur, name="", sem=None):
        ops.append({"qs": qs, "fn": fn, "r": reads, "w": writes, "dur": dur, "name": name, "sem": sem, "id": len(ops), "cls": cls[0], "part": cls[1]})

    def R(buf, lo=0, hi=None):
        if isinstance(buf, tuple) or len(SCRATCH[buf][1]) > 2:
            return (buf, 0, 512)
        return (buf, lo, SCRATCH[buf][1][1] if hi is None else hi)

    def v(fn, reads, writes, cyc, name=""):
        op("V", fn, reads, writes, 0.055 + CYC * max(cyc, 64), name)

    def s(fn, reads, writes, cyc, name=""):
        op("S", fn, reads, writes, 0.065 + CYC * max(cyc, 64), name)

    def gp(fn, reads, writes, n, name=""):
        op("G", fn, reads, writes, (0.17 * CYC / 0.00083 + 2 * CYC * n) * cost.get("GX", 1.0), name)

    def mm(out, terms, reads, name, first=True, last=True):
        def fn(e, B, inc):
            for i, x in enumerate(terms):
                a, z = (x[6], x[7]) if len(x) > 6 else (first and i == 0, last and i == len(terms) - 1)
                inc(e.matmul(B(out, x[0]), B(x[1])[x[2]], B(x[3])[x[4]], a, z))
        op("T", fn, reads, [R(out)], sum(x[5] for x in terms) * TCYC + 0.03, name)

    def c(lo, hi, st=1, p=128):
        return (slice(0, p), slice(lo, hi, st))

    def ts(dst, src, s1, o1, s2=None, o2=None, lo=0, hi=1, cyc=64, slo=None, name="ts", dview=None):
        a, b = (lo, hi) if slo is None else (slo, slo + hi - lo)
        w = slice(lo, hi) if dview is None else dview
        val = lambda B, x: B(x[0])[:, x[1]:x[1] + 1] if isinstance(x, tuple) else x

        def fn(e, B, inc):
            if o2 is None:
                inc(e.tensor_scalar(out=B(dst)[:, w], in0=B(src, slice(a, b)), scalar1=val(B, s1), scalar2=None, op0=o1))
            else:
                inc(e.tensor_scalar(out=B(dst)[:, w], in0=B(src, slice(a, b)), scalar1=val(B, s1), scalar2=val(B, s2), op0=o1, op1=o2))
        cols = [R(x[0], x[1], x[1] + 1) for x in (s1, s2) if isinstance(x, tuple)]
        v(fn, [R(src, a, b)] + cols, [R(dst, w.start, w.stop)], cyc, name)

    def tt(dst, in0, in1, o, lo, hi, cyc=None, slo=None, name="tt", lo1=None):
        a, b = (lo, hi) if slo is None else (slo, slo + hi - lo)
        a1, b1 = (lo, hi) if lo1 is None else (lo1, lo1 + hi - lo)
        v(lambda e, B, inc: inc(e.tensor_tensor(out=B(dst)[:, lo:hi], in0=B(in0, slice(a, b)), in1=B(in1)[:, a1:b1], op=o)),
          [R(in0, a, b), R(in1, a1, b1)], [R(dst, lo, hi)], (hi - lo) if cyc is None else cyc, name)

    def cp(dst, src, lo, hi, cyc, slo=None, name="cp"):
        a, b = (lo, hi) if slo is None else (slo, slo + hi - lo)
        v(lambda e, B, inc: inc(e.tensor_copy(out=B(dst)[:, lo:hi], in_=B(src)[:, a:b])), [R(src, a, b)], [R(dst, lo, hi)], cyc, name)

    def scan(dst, dv, a, av, b, bv, init, o0, o1, cyc, name):
        rng = lambda x, w: R(x, w.start, w.stop)
        v(lambda e, B, inc: inc(e.tensor_tensor_scan(B(dst)[:, dv], B(a, av), B(b)[:, bv], init, o0, o1)),
          [rng(a, av), rng(b, bv)], [rng(dst, dv)], cyc, name)

    op("A", lambda e, B, inc: inc(e.dma_start(B("r0i")[:, :], B("IN")["r0"][:, :])), [], [R("r0i")], 0.55 * cost["LX"], "load r0", sem="lr")
    op("Y", lambda e, B, inc: inc(e.dma_start(B("xs")[:, :], B("IN")["x"][:, :])), [], [R("xs")], cost["LX"], "load x", sem="lx")
    op("Y", lambda e, B, inc: inc(e.dma_start(B("c0i")[:, :], B("IN")["c0"][:, :])), [], [R("c0i")], 1.4 * cost["LX"], "load c0", sem="lc")

    def fill(buf, val, lo=0, hi=None, st=1):
        hi = SCRATCH[buf][1][1] if hi is None else hi
        v(lambda e, B, inc: inc(e.memset(B(buf)[:, lo:hi:st], val)), [], [R(buf, lo, hi)], (hi - lo) / st / 2, "fill")

    def sfill(buf, val, lo=0, hi=None, st=1):
        hi = SCRATCH[buf][1][1] if hi is None else hi
        n, src = len(range(lo, hi, st)), "ones" if val else "zero"
        s(lambda e, B, inc: inc(e.activation(B(buf)[:, lo:hi:st], B(src)[:, 0:n], F.Copy, scale=val)), [R(src, 0, n)], [R(buf, lo, hi)], n, "fill")

    def sel(dst, src, pat, cmp, fillv, base, cm, view=None, sview=None):
        n = 1
        for x in pat:
            n *= x[1]
        w = slice(0, n) if view is None else view
        u = w if sview is None else sview
        gp(lambda e, B, inc: inc(e.affine_select(out=B(dst)[:, w], in_=B(src)[:, u], pattern=pat, compare_op=cmp, fill=fillv, base=base, channel_multiplier=cm)),
           [R(src, u.start, u.stop)], [R(dst, w.start, w.stop)], n, "sel " + dst)

    def iota(dst, lo, hi, pat, base, cm, flt=False):
        if flt:
            gp(lambda e, B, inc: inc(e.iota(B(dst)[:, lo:hi], pat, base, cm, allow_small_or_imprecise_dtypes=True)), [], [R(dst, lo, hi)], hi - lo, "iota0")
        else:
            gp(lambda e, B, inc: inc(e.iota(B(dst)[:, lo:hi], pat, base, cm)), [], [R(dst, lo, hi)], hi - lo, "iota0")

    def weights(dst, parts):
        for x, y, src in parts:
            gp(lambda e, B, inc, x=x, y=y, src=src: inc(e.affine_select(out=B(dst)[:, x, :, y], in_=B(src)[:, 0:8], pattern=[[0, 8]], compare_op=A.is_ge,
                                                                        fill=0.0, base=0, channel_multiplier=0)),
               [R(src, 0, 8)], [(dst, 3 * x + y, 3 * x + y + 1)], 8, "sel " + dst)

    NE, GE = A.not_equal, A.is_ge
    fill("zero", 0.0)
    fill("ones", 1.0)
    for a, z, val in (("bma", "bm", -1.0), ("b2a", "b2", 2.0)):
        sel(a, "zero", [[16, 8]], A.is_gt, val, 0, -1)
        sel(z, a, [[16, 8]], GE, 0.0, 15, -1)
    for x in ("wo", "we", "wx"):
        v(lambda e, B, inc, x=x: inc(e.memset(B(x)[:, :, :, :], 0.0)), [], [R(x)], 64, "fill")
    weights("wo", [(0, 0, "bm"), (0, 1, "bm")])
    sfill("col", -40.5, CTH, CTH + 1)
    sel("cap", "ones", [[0, CH // 16], [1, 16]], NE, 0.0, -15, 0)
    sel("ey", "zero", [[-1, 128]], NE, 1.0, 0, 1)
    sel("ney", "zero", [[-1, 128]], NE, -1.0, 0, 1)
    sfill("ka", 0.0, 15, NB * KA, KA)
    sfill("ms", 0.0)
    w8 = slice(0, 8)
    sel("b2a", "ones", [[-16, 8]], GE, 0.0, 0, 1)
    sel("ms", "b2a", [[16, 8]], GE, 0.0, 14, -1, slice(15, 143, 16), w8)
    sel("ms", "zero", [[-16, 8]], NE, 1.0, -15, 1, slice(159, 287, 16), w8)
    sel("ms", "zero", [[-16, 8]], NE, 0.125, -15, 1, slice(303, 431, 16), w8)
    sfill("c192", SH / 8.0)
    iota("ki", 0, 1, [[0, 1]], 0, 1)
    iota("rio", 0, 16, [[1, 16]], 0, 0, True)
    sel("c15", "ney", [[-16, 8], [0, 16]], NE, 1.0, 0, 1)
    sel("c15", "zero", [[0, 8]], GE, 0.0, 0, 0, slice(0, 128, 16), w8)
    sel("ni15", "c15", [[0, 8], [1, 16]], NE, 0.0, -15, 0)
    ts("kp", "ki", 15, A.bitwise_and)
    cp("col", "kp", CQ, CQ + 1, 64, slo=0)
    ts("col", "kp", 15.0, A.is_equal, lo=C15, hi=C15 + 1, slo=0)
    ts("col", "col", 10240.0, A.mult, 6144.0, A.add, lo=CSC, hi=CSC + 1, slo=C15)
    ts("col", "col", -16896.0, A.mult, -7680.0, A.add, lo=CBI, hi=CBI + 1, slo=C15)
    ts("col", "kp", 16.0, A.add, lo=CQ2, hi=CQ2 + 1, slo=0)
    sfill("cache", 0.0, 0, D0)
    gp(lambda e, B, inc: inc(e.affine_select(out=B("cache")[:, D0:D0 + H], in_=B("c0i")[:, 0:H], pattern=[[0, H]], compare_op=GE, fill=0.0, base=0,
                                             channel_multiplier=0)), [R("c0i")], [R("cache", D0, D0 + H)], H, "cache")
    cls[0] = "K0"
    iota("ia", 0, 128, [[0, 8], [1, 16]], 128, -1)
    iota("ia", 128, 256, [[1, 8], [1, 16]], 129, -1)
    ts("ib", "ia", 15, A.bitwise_and, hi=256, cyc=256)
    ts("pq", "ib", 0.0, A.is_equal, hi=256, cyc=256)
    tt("pd", "pq", "pq", A.subtract, 0, 128, 256, lo1=128)
    sel("bmf", "bm", [[0, 8]], GE, 0.0, 0, 0)
    for g in range(8):
        s(lambda e, B, inc, g=g: inc(e.activation(B("pb")[:, 128 * g:128 * g + 128], B("pd")[:, 0:128], F.Copy, scale=B("bmf")[:, g:g + 1])),
          [R("pd"), R("bmf")], [R("pb", 128 * g, 128 * g + 128)], 128, "pb")
    cls[0] = "C0"
    sel("dl", "ey", [[-1, 128]], NE, -1.0, 1, 1)
    sel("dl", "ones", [[-16, 8]], A.is_equal, 0.0, 0, 1, slice(0, 128, 16), w8)
    ts("ks", "ki", 4, A.arith_shift_right)
    tt("kt", "ks", "kp", A.add, 0, 1, 64)
    ts("ks", "kt", 1.0, A.add)
    ts("kt", "ks", 15, A.bitwise_and)
    tt("col", "kp", "kt", A.min, CLO, CLO + 1, 64, slo=0, lo1=0)
    tt("col", "kp", "kt", A.max, CHI, CHI + 1, 64, slo=0, lo1=0)
    sfill("vw", 0.0)
    ts("fa", "rio", ("col", CLO), A.is_gt, 2.0 ** -8, A.max, hi=16)
    v(lambda e, B, inc: inc(e.tensor_reduce(B("col")[:, CW:CW + 1], B("fa")[:, 0:16], AX.X, A.mult)), [R("fa")], [R("col", CW, CW + 1)], 64, "red")
    ts("fb", "rio", ("col", CLO), A.is_gt, 17.0 * 2.0 ** 60, A.mult, hi=16)
    ts("fc", "rio", ("col", CHI), A.is_le, hi=16)
    tt("fa", "fb", "fc", A.mult, 0, 16, 64)
    ts("vw", "fa", -2.0 ** 60, A.add, ("col", CW), A.mult, lo=112, hi=128, slo=0)
    ts("vw", "rio", ("col", CHI), A.is_equal, -4096.0, A.mult, lo=352, hi=368, slo=0)
    sel("nw", "zero", [[-1, 128]], NE, 256.0, -1, 1)
    sel("nw", "nw", [[-16, 8], [0, 16]], NE, -296.0, 0, 1)
    sel("nw", "zero", [[0, 2], [-16, 8], [0, 16]], NE, 216.0, 0, 1, slice(128, 384), slice(0, 256))
    sel("nw", "nw", [[-2, 64]], NE, -256.0, -2, 1, slice(129, 256, 2))
    sel("nw", "nw", [[-2, 64]], NE, 256.0, -2, 1, slice(257, 384, 2))
    sel("nw", "nw", [[-16, 8], [0, 8]], NE, -40.0, 0, 1, slice(257, 384, 2))
    sel("nw", "zero", [[0, 2], [-16, 8]], NE, 512.0, 0, 1, slice(143, 384, 16), slice(0, 16))
    weights("wo", [(2, 1, "bm")])
    weights("we", [(x, y, "bm") for x, y in ((0, 0), (0, 1), (1, 0), (1, 2), (2, 2))])
    weights("wx", [(x, x, "b2") for x in (0, 1)])
    sel("hey", "zero", [[-1, 128]], NE, -0.5, 0, 1)
    sel("cap2", "zero", [[0, CH // 16], [1, 16]], NE, 1.0, -15, 0)
    sel("e15", "ey", [[0, 8], [1, 16]], A.is_equal, 0.0, -15, 0)
    sfill("kb", 1.0, 15, NB * KA, KA)
    sfill("col", 0.5, CNH, CNH + 1)
    sfill("col", float(SH), CSH, CSH + 1)
    for x in range(2):
        sel("pe", "zero", [[-16, 4], [0, 8], [-1, 16]], NE, 1.0, -64 * x, 1, slice(512 * x, 512 * x + 512), slice(0, 512))
    for x in range(4):
        sel("po", "zero", [[-1, 32], [0, 16]], NE, -1.0, -32 * x, 1, slice(512 * x, 512 * x + 512), slice(0, 512))
    sfill("lw", 0.0)
    sel("lwa", "zero", [[16, 8]], A.is_gt, -4096.0, 0, -1)
    sel("lw", "lwa", [[16, 8]], GE, 0.0, 15, -1, slice(120, 128), w8)
    iota("onesf", 0, 128, [[0, 128]], 1, 0, True)
    sel("tri", "onesf", [[1, 128]], GE, 0.0, 0, -1)
    sel("tra", "tri", [[-16, 8], [0, 16]], GE, 0.0, 0, 1)
    sel("tri", "tra", [[-1, 128]], NE, 0.0, 0, 1)
    sel("eyf", "onesf", [[-1, 128]], A.is_equal, 0.0, 0, 1)
    sel("t15", "tra", [[0, 8], [1, 16]], NE, 0.0, -15, 0)
    ts("kw", "onesf", ("col", C15), A.mult, 1.0 / 256, A.mult, hi=128, cyc=128)

    al = c(0, 128)

    def gather(vb, off, j0, j1):
        KG = KGS.get(cls[0][0] + str(cls[1]), 32)
        for j in range(j0, j1, KG):
            def fn(e, B, inc, j=j):
                o, w = B(vb)[:, 16 * j:16 * (j + KG)], B("xs")[:, 0:W].indirect(B(off)[:, j:j + KG])
                if B("Q") == "V":
                    inc(e.tensor_copy(out=o, in_=w))
                else:
                    inc(e.activation(o, w, F.Copy))
            op("V" if (P - KG - j) // 32 in VG.get(cls[0], ()) else "S", fn, [R("xs"), R(off, j, j + KG)], [R(vb, 16 * j, 16 * (j + KG))], 0.065 + GF * CYC * 16 * KG, "gather")

    def maxima(dst, vb, j0, j1, d):
        lo, hi = 16 * j0, 16 * j1
        scan(dst, slice(lo // d, hi // d - 1), vb, slice(lo, hi - d, d), vb, slice(lo + d, hi, d), 16.0, A.min, A.max, 8 * (j1 - j0) / d, "max%d" % d)

    def rows(buf, j, p, k=16):
        return c(k * j + p, k * (j + BL), k)

    def lists(out, o0, n, m0, src, j0, j1):
        return [(slice(o0, o0 + n), "ms", c(m0 + 15 - q, m0 + 143 - q), src, c(j0 + q, j1, 16), 64) for q in range(16)]

    def phase_a(t, ch, j0, j1):
        CH, NL, rf, i0 = j1 - j0, (j1 - j0) // 16, "rf%d" % t, 16 + ch * KA
        ds = tile()
        first = True
        for j in range(j1 - BL, j0 - 1, -BL):
            gather("va", "ru", j, j + BL)
            maxima("mx", "va", j, j + BL, 1)
            x = (j - j0) // BL
            va = [((x, slice(max(p - 1, 0), p + 1)), "va", rows("va", j, p), "wo", (ALL, 0, ALL, slice(0, 1 + (p > 0))), 64)
                  for p in list(range(1, 16, 2)) + list(range(0, 16, 2))]
            mm(ds, va, [R("va", 16 * j, 16 * (j + BL)), ("wo", 0, 2)], "sum a", first, False)
            mm(ds, [((x, p), "mx", rows("mx", j, p), "b2", c(0, 8), 64) for p in range(15)], [R("mx", 16 * j, 16 * (j + BL)), R("b2")], "sum m", False, j == j0)
            first = False
        s(lambda e, B, inc: inc(e.activation(B("sa")[:, j0:j1], B(ds, slice(0, CH)), F.Sign, bias=B("col")[:, CTH:CTH + 1])),
          [R(ds), R("col", CTH, CTH + 1)], [R("sa", j0, j1)], CH, "bad")
        scan("ka", slice(i0, i0 + CH), "sa", slice(j0, j1), "cap", slice(0, CH), 0.0, A.max, A.min, CH / 2, "ka")

    def send(src, dst, j0, j1, gone, come):
        op("G", ("send", src, dst, j0, j1), [R(src, j0, j1)], [], cost["SEND"], "send", sem=gone)
        ops[-1]["sem2"] = come
        op("N", None, [R(src, j0, j1)], [R(dst, j0, j1)], cost["HOP"], "arrive", sem=come)
        ops[-1]["after"] = len(ops) - 2

    def ends(t):
        if t == 0:
            l15 = tile()
            mm(l15, lists(l15, 0, 32, 144, "rf0", 0, P), [R("ms"), R("rf0")], "r15")
            ts("r150", l15, float(SH + 64), A.add, hi=32, name="r15")
        if t < RO - 1:
            send("r15%d" % t, "r15%d" % (t + 1), 0, 32, "ld%d" % (t + 1), "ad%d" % (t + 1))

    def turn(o0, n, buf, i0, m, start=True, stop=True):
        return [(slice(o0 + x, o0 + x + 128), buf, c(i0 + x, i0 + x + 128), m, al, 128, start, stop) for x in range(0, n, 128)]

    def phase_b(t, ch, j0, j1):
        CH, NL, k0, k1, i0 = j1 - j0, (j1 - j0) // 16, j0 // 16, j1 // 16, 16 + ch * KA
        kr, rf, r15 = [R("ka", i0 - 1, i0 + CH), R("ey"), R("ney")], "rf%d" % t, "r15%d" % t
        qt = tile()
        a, b = turn(0, CH, "ka", i0, "ey", True, False), turn(0, CH, "ka", i0 - 1, "ney", False, True)
        mm(qt, [x for ab in zip(a, b) for x in ab], kr + [R(rf, j0, j1)], "ind")
        tt("indr", qt, rf, A.mult, j0, j1, slo=0, name="indr")
        qa = tile()
        mm(qa, turn(0, CH, "ka", i0 - 1, "ey"), kr, "a")
        kc = t * NB + ch

        def fnm(e, B, inc):
            sc, bi = B("col")[:, CSC:CSC + 1], B("col")[:, CBI:CBI + 1]
            if t < RO - 1:
                inc(e.activation(B("nm")[:, j0:j1], B(qa, slice(0, CH)), F.Identity, bias=bi, scale=sc, accum_out=B("kacc")[:, kc:kc + 1]))
            else:
                inc(e.activation(B("nm")[:, j0:j1], B(qa, slice(0, CH)), F.Identity, bias=bi, scale=sc))
        s(fnm, [R(qa), R("col", CSC, CBI + 1)], [R("nm", j0, j1), R("kacc", kc, kc + 1)], CH + 24, "nm")
        ll = tile()
        mm(ll, lists(ll, 0, NL, 0, "indr", j0, j1) + [(slice(0, NL), "ones", c(0, 128, 1, 8), "c192", c(0, NL, 1, 8), 64)],
           [R("ms"), R("ones"), R("c192"), R("indr", j0, j1), R(r15)], "rk")
        if t:
            tt("pri", ll, r15, A.mult, k0, k1, slo=0, name="l")
            ts("pi", "pri", ("kcol", t), A.add, lo=k0, hi=k1, name="l")
        else:
            tt("pi", ll, r15, A.mult, k0, k1, slo=0, name="l")
        ts("hm", "pi", 6, A.arith_shift_right, H - 1, A.bitwise_and, lo=k0, hi=k1, name="l")
        cp("hu", "hm", k0, k1, 64, name="l")
        wm = tile()
        mm(wm, [(slice(0, CH), "ey", al, rf, c(j0, j1), CH), (slice(0, CH), "ni15", al, "nm", c(j0, j1), CH)],
           [R("ey"), R("ni15"), R(rf, j0, j1), R("nm", j0, j1), R("hm", k0, k1), R("cache")], "wm")
        v(lambda e, B, inc: inc(e.tensor_tensor(out=B("t1")[:, j0:j1], in0=B("cache")[:, D0:D0 + H].indirect(B("hu")[:, k0:k1]), in1=B("nm")[:, j0:j1], op=A.add)),
          [R("cache"), R("hu", k0, k1), R("nm", j0, j1)], [R("t1", j0, j1)], GF * CH, "cache gather")
        tt("r2", wm, "t1", A.max, j0, j1, slo=0, name="r2")
        ts("r2u", "r2", float(SH), A.add, lo=j0, hi=j1, cyc=CH / 2, name="r2u")

    def phase_p(j0, j1):
        CH = j1 - j0
        gpt, b0 = 512 // CH, 8 * j0
        for g0 in range(0, 8, gpt):
            d = tile()
            mm(d, [(slice(i * CH, (i + 1) * CH), "pb", c(128 * (g0 + i), 128 * (g0 + i + 1)), "r2", c(j0, j1), CH, True, True) for i in range(gpt)],
               [R("pb"), R("r2", j0, j1)], "pairs")
            ts("eqp", d, 0.0, A.is_equal, lo=b0 + g0 * CH, hi=b0 + (g0 + gpt) * CH, cyc=gpt * CH, slo=0, name="eq")
        vt = tile()
        for g0 in (0, 4):
            mm(vt, [(slice(0, CH), "vw", c(112 - 16 * g, 240 - 16 * g), "eqp", c(b0 + g * CH, b0 + (g + 1) * CH), CH) for g in range(g0, g0 + 4)],
               [R("vw"), R("eqp", b0 + g0 * CH, b0 + (g0 + 4) * CH)] + ([] if g0 else [R("eqp", b0 + 4 * CH, b0 + 6 * CH)]), "loop", g0 == 0, g0 == 4)
        ts("nq", vt, 0.0, A.is_le, lo=j0, hi=j1, cyc=CH, slo=0, name="nq")
        dt_ = tile()
        mm(dt_, [(slice(0, CH), "dl", al, "r2", c(j0, j1), CH)], [R("dl"), R("r2", j0, j1), R("eqp", b0, b0 + 8 * CH)], "delta")
        tt("yp", dt_, "nq", A.mult, j0, j1, slo=0, name="yp")

    def winners(t):
        if t < RO - 1:
            kt = tile()
            mm(kt, [(slice(0, 1), "kw", al, "kacc", c(t * NB + x, t * NB + x + 1), 256) for x in range(len(PARTS[t]))],
               [R("kw"), R("kacc", t * NB, t * NB + NB)], "K")
            ts("kcol", kt, 96.0 * 8 * P, A.add, lo=t + 1, hi=t + 2, slo=0, name="K")
        lf = tile()
        mm(lf, lists(lf, 0, 32, 288, "nm", 0, P), [R("ms"), R("nm"), R("hm")], "fail")
        tt("hh", lf, "hm", A.add, 0, 32, name="w")
        pt = tile()
        mm(pt, [(slice(32 * g, 32 * g + 32), "pb", c(128 * g, 128 * g + 128), "hh", c(0, 32), 64, True, True) for g in range(8)], [R("pb"), R("hh")], "h pairs")
        for x0 in (0, 8):
            mm(pt, [y for x in range(x0, x0 + 8) for y in
                    ((slice(256 + 16 * x, 272 + 16 * x), "pe", c(128 * (x // 2), 128 * (x // 2 + 1)), "hh", c(0, 32, 2), 64, True, False),
                     (slice(256 + 16 * x, 272 + 16 * x), "po", c(128 * x, 128 * x + 128), "hh", c(1, 32, 2), 64, False, True))],
               [R("pe"), R("po"), R("hh")], "h pairs")
        ts("eqh", pt, 0.0, A.is_equal, hi=512, cyc=512, name="w")
        z = tile()
        mm(z, [(slice(0, 32), "vw", c(352 - 16 * g, 480 - 16 * g), "eqh", c(32 * g, 32 * g + 32), 64) for g in range(8)]
           + [((0, slice(0, 2), slice(1, 16, 2)), "lw", c(120 - 8 * x, 248 - 8 * x), "eqh", c(256 + 16 * x, 272 + 16 * x), 64) for x in range(16)]
           + [(slice(0, 32), "ey", al, "hh", c(0, 32), 64)], [R("vw"), R("lw"), R("eqh"), R("ey"), R("hh")], "lose")
        for x in (0, 1):
            v(lambda e, B, inc, x=x: inc(e.tensor_scalar(out=B("wu")[:, x:32:2], in0=B(z, (0, slice(0, 2), slice(x, 16, 2))), scalar1=float(H + D0),
                                                         scalar2=B("col")[:, CQ + x:CQ + x + 1], op0=A.add, op1=A.max)),
              [R(z), R("col", CQ, CQ + 2)], [("wu", x, x + 1)], 64, "w")

    def phase_d(t, j0, j1):
        ds = tile()
        s02 = slice(0, 3, 2)
        va = [((slice(0, 3), slice(p - 1, p + 1)), "vd", rows("vd", j0, p), "wo", (ALL, ALL, ALL, ALL), 64) for p in range(1, 16, 2)]
        for p in range(0, 15, 2):
            lo, hi = max(p - 1, 0), min(p + 2, 15)
            va.append(((slice(0, 3), slice(lo, hi)), "vd", rows("vd", j0, p), "we", (ALL, ALL, ALL, slice(lo - p + 1, hi - p + 1)), max(64, 24 * (hi - lo))))
        mx = [((s02, slice(p, p + 2)), "md", rows("md", j0, p), "wx", (ALL, ALL, ALL, ALL), 64) if p % 2 == 0 and p < 14 else
              ((0, p), "md", rows("md", j0, p), "b2", c(0, 8), 64) for p in range(15)]
        mm(ds, va, [R("vd", 16 * j0, 16 * j1), R("we"), R("wo")], "sum d", True, False)
        mm(ds, mx, [R("md", 16 * j0, 16 * j1), R("b2"), R("wx")], "sum m", False, False)
        mm(ds, [((1, 2 * p + 1), "m2", rows("m2", j0, p, 8), "b2", c(0, 8), 64) for p in range(7)], [R("m2", 8 * j0, 8 * j1), R("b2")], "sum m", False, False)
        mm(ds, [(slice(0, 384), "nq", c(j0, j1), "nw", c(0, 384), 384)], [R("nq", j0, j1), R("yp", j0, j1), R("nw")], "loop d", False, True)
        s(lambda e, B, inc: inc(e.activation(B("sn")[:, :, j0:j1], B(ds, slice(0, 384)), F.Sign, bias=B("col")[:, CNH:CNH + 1], scale=-1.0)),
          [R(ds), R("col", CNH, CNH + 1)], [("sn", j0, j1), ("sn", P + j0, P + j1)], 3 * BL, "near")

    def phase_e(t, b, j0, j1):
        BL, last = j1 - j0, t == RO - 1
        nt = tile()
        mm(nt, [(slice(x, x + 128), "sn", (ALL, y, slice(j0 + x, j0 + x + 128)), "hey", al, 128, y == 1, y == 2) for x in range(0, BL, 128) for y in (1, 2)],
           [("sn", j0, j1), R("hey")], "near")
        tt("t5", nt, "yp", A.mult, j0, j1, slo=0, name="t5")
        rt = tile()
        whole = [(slice(0, BL), "tri", al, "yp", c(j0, j1), 4 * BL)]
        if last:
            mm(rt, whole + [(slice(0, BL), "eyf", al, "t5", c(j0, j1), 4 * BL)], [R("tri"), R("eyf"), R("yp", j0, j1), R("t5", j0, j1)], "rn")
            s(lambda e, B, inc: inc(e.activation(B("yrs")[:, j0:j1], B(rt, slice(0, BL)), F.Identity, bias=B("col")[:, CSH:CSH + 1])),
              [R(rt), R("col", CSH, CSH + 1)], [R("yrs", j0, j1)], BL, "yr")
            op("Y", lambda e, B, inc: inc(e.dma_start(B("IN")["yr"][:, j0:j1], B("yrs")[:, j0:j1])), [R("yrs", j0, j1)], [("yr", j0, j1)], 0.5 * cost["LX"], "store yr", sem="oy%d" % b)
        else:
            mm(rt, whole, [R("tri"), R("yp", j0, j1), ("sn", j0, j1)], "rn")
            tt("rn%d" % t, rt, "t5", A.add, j0, j1, slo=0, name="rn")
            send("rn%d" % t, "rf%d" % (t + 1), j0, j1, "ls%d_%d" % (t + 1, b), "ar%d_%d" % (t + 1, b))

    def phase_s(t, b, j0, j1):
        BL, i0 = j1 - j0, 16 + b * KA
        v(lambda e, B, inc: inc(e.tensor_tensor_scan(B("kb")[:, i0:i0 + BL], B("sn")[:, 0, j0:j1], B("cap2")[:, 0:BL], 1.0, A.min, A.max)),
          [("sn", P + j0, P + j1), R("cap2")], [R("kb", i0, i0 + BL)], BL / 2, "kb")
        at = tile()
        mm(at, turn(0, BL, "kb", i0 - 1, "ey"), [R("kb", i0 - 1, i0 + BL), R("ey")], "a2")
        tt("y2", at, "yp", A.mult, j0, j1, slo=0, name="y2")
        sk = tile()
        mm(sk, [(slice(0, BL), "e15", al, "r2", c(j0, j1), BL), (slice(0, BL), "t15", al, "y2", c(j0, j1), 4 * BL)],
           [R("t15"), R("e15"), R("r2", j0, j1), R("y2", j0, j1)], "st")
        s(lambda e, B, inc: inc(e.activation(B("st")[:, j0:j1], B(sk, slice(0, BL)), F.Identity, bias=B("col")[:, CSH:CSH + 1])),
          [R(sk), R("col", CSH, CSH + 1)], [R("st", j0, j1)], BL, "st")
        for k in range(j1 // 16 - 2, j0 // 16 - 1, -2):
            op("V", lambda e, B, inc, k=k: inc(e.tensor_copy(out=B("cache")[:, 0:D0 + H].indirect(B("wu")[:, k:k + 2]), in_=B("st")[:, 16 * k:16 * k + 32])),
               [R("wu"), R("st", j0, j1)], [R("cache")], 0.05 + cost["SCF"] * 32 * CYC, "scatter")

    for t in range(RO):
        for j0, j1 in spans(SENDS[t - 1] if t else (P,)):
            cls[0], cls[1] = "A%d" % t, (P - j1) // CH
            if t:
                ts("ru", "rf%d" % t, float(SH), A.add, lo=j0, hi=j1, cyc=(j1 - j0) / 2, name="ru")
            else:
                cp("ru", "r0i", j0, j1, P, name="ru")
                ts("rf0", "ru", float(-SH), A.add, lo=j0, hi=j1, cyc=P / 2, name="rf")
        for ch, (j0, j1) in enumerate(spans(PARTS[t])):
            cls[0], cls[1] = "A%d" % t, ch
            phase_a(t, ch, j0, j1)
        cls[0], cls[1] = "R%d" % t, 0
        ends(t)
        for ch, (j0, j1) in enumerate(spans(PARTS[t])):
            cls[0], cls[1] = "B%d" % t, ch
            phase_b(t, ch, j0, j1)
        for ch, (j0, j1) in enumerate(spans(LOOPS[t])):
            cls[0], cls[1] = "P%d" % t, ch
            phase_p(j0, j1)
        cls[0], cls[1] = "W%d" % t, 0
        winners(t)
        for j0, j1 in spans(DISTS[t]):
            cls[0], cls[1] = "D%d" % t, (P - j1) // BL
            gather("vd", "r2u", j0, j1)
            maxima("md", "vd", j0, j1, 1)
            maxima("m2", "vd", j0, j1, 2)
            for j in range(j1 - BL, j0 - 1, -BL):
                cls[1] = (P - BL - j) // BL
                phase_d(t, j, j + BL)
        for name, phase, sizes in (("E", phase_e, SENDS[t]), ("S", phase_s, COPIES[t])):
            for b, (j0, j1) in enumerate(spans(sizes)):
                cls[0], cls[1] = "%s%d" % (name, t), (P - j1) // BL
                phase(t, b, j0, j1)
    op("Y", lambda e, B, inc: inc(e.dma_start(B("IN")["yc"][:, :], B("cache")[:, D0:D0 + H])), [R("cache")], [("yc", 0, H)], 0.7 * cost["LX"], "store yc", sem="oc")
    return ops, tiles


def deps_of(ops, key, cross):
    hist, out = {}, []
    for o in ops:
        d = {}
        for rw, regs in (("r", o["r"]), ("w", o["w"])):
            for (b, lo, hi) in regs:
                for (lo2, hi2, rw2, o2) in hist.get(key(b), ()):
                    if o2 is o or lo2 >= hi or hi2 <= lo:
                        continue
                    kind = rw2 + rw
                    if kind == "rr" and not (cross(b) and o2["q"] != o["q"]):
                        continue
                    d.setdefault(o2["id"], set()).add((kind, cross(b)))
        if "after" in o:
            d.setdefault(o["after"], set()).add(("wr", False))
        for rw, regs in (("r", o["r"]), ("w", o["w"])):
            for (b, lo, hi) in regs:
                h = hist.setdefault(key(b), [])
                if rw == "w":
                    h[:] = [x for x in h if not (lo <= x[0] and x[1] <= hi)]
                h.append((lo, hi, rw, o))
        out.append(d)
    return out


def free_of_wait(o, o2, kinds):
    return o["q"] == o2["q"] == "T" and all(cr for _, cr in kinds)


def schedule(cost=COST, bias=BIAS):
    ops, tiles = build_ops(cost)
    LAT = cost["LAT"]
    for o in ops:
        o["q"] = o["qs"][0]
        for b, lo, hi in o["r"] + o["w"]:
            if isinstance(b, tuple):
                tiles[b[1]]["users"] += 1
    dep = deps_of(ops, lambda b: b, lambda b: isinstance(b, tuple))
    n = len(ops)
    succ = [[] for _ in range(n)]
    left = [len(dep[i]) for i in range(n)]
    for i in range(n):
        for d in dep[i]:
            succ[d].append(i)
    beat, due = cost["LX"], {}
    for i, o in enumerate(ops):
        if o["name"] == "gather" and o["q"] == "S":
            beat += o["dur"] * bias["beat"] / 100
            due[i] = beat
    rank = [0.0] * n
    for i in range(n - 1, -1, -1):
        rank[i] = ops[i]["dur"] + max([rank[j] + LAT * bias["gap"] / 10 for j in succ[i]] + [-due.get(i, beat + 0.1 * bias.get("tail", 80))])
    for i, o in enumerate(ops):
        early = o["cls"][0] == "K" or o["name"] in ("load x", "iota0") or (o["cls"][0] == "C" and o["q"] in "VS")
        short = o["q"] == "S" and o["name"] in ("bad", "nm", "st", "near")
        rank[i] += 30 * early + 50 * short + 0.1 * (bias.get(o["cls"][0] + str(o["part"]), 0) + bias.get(o["name"], 0))
    rank = bias.get("rank", rank)
    free = {q: 0.0 for q in "VSTGYAN"}
    pool = {"p%d" % i: 0.0 for i in range(NPS)}
    endt, order, est = [0.0] * n, [], {}
    ready = [i for i in range(n) if left[i] == 0]
    while ready:
        cands = []
        for i in ready:
            o = ops[i]
            if i not in est:
                est[i] = max([endt[d] + (0.0 if free_of_wait(o, ops[d], kk) else LAT) for d, kk in dep[i].items()] or [0.0])
            e0 = est[i]
            new = [b for b, lo, hi in o["w"] if isinstance(b, tuple) and tiles[b[1]]["buf"] is None]
            if new:
                if len(pool) < 1 + (o["name"] in ("sum a", "sum d", "init d", "rn", "st")):
                    continue
                e0 = max(e0, min(pool.values()) + LAT)
            for q in o["qs"]:
                cands.append((max(e0, free[q] if q != "N" else 0.0), -rank[i], i, q))
        assert cands, "no operation can go on"
        t0 = min(x[0] for x in cands)
        q0 = min(cands)[3]
        st, _, i, q = min([x for x in cands if x[3] == q0 and x[0] <= t0 + 0.01 * max(bias["wait"], 0)], key=lambda x: (x[1], x[0]))
        o = ops[i]
        o["q"] = q
        for b, lo, hi in o["w"]:
            if isinstance(b, tuple) and tiles[b[1]]["buf"] is None:
                bb = min(pool, key=lambda x: pool[x])
                del pool[bb]
                tiles[b[1]]["buf"] = bb
        e = st + o["dur"]
        endt[i], o["t0"], o["t1"] = e, st, e
        free[q] = st + 0.1 if q in "YA" else e
        if q == "A":
            free["S"] = max(free["S"], 0.1)
        for b, lo, hi in o["r"] + o["w"]:
            if isinstance(b, tuple):
                tl = tiles[b[1]]
                tl["users"] -= 1
                tl["end"] = max(tl.get("end", 0.0), e)
                if tl["users"] == 0:
                    pool[tl["buf"]] = tl["end"]
        order.append(i)
        ready.remove(i)
        for j in succ[i]:
            left[j] -= 1
            if left[j] == 0:
                ready.append(j)
    assert len(order) == n
    return [ops[i] for i in order], tiles, max(endt)


def tighten(seq, dep, costs, steps):
    n, byid, rng = len(seq), {o["id"]: o for o in seq}, np.random.RandomState(0)
    need, succ = [None] * n, [[] for _ in range(n)]
    for o, d in zip(seq, dep):
        need[o["id"]] = [(i, not free_of_wait(o, byid[i], kk)) for i, kk in d.items()]
        for i in d:
            succ[i].append(o["id"])
    queues = {q: [o["id"] for o in seq if o["q"] == q] for q in "VSTG"}
    cases = [([o["dur"] for o in build_ops(x)[0]], x["LAT"]) for x in costs]

    def times():
        before, after = [None] * n, [None] * n
        for line in queues.values():
            for a, b in zip(line, line[1:]):
                before[b], after[a] = a, b
        left = [len(need[i]) + (before[i] is not None) for i in range(n)]
        order = [i for i in range(n) if not left[i]]
        for i in order:
            for j in succ[i] + ([after[i]] if after[i] is not None else []):
                left[j] -= 1
                if not left[j]:
                    order.append(j)
        if len(order) < n:
            return (1e9,)
        ends, whys = [], []
        for dur, lat in cases:
            end, why = [0.0] * n, [None] * n
            for i in order:
                w = before[i]
                m = 0.0 if w is None else end[w]
                for d, wait in need[i]:
                    e = end[d] + lat if wait else end[d]
                    if e > m:
                        m, w = e, d
                end[i], why[i] = m + dur[i], w
            ends.append(end)
            whys.append(why)
        return sum(max(e) for e in ends) / len(ends), ends, whys, before

    cur = best = times()
    for step in range(steps):
        case = rng.randint(len(cases))
        end, why = cur[1][case], cur[2][case]
        i, path = end.index(max(end)), []
        while i is not None:
            if why[i] is not None and why[i] == cur[3][i] and i not in succ[why[i]]:
                path.append(i)
            i = why[i]
        u = path[rng.randint(len(path))]
        q, k = byid[u]["q"], (1, 1, 2, 3, 5, 8)[rng.randint(6)]
        line = queues[q]
        p = line.index(u)
        if rng.randint(2):
            queues[q] = line[:max(p - k, 0)] + [u] + line[max(p - k, 0):p] + line[p + 1:]
        else:
            queues[q] = line[:p - 1] + line[p:p + k] + [line[p - 1]] + line[p + k:]
        new = times()
        if new[0] - cur[0] <= -math.log(1.0 - rng.rand()) * 0.15 * (1.0 - step / steps):
            cur = new
            best = min(best, cur, key=lambda x: x[0])
        else:
            queues[q] = line
    for o in seq:
        o["t0"], o["t1"] = best[1][0][o["id"]] - cases[0][0][o["id"]], best[1][0][o["id"]]
    return sorted(seq, key=lambda o: o["t0"])


PLAN = {}


def plan():
    if not PLAN:
        seq, tiles, end = schedule()
        key = lambda b: tiles[b[1]]["buf"] if isinstance(b, tuple) else b
        seq = tighten(seq, deps_of(seq, key, lambda b: isinstance(b, tuple)), [dict(COST, **x) for x in CASES], STEPS)
        PLAN["seq"], PLAN["tiles"] = seq, tiles
        PLAN["dep"] = deps_of(seq, key, lambda b: isinstance(b, tuple))
    return PLAN


def rank_program(g, core, T, topo):
    rank = T.rank_of(core)
    if rank is None:
        return
    pl = plan()
    tiles = pl["tiles"]
    byid = {o["id"]: o for o in pl["seq"]}
    dst = T.cores[(rank + ST) % len(T.cores)]
    src = T.cores[(rank - ST) % len(T.cores)]
    rid, pid, _ = topo.addr(dst)
    emask, ne, ne_in = topo.mask(core, dst), len(topo.engines(core, dst)), len(topo.engines(src, core))
    eng = {"V": g.vector, "S": g.scalar, "T": g.tensor, "G": g, "Y": g.sync, "A": g.scalar}
    host = {"V": "V", "S": "S", "T": "T", "G": "G", "Y": "Y", "A": "S"}
    ins = {"x": T.x, "r0": T.r0, "c0": T.c0, "yc": T.yc, "yr": T.yr}
    cur = ["V"]

    def B(name, cols=None):
        if name == "Q":
            return cur[0]
        if name == "IN":
            return ins
        if cols is not None:
            return B(name)[bank_view(cols) if isinstance(name, tuple) else (slice(0, 128), cols)]
        return T[tiles[name[1]]["buf"]] if isinstance(name, tuple) else T[name]

    cnt = {"V": 0, "S": 0, "T": 0, "G": 0}
    known = {q: {} for q in "VSTGY"}
    done, pend = {}, {}

    def inc(x, q):
        cnt[q] += 1
        x.then_inc(T.sem["q" + q], 1)

    for o, dep in zip(pl["seq"], pl["dep"]):
        q = o["q"]
        if q == "N":
            done[o["id"]] = (o["sem"], ne_in, {})
            pend[o["sem"]] = ne_in
            continue
        h = host[q]
        kn, need = known[h], {}
        for d, kinds in dep.items():
            sem, n, imp = done[d]
            if free_of_wait(o, byid[d], kinds):
                continue
            if n > need.get(sem, (0, None))[0]:
                need[sem] = (n, imp)
        for sem in sorted(need, key=lambda x: -need[x][0]):
            n, imp = need[sem]
            if kn.get(sem, 0) >= n:
                continue
            eng[q].wait_ge(T.sem[sem], n)
            kn[sem] = n
            for s2, c2 in imp.items():
                kn[s2] = max(kn.get(s2, 0), c2)
        cur[0] = q
        if isinstance(o["fn"], tuple):
            _, a, z, j0, j1 = o["fn"]
            g.remote_dma(T[z][:, j0:j1], T[a][:, j0:j1], T.sem[o["sem2"]], T.sem[o["sem"]], pid, rid, emask)
            done[o["id"]] = (o["sem"], ne, {})
            pend[o["sem"]] = ne
        elif o["sem"]:
            o["fn"](eng[q], B, lambda x: x.then_inc(T.sem[o["sem"]], 16))
            done[o["id"]] = (o["sem"], 16, dict(kn))
            pend[o["sem"]] = 16
        else:
            o["fn"](eng[q], B, lambda x: inc(x, h))
            imp = dict(kn)
            imp["q" + h] = cnt[h]
            done[o["id"]] = ("q" + h, cnt[h], imp)
    for q in "VSTG":
        g.wait_ge(T.sem["q" + q], cnt[q])
    for sname in pend:
        if known["G"].get(sname, 0) < pend[sname]:
            g.wait_ge(T.sem[sname], pend[sname])
